import numpy as np, ml_dtypes
CORES = [2,6,10,14,18,22,26,30]
N = 8
BF = ml_dtypes.bfloat16
def f(rng, *shape):
    return (rng.standard_normal(shape, dtype=np.float32) * np.exp2(rng.integers(-2, 3, shape[:-1] + (1,)))).astype(BF)
def wide(rng, *shape):
    v = f(rng, *shape).astype(np.float32); k = shape[:-2] + (1, shape[-1])
    return (v * np.exp2(rng.integers(-6, 7, k)) * (rng.random(k) > 0.0625)).astype(BF)
W, V, L, DM, ST = 4096, 512, 192, 2, 5
def hotty(rng, hot, n, share):
    h = hot[np.arange(8)[None, :, None, None], rng.integers(0, hot.shape[1], (N, 8, 16, n))]
    return np.where(rng.random((N, 8, 16, n)) < share, h, rng.integers(0, W, (N, 8, 16, n)))
def parts(rng):
    hot = rng.integers(0, W, (8, W // 16)); share = rng.choice(np.array([0.25, 0.5, 0.75]), (N, 8, 1, 1))
    refs = hotty(rng, hot, V, share); gloss = hotty(rng, hot, W, share)
    u = rng.random((N, ST, L))
    need = np.where(u < 0.4, rng.integers(1, 45, u.shape), np.where(u < 0.9, rng.integers(58, 71, u.shape), rng.integers(90, 129, u.shape)))
    v = rng.integers(0, V, (N, 8, L)); p = rng.integers(0, V, (N, DM, 8, L)); a = rng.integers(0, 16, (N, DM, 8, L)); d = rng.integers(0, DM + 1, (N, L))
    return refs, gloss, f(rng, N, 128, W), f(rng, N, 128, L), need, v, p, a, d
def pack(refs, gloss, facts, cases, need, v, p, a, d):
    i = lambda x: np.ascontiguousarray(x).astype(np.int32)
    return {"refs": i(refs.reshape(N, 128, V)), "gloss": i(gloss.reshape(N, 128, W)), "facts": np.ascontiguousarray(facts).astype(BF), "cases": np.ascontiguousarray(cases).astype(BF), "need": i(need),
            "vp0": i(np.concatenate([v, p.reshape(N, 8 * DM, L)], axis=1)), "act0": i(a.reshape(N, 8 * DM, L)), "dep0": i(d.reshape(N, 1, L))}
def setup_inputs(rng):
    return pack(*parts(rng))
def skew(rng, n):
    e = rng.choice(np.array([1.0, 2.0, 4.0]), (N, 8, 16, 1)); x = np.minimum((W * rng.random((N, 8, 16, n)) ** e).astype(np.int64), W - 1)
    return np.where(rng.random((N, 8, 1, 1)) < 0.5, W - 1 - x, x)
def setup_inputs_spread(rng):
    refs, gloss, facts, cases, need, v, p, a, d = parts(rng)
    need = np.where(rng.random(need.shape) < 0.3, rng.integers(1, 129, need.shape), need)
    far = np.exp2(40.0 * (rng.permutation(128)[None, :, None] % 3 - 1)).astype(np.float32)
    return pack(skew(rng, V), skew(rng, W), wide(rng, N, 128, W).astype(np.float32) * far, wide(rng, N, 128, L).astype(np.float32) * far, need, v, p, a, d)
def tips(rng, x, top, share):
    return np.where(rng.random(x.shape) < share, top * rng.integers(0, 2, x.shape), x)
def setup_inputs_ends(rng):
    refs, gloss, facts, cases, need, v, p, a, d = parts(rng)
    al = rng.random((N, 1, L)) < 0.5; al[:, :, 0] = True; al[:, :, L - 1] = True
    bit = np.where(rng.random((N, 1, 16, V)) < 0.7, rng.integers(0, 2, (N, 1, 16, V)), rng.integers(0, 2, (N, 8, 16, V)))
    refs = np.where(rng.random(refs.shape) < 0.9, (W - 1) * bit, refs)
    refs[..., 0] = (W - 1) * (np.arange(16) & 1); refs[..., V - 1] = (W - 1) * (np.arange(16) == 15)
    gloss = tips(rng, gloss, W - 1, 0.85)
    for c in (0, W - 1): gloss[..., c] = (W - 1) * rng.integers(0, 2, (N, 8, 16))
    gloss[:, :, 0, 0] = 0; gloss[:, :, 0, W - 1] = W - 1; gloss[:, :, 15, 0] = W - 1; gloss[:, :, 15, W - 1] = 0
    v = (V - 1) * np.where(al, rng.integers(0, 2, (N, 1, L)), rng.integers(0, 2, (N, 8, L)))
    p = tips(rng, p, V - 1, 0.9); a = np.where(al[:, None], 15 * rng.integers(0, 2, (N, DM, 1, L)), tips(rng, a, 15, 0.9))
    d = tips(rng, d, DM, 0.8); d[:, 0] = DM; d[:, L - 1] = DM
    need = np.where(rng.random(need.shape) < 0.8, np.where(rng.random(need.shape) < 0.5, 1, 128), rng.integers(40, 90, need.shape))
    need[:, 0, 0] = 128; need[:, 0, L - 1] = 128
    facts[:, :, 0] = -64; facts[:, :, W - 1] = 64
    u = rng.random((N, 1, L)); u[:, :, 0] = 0.1; u[:, :, L - 1] = 0.1
    z = np.where(u < 0.25, np.float32(-64), cases.astype(np.float32)); one = rng.integers(0, 128, (N, 1, L)) == np.arange(128)[None, :, None]
    z = np.where(one & (u > 0.6) & (u < 0.8), np.float32(-128), np.where(one & (u >= 0.8), np.float32(128), z))
    return pack(refs, gloss, facts, z, need, v, p, a, d)
def setup_inputs_corners(rng):
    refs, gloss, facts, cases, need, v, p, a, d = parts(rng)
    facts = rng.integers(-3, 4, (N, 128, W)).astype(np.float32); z = rng.integers(-3, 4, (N, 128, L)).astype(np.float32)
    k = rng.integers(0, 6, (N, L)); k[:, :6] = np.arange(6); k[:, L - 6:] = np.arange(6)[::-1]
    cnt = np.where(k == 0, 128, np.where(k == 1, 0, np.where(k == 2, 64, rng.choice(np.array([1, 127]), (N, L)))))
    order = np.argsort(rng.random((N, 128, L)), axis=1)
    z = np.where((k < 4)[:, None, :], np.where(order < cnt[:, None, :], 1024.0, -1024.0), z)
    other = (np.arange(128)[None, :, None] >> 4) != rng.integers(0, 8, (N, 1, L))
    z = np.where((k == 5)[:, None, :] & other, 1024.0, z)
    kk = k[:, None, :]; s = need.shape
    need = np.where(kk < 2, np.where(rng.random(s) < 0.5, 1, 128), np.where(kk < 4, cnt[:, None, :] + rng.integers(0, 2, s), np.where(kk == 4, rng.integers(62, 84, s), rng.integers(118, 125, s))))
    ve = np.array([0, 1, V - 2, V - 1])
    v = np.where(rng.random(v.shape) < 0.7, rng.choice(ve, v.shape), v); p = np.where(rng.random(p.shape) < 0.7, rng.choice(ve, p.shape), p)
    a = np.where(rng.random(a.shape) < 0.7, rng.choice(np.array([0, 1, 14, 15]), a.shape), a)
    return pack(refs, gloss, facts, z, need, v, p, a, d)
def setup_inputs_crowd(rng):
    refs, gloss, facts, cases, need, v, p, a, d = parts(rng)
    a = rng.integers(8, 16, a.shape); a[:, 0] = rng.integers(1, 8, (N, 8, L))
    cases[:, :48] = 2048; cases[:, 48:96] = -2048; cases[:, 96:100] = 512
    for g in range(8):
        s = 1 + rng.permutation(W - 2)[:4]
        if g < 4:
            if g < 2: s[1] = (W - 1) * (1 - g)
            gloss[:, g, 8:, s[0]] = s[1]; gloss[:, g, 8:, s[1]] = s[1]; refs[:, g, 0] = s[0]
            if g >= 2:
                gloss[:, g, 8:, s[2]] = s[3]; gloss[:, g, 8:, s[3]] = s[3]
                w = int(rng.integers(0, V)); refs[:, g, 0, w] = s[2]
                v[:, g] = np.where(v[:, g] == w, (w + 1) % V, v[:, g]); v[np.arange(N), g, rng.integers(0, L, N)] = w
        elif g == 4:
            for c in s: gloss[:, g, 8:, c] = c
            refs[:, g] = s[rng.integers(0, 4, (N, 16, V))]
        elif g == 5:
            o = rng.permutation(W); own = o[:N * L]; rest = o[N * L:]; gg = gloss[:, g]
            gg[:, 8:, own] = own; gg[:, 8:, rest] = rest[rng.integers(0, W - N * L, (N, 8, W - N * L))]
            gg[:, 1:8, own] = 2 * (gg[:, 1:8, own] // 2); gg[:, 1:8, rest] = 2 * (gg[:, 1:8, rest] // 2) + 1
            refs[:, g, 0] = own.reshape(N, L)[:, np.arange(V) % L]; refs[:, g, 1:] = rest[rng.integers(0, W - N * L, (N, 15, V))]
            v[:, g] = np.argsort(rng.random((N, L)), axis=1) + L * rng.integers(0, V // L, (N, L))
            a[:, 0, g] = np.minimum(a[:, 0, g], 6); a[:, 0, g, L - 1] = 7
        else:
            gloss[:, g, 1:, s[0]] = s[0]; refs[:, g, 0] = s[0]; facts[:, 16 * g:16 * g + 16, s[0]] = 1024
    need = rng.integers(50, 58, need.shape); need[:, 0] = rng.integers(49, 53, (N, L)); need[::2, 2] = 128
    need[:, ST - 1] = np.where(rng.random((N, L)) < 0.5, 1, need[:, ST - 1])
    d[:] = DM; d[1::2] = np.where(rng.random(d[1::2].shape) < 0.1, rng.integers(0, DM, d[1::2].shape), DM)
    return pack(refs, gloss, facts, cases, need, v, p, a, d)
def setup_inputs_calm(rng):
    refs, gloss, facts, cases, need, v, p, a, d = parts(rng)
    hi = np.arange(8)[:, None] >= 4; few = np.where(hi, W - 4 + np.arange(4), np.arange(4))
    refs[:, :7] = hotty(rng, few, V, 1.0)[:, :7]; gloss[:, :7] = hotty(rng, few, W, 1.0)[:, :7]
    v = rng.integers(0, 4, v.shape) + (V - 4) * hi; p = rng.integers(0, 4, p.shape) + (V - 4) * hi; a = rng.integers(0, 4, a.shape) + 12 * hi
    return pack(refs, gloss, facts, cases, need, v, p, a, d)
def check_inputs(d):
    bad = []
    for k, lo, hi in (("refs", 0, W - 1), ("gloss", 0, W - 1), ("need", 1, 128), ("vp0", 0, V - 1), ("act0", 0, 15), ("dep0", 0, DM)):
        if np.min(d[k]) < lo or np.max(d[k]) > hi: bad.append("range of " + k)
    for k in ("facts", "cases"):
        if not np.all(np.isfinite(np.asarray(d[k]).astype(np.float32))): bad.append("not finite: " + k)
    return bad
def reference(refs, gloss, facts, cases, need, vp0, act0, dep0):
    R = refs.astype(np.int64).reshape(N, 8, 16, V); GL = gloss.astype(np.int64).reshape(N, 8, 16, W)
    X = facts.astype(np.float32).reshape(N, 8, 16, W); Z = cases.astype(np.float32).reshape(N, 8, 16, L)
    v = vp0[:, :8].astype(np.int64); p = vp0[:, 8:].astype(np.int64).reshape(N, DM, 8, L)
    a = act0.astype(np.int64).reshape(N, DM, 8, L); d = dep0[:, 0].astype(np.int64); c = need.astype(np.int64)
    gi = np.arange(8)[:, None, None]; lane = np.arange(L); shown = np.zeros((N, 8, 16, L), np.int64)
    for t in range(ST):
        writes = []
        for r in range(N):
            q = (r + 1 + t % (N - 1)) % N
            B = np.take_along_axis(R[r], v[r][:, None, :], 2)
            for j in range(DM, 1, -1): B = GL[r][gi, a[r, j - 1][:, None, :], B]
            a1 = np.array(a[r, 0]); T = GL[q][gi, a1[:, None, :], B]; shown[r] = T
            n = np.zeros((16, L), np.int64)
            for g in range(8): n = n + np.sum((X[q, g][:, T[g]] <= Z[r, g][:, None, :]).astype(np.int64), axis=0)
            met = n >= c[r, t][None, :]
            every = np.all(met, axis=0); some = np.any(met, axis=0); fu = np.argmin(met, axis=0); hm = np.argmax(met, axis=0)
            tf = T[:, fu, lane]; bf = B[:, fu, lane]; th = T[:, hm, lane]
            pop = every & (d[r] > 0); push = ~every & (d[r] < DM); put = ~every & some & (d[r] == DM)
            after = (v[r] + 1) & (V - 1); nv = np.where(push, tf & (V - 1), after)
            for j in range(1, DM + 1):
                leave = pop & (d[r] == j); enter = push & (d[r] == j - 1)
                nv = np.where(leave, p[r, j - 1], nv)
                a[r, j - 1] = np.where(enter, tf & 15, np.where(leave, 0, a[r, j - 1])); p[r, j - 1] = np.where(enter, after, p[r, j - 1])
            v[r] = nv; d[r] = d[r] + push.astype(np.int64) - pop.astype(np.int64)
            writes.append((q, a1, bf, th, np.nonzero(put)[0]))
        for q, a1, bf, th, who in writes:
            for g in range(8):
                places, first = np.unique(bf[g, who], return_index=True); w = who[first]
                GL[q, g, a1[g, w], bf[g, w]] = th[g, w]
    yvp = np.concatenate([v, p.reshape(N, 8 * DM, L)], axis=1)
    return {"yt": shown.reshape(N, 128, L).astype(np.float32), "yg": np.sum(GL.reshape(N, 128, 16, W // 16), axis=2).astype(np.float32), "yvp": yvp.astype(np.float32),
            "yact": a.reshape(N, 8 * DM, L).astype(np.float32), "ydep": d.reshape(N, 1, L).astype(np.float32)}

@@ -1,0 +1,740 @@
+import numpy as np
+from concourse.mybir import AluOpType, ActivationFunctionType
+
+A, F = AluOpType, ActivationFunctionType
+
+L, ST, NA, NV = 192, 5, 4096, 512
+TW = NA + 32
+LO = (128, 64, 0)
+NE = 8
+
+f32, b16, h16, i32, u16 = "float32", "bfloat16", "float16", "int32", "uint16"
+
+
+def _s(n, dt):
+    return ("sbuf", [128, n], dt)
+
+
+SCRATCH = {
+    "GI": _s(NA, i32), "TAB": _s(TW, f32), "FX": _s(NA, b16), "RF": _s(NV + 8, i32), "CS": _s(L, b16),
+    "CNs": _s(2 * L, b16), "CN": _s(ST * 2 * L, b16),
+    "NDi": _s(L, i32), "NDf": _s(L, f32), "SI": _s(L, i32), "SF": _s(L, f32), "SH": _s(L, h16),
+    "DI": _s(L, i32), "DF": _s(L, f32), "DH": _s(L, h16),
+    "WA": _s(48, f32), "WB": _s(48, f32), "WC": _s(48, f32), "AL": _s(ST * 24, f32),
+    "RPs": _s(ST * 12, i32), "RPl": _s(ST * 12, i32), "BS": _s(ST * L, u16), "BL": _s(ST * L, u16),
+    "YS": _s(L, f32), "YL": _s(L, f32),
+    "G": _s(4 * 512, f32), "M": _s(3 * 1024, h16), "CB": _s(3 * 1024, b16),
+    "R16": _s(L, u16), "TU": _s(L, u16), "VU": _s(16, u16), "RA": _s(L, b16), "RD": _s(2 * L, b16),
+    "XA": _s(128, f32), "MT1": _s(384, b16), "MT2": _s(384, b16), "NM": _s(L, f32),
+    "TB": _s(3 * 256, f32), "UN": _s(64, b16), "X": _s(256, h16),
+    "OB": _s(16, u16), "BCF": _s(16, f32), "BCS": _s(16, f32), "RB": _s(L, f32), "TH": _s(L, f32),
+    "DD": _s(L, f32), "EE": _s(L, f32), "EQ": _s(L, f32), "SC": _s(L, f32), "T2": _s(16, f32), "OF": _s(24, u16),
+    "U3": _s(8, f32), "CC": _s(8, f32), "TI": _s(8, i32), "FF": _s(144, f32), "PP": _s(144, f32), "SO": _s(144, f32),
+    "MD": _s(12, f32), "RO": _s(576, h16), "OUT": _s(L, f32), "Y1": _s(1024, f32), "Y2": _s(512, f32), "Y3": _s(256, f32),
+    "Y4": _s(256, f32), "NO": _s(128, f32), "YG": _s(256, f32),
+    "PI": _s(4, i32), "PJ": _s(8, i32), "PF": _s(8, f32), "K2": _s(8, f32), "XI": _s(L, f32), "SR": _s(144, f32),
+    "GB": _s(128, f32), "DM": _s(128, f32), "IOT": _s(16, u16), "ONE": _s(1024, b16), "EXP": _s(1024, b16),
+    "WS": _s(144, h16), "W2": _s(144, b16), "W2h": _s(144, h16), "WQ": _s(5 * 144, h16), "ONh": _s(5 * 144, h16),
+    "BD": _s(128, b16), "BDh": _s(128, h16), "BDq": _s(128, h16), "BD8": _s(128, b16), "BD1": _s(128, b16),
+    "TA": _s(128, f32), "TC": _s(128, f32), "TD": _s(128, f32), "T1": _s(128, b16), "T3": _s(128, b16), "NI": _s(128, f32),
+    "Ih": _s(128, h16), "Ib": _s(128, b16), "NEG": _s(128, b16), "TRI": _s(64, h16), "DG": _s(144, f32), "DGh": _s(16, h16),
+    "D0": _s(L, f32), "NS": _s(640, b16), "MON": _s(640, b16), "RT": _s(144, f32), "RU": _s(144, f32), "RV": _s(144, f32),
+    "RZ": _s(144, f32), "LC": _s(16, u16), "LF": _s(16, u16), "JT": _s(16, f32), "JU": _s(16, f32), "JI": _s(16, i32), "JK": _s(16, i32),
+    "CD": _s(144, f32), "RS": _s(144, f32), "LI": _s(16, f32), "LO": _s(16, u16), "BI": _s(L, f32), "BG": _s(L, f32),
+}
+for _n in ("PM0", "PM1", "PL", "PC", "PZ", "PS", "PU", "PX"):
+    SCRATCH[_n] = ("psum", [128, 512], f32)
+
+_LOCAL = ["g0", "g1", "g2", "g3", "fx", "rf", "rw", "cs", "nd", "s0", "s1", "s2", "dp", "oyt", "oyg", "o0", "o1", "o2", "o3"]
+SEMAPHORES = (["eV", "eS", "eT", "eP", "ls"] + _LOCAL + ["yt0", "yt1", "yt2"] + ["cn%d" % t for t in range(ST)]
+              + ["%s%d_%d" % (n, ch, t) for t in range(ST) for ch in range(3) for n in "albr"])
+
+
+class Shape(np.ndarray):
+    def indirect(self, off):
+        return np.zeros((128, 16 * off.shape[1]), np.complex64)
+
+
+def shadow(T):
+    io = {"refs": (128, NV), "gloss": (128, NA), "facts": (128, NA), "cases": (128, L), "need": (ST, L), "vp0": (24, L),
+          "act0": (16, L), "dep0": (1, L), "yt": (128, L), "yg": (128, 256), "yvp": (24, L), "yact": (16, L), "ydep": (1, L)}
+    wide = {f32: np.float32, i32: np.float32}
+    fields = {k: np.zeros(v, np.float16 if k in ("facts", "cases") else np.float32).view(Shape) for k, v in io.items()}
+    fields.update({k: np.zeros(v[1], wide.get(v[2], np.float16)).view(Shape) for k, v in SCRATCH.items()})
+    fields["cores"] = list(T.cores)
+    rec = np.zeros(1, [(k, "O") for k in fields]).view(np.recarray)
+    for k, v in fields.items():
+        rec[k][0] = v
+    return rec[0]
+
+
+CYC, GATHER, SCATTER, FIX, WAKE, FAR, NEAR, PEC = 1.04, 1.56, 3.8, 50.0, 100.0, 2500.0, 1900.0, 0.5
+
+
+def cost(eng, kind, aps, rd):
+    n = int(np.prod(aps[0].shape[1:]))
+    if kind == "d":
+        return 60.0, NEAR
+    if kind == "r":
+        return 300.0, FAR + aps[0].nbytes / 40.0
+    if eng == "P":
+        return 150.0 + 2 * n * CYC, 0.0
+    if eng == "T":
+        return max(min(64, aps[1].shape[1]), aps[2].shape[1]) * PEC * (4 if aps[1].itemsize == 4 else 1), 60.0
+    if aps[0].dtype == np.complex64:
+        return FIX + n * SCATTER * CYC, 0.0
+    if len(aps) > 1 and aps[1].dtype == np.complex64:
+        return FIX + n * GATHER * CYC, 0.0
+    per = 0.5 if eng == "V" and all(a.itemsize == 2 for a in aps) else 1.0
+    if len(aps) == 3 and not any(k[0] == "#" for k in rd):
+        per = 2.0
+    return FIX + max(16, n * per) * CYC, 0.0
+
+
+def depends(ops):
+    writer, readers, last, out = {}, {}, {}, []
+    for i, (eng, fn, rd, wr, ev) in enumerate(ops):
+        deps = set()
+        for k in list(rd) + list(wr):
+            if k in writer:
+                deps.add(writer[k])
+            if k[0] == "#":
+                if k in last and ops[last[k]][0] != eng:
+                    deps.add(last[k])
+                last[k] = i
+        for k in wr:
+            deps.update(readers.get(k, ()))
+        for k in rd:
+            readers.setdefault(k, []).append(i)
+        for k in wr:
+            writer[k] = i
+            readers[k] = []
+        out.append(deps - {i})
+    return out
+
+
+def arrange(ops):
+    single, groups, head = depends(ops), [], {}
+    for i, o in enumerate(ops):
+        if not (i and o[0] == ops[i - 1][0] == "T" and o[3] == ops[i - 1][3]):
+            groups.append([])
+        groups[-1].append(i)
+        head[i] = len(groups) - 1
+    deps = [{head[j] for i in gr for j in single[i]} - {k} for k, gr in enumerate(groups)]
+    each = [cost(o[0], o[1][0], o[1][2], o[2]) if o[0] else (0.0, 0.0) for o in ops]
+    dur = [(sum(each[i][0] for i in gr), each[gr[0]][1]) for gr in groups]
+    ops = [ops[gr[0]] for gr in groups]
+    n = len(ops)
+    sender = {o[1][3]: i for i, o in enumerate(ops) if o[0] and o[1][0] == "r"}
+    loaded, before_load, issue = 1200.0, {}, []
+    for i, o in enumerate(ops):
+        if o[0] is None:
+            deps[i].add(sender[o[4][0]])
+        elif o[1][0] == "d" and not o[2]:
+            if o[0] in before_load:
+                issue.append((before_load[o[0]], i))
+            before_load[o[0]] = i
+            loaded += o[1][2][0].nbytes / 250.0 if o[0] == "Y" else 0.0
+            dur[i] = (60.0, NEAR + (loaded if o[0] == "Y" else 600.0))
+    users = [[] for o in ops]
+    for i in range(n):
+        for j in deps[i]:
+            users[j].append(i)
+    left = [len(d) for d in deps]
+    topo_order, stack = [], [i for i in range(n) if not left[i]]
+    while stack:
+        i = stack.pop()
+        topo_order.append(i)
+        for u in users[i]:
+            left[u] -= 1
+            if not left[u]:
+                stack.append(u)
+    ahead = [0.0] * n
+    for i in reversed(topo_order):
+        ahead[i] = sum(dur[i]) + max([ahead[u] + (0.0 if ops[u][0] == ops[i][0] == "T" else WAKE) for u in users[i]], default=0.0)
+    for a, b in reversed(issue):
+        ahead[a] = max(ahead[a], ahead[b] + 2 * JITTER + 1.0)
+    best_plan = min(fill(ops, deps, users, dur, ahead, seed) for seed in SEEDS)
+    return [i for k in best_plan[1] for i in groups[k]]
+
+
+def fill(ops, deps, users, dur, ahead, seed):
+    n = len(ops)
+    ahead = [a + (seed.get(o[0], 0.0) if d[0] < seed["short"] else 0.0) for a, o, d in zip(ahead, ops, dur)]
+    ahead = [a + (seed["hot"] if (o[3] and o[3][0].startswith(HOT)) or (o[0] == "P" and o[1][0] == "r") else 0.0) for a, o in zip(ahead, ops)]
+    left = [len(d) for d in deps]
+    ready, done, free, order = {}, [0.0] * n, {}, []
+    pool = {e: [] for e in ("V", "S", "T", "P", "Y", None)}
+
+    def release(i):
+        ready[i] = max([done[j] + (-60.0 if ops[j][0] == ops[i][0] == "T" else 0.0 if ops[i][0] is None else WAKE) for j in deps[i]], default=0.0)
+        pool[ops[i][0]].append(i)
+    for i in range(n):
+        if not left[i]:
+            release(i)
+    while len(order) < n:
+        best = None
+        for e, cand in pool.items():
+            if not cand:
+                continue
+            at = max(free.get(e, 0.0), min(ready[i] for i in cand))
+            if best is None or at < best[0]:
+                best = (at, e)
+        at, e = best
+        i = max((j for j in pool[e] if ready[j] <= at + LEEWAY), key=lambda j: (ahead[j], -j))
+        pool[e].remove(i)
+        start = max(at, ready[i])
+        if e is not None:
+            free[e] = start + dur[i][0]
+        done[i] = start + sum(dur[i])
+        order.append(i)
+        for u in users[i]:
+            left[u] -= 1
+            if not left[u]:
+                release(u)
+    return max(done), order
+
+
+LEEWAY, JITTER = 0.0, 10000.0
+SEEDS = [{"short": 250.0, "S": s, "V": v, "hot": h} for s in (2000.0, 5000.0) for v in (0.0, 500.0, 1000.0, 2000.0) for h in (0.0, 1000.0, 2000.0, 4000.0, 8000.0)]
+HOT = ("#PS", "#PU", "#PZ", "#PX", "#PC", "X", "UN", "RPs", "OB", "U3", "CC", "FF", "PP", "SO", "TI", "W")
+PIECES = "100 101 110 111 120 121 200 201 210 300 211 301 220 221 310 311 320 321"
+WRITES = ((0, 1), (2,))
+ZB = ("PZ", "PX", "PZ")
+ON = {"TB": "VVV", "UN": "SSS", "TH": "SSS", "BC": "SSS", "NM": "SSS", "ask": "SSV", "serve": "VVV", "W": "SSS"}
+ORDER = []
+
+
+def emit(g, T, ops):
+    q = {"V": g.vector, "S": g.scalar, "T": g.tensor, "P": g, "Y": g.sync}
+    known = {e: ({}, set()) for e in q}
+    clock, waits, need = [], [], set()
+    every = depends(ops)
+    for i, (eng, fn, rd, wr, ev) in enumerate(ops):
+        deps = every[i]
+        mine = []
+        if eng is not None:
+            kc, ks = known[eng]
+            for j in sorted(deps - {i}, reverse=True):
+                ej, evj = ops[j][0], ops[j][4]
+                if evj is None:
+                    if (ej == eng == "T") or kc.get(ej, -1) >= j:
+                        continue
+                    kc[ej] = j
+                    need.add(j)
+                else:
+                    if j in ks:
+                        continue
+                    ks.add(j)
+                mine.append(j)
+                for e, n in clock[j][0].items():
+                    if kc.get(e, -1) < n:
+                        kc[e] = n
+                ks.update(clock[j][1])
+            clock.append((dict(kc), set(ks)))
+        else:
+            clock.append(({}, set()))
+        waits.append(mine)
+    count, num, sent, seen = {}, {}, 0, set()
+    for i in sorted(need):
+        count[ops[i][0]] = count.get(ops[i][0], 0) + 1
+        num[i] = count[ops[i][0]]
+    for i, (eng, fn, rd, wr, ev) in enumerate(ops):
+        if eng is None:
+            continue
+        for j in waits[i]:
+            if ops[j][4] is None:
+                q[eng].wait_ge(T.sem["e" + ops[j][0]], num[j])
+            else:
+                q[eng].wait_ge(T.sem[ops[j][4][0]], ops[j][4][1])
+                seen.add(j)
+        ins = fn[1]()
+        if fn[0] == "d":
+            ins.then_inc(T.sem[ev[0]], 16)
+        elif fn[0] == "r":
+            sent += NE if ev[0] == "ls" else 0
+        elif i in need:
+            ins.then_inc(T.sem["e" + eng], 1)
+    for i, (eng, fn, rd, wr, ev) in enumerate(ops):
+        if ev is not None and ev[0] != "ls" and i not in seen:
+            g.wait_ge(T.sem[ev[0]], ev[1])
+    g.wait_ge(T.sem["ls"], sent)
+
+
+def rank_program(g, core, T, topo):
+    rank = T.rank_of(core)
+    if rank is None:
+        return
+    if not ORDER:
+        ORDER.extend(arrange(calls(g, core, rank, shadow(T), topo)))
+    ops = calls(g, core, rank, T, topo)
+    emit(g, T, [ops[i] for i in ORDER])
+
+
+def calls(g, core, rank, T, topo):
+    n_ranks = len(T.cores)
+    ops = []
+    V, S, PE = g.vector, g.scalar, g.tensor
+
+    def op(eng, fn, aps, rd, wr):
+        ops.append((eng, ("c", fn, aps), rd, wr, None))
+
+    def ts(out, in0, s1, s2, o0, o1, rd, wr):
+        if o1 is None:
+            op("V", lambda: V.tensor_scalar(out, in0, s1, None, o0), (out, in0), rd, wr)
+        else:
+            op("V", lambda: V.tensor_scalar(out, in0, s1, s2, o0, o1), (out, in0), rd, wr)
+
+    def tt(out, a, b, o, rd, wr):
+        op("V", lambda: V.tensor_tensor(out, a, b, o), (out, a, b), rd, wr)
+
+    def cp(out, a, rd, wr):
+        op("V", lambda: V.tensor_copy(out, a), (out, a), rd, wr)
+
+    def ms(out, val, wr):
+        op("V", lambda: V.memset(out, val), (out,), [], wr)
+
+    def scan(out, d0, d1, rd, wr):
+        op("V", lambda: V.tensor_tensor_scan(out, d0, d1, 0.0, A.mult, A.add), (out, d0), rd, wr)
+
+    def act(out, a, fn, rd, wr, bias=0.0, scale=1.0):
+        op("S", lambda: S.activation(out, a, fn, bias=bias, scale=scale), (out, a), rd, wr)
+
+    def lin(on, out, a, scale, bias, rd, wr):
+        if on == "S":
+            act(out, a, F.Identity, rd, wr, bias=bias, scale=scale)
+        else:
+            ts(out, a, scale, bias, A.mult, A.add, rd, wr)
+
+    def mm(out, lt, rhs, start, stop, rd, bank):
+        op("T", lambda: PE.matmul(out, lt, rhs, start, stop), (out, lt, rhs), rd, [bank])
+
+    def iota(out, pat, base, cm, wr, integer=False):
+        if integer:
+            op("P", lambda: g.iota(out, pat, base, cm), (out,), [], wr + ["pool"])
+        else:
+            op("P", lambda: g.iota(out, pat, base, cm, allow_small_or_imprecise_dtypes=True), (out,), [], wr + ["pool"])
+
+    def sel(out, a, pat, base, cm, rd, wr):
+        op("P", lambda: g.affine_select(out, a, pat, A.is_equal, 0.0, base, cm), (out,), rd, wr + ["pool"])
+
+    def dma(eng, sem, out, a, rd, wr):
+        e = {"Y": g.sync, "S": S}[eng]
+        ops.append((eng, ("d", lambda: e.dma_start(out, a), (out,)), rd, wr, (sem, 16)))
+
+    def send(dst_rank, out, a, sem, rd, local="ls"):
+        dst = T.cores[dst_rank]
+        rid, pid = topo.addr(dst)[:2]
+        bits = sum(1 << e for e in topo.engines(core, dst)[:NE])
+        ops.append(("P", ("r", lambda: g.remote_dma(out, a, T.sem[sem], T.sem[local], pid, rid, bits), (out,), sem), rd, [], (local, NE)))
+
+    def arrive(sem, wr):
+        ops.append((None, None, [], wr, (sem, NE)))
+
+    def partner(t):
+        return (rank + 1 + t % (n_ranks - 1)) % n_ranks
+
+    def asker(t):
+        return (rank - 1 - t % (n_ranks - 1)) % n_ranks
+
+    def run(fs):
+        for fn in fs:
+            fn()
+
+    def weave(a, b):
+        for j in range(max(len(a), len(b))):
+            for x in (a, b):
+                if j < len(x):
+                    x[j]()
+
+    W = (T.WA, T.WB, T.WC)
+    r15, g16, r3, gg = (T.PF[:, j:j + 1] for j in range(4))
+    k2, dum = T.K2[:, 0:1], T.K2[:, 4:5]
+    TABK = ["TAB0", "TAB1", "TAB2", "TAB3"]
+
+    for j in range(4):
+        dma("Y", "g%d" % j, T.GI[:, 1024 * j:1024 * j + 1024], T.gloss[:, 1024 * j:1024 * j + 1024], [], ["GI%d" % j])
+    dma("Y", "fx", T.FX[:], T.facts[:], [], ["FX"])
+    dma("S", "s0", T.SI[0:24, :], T.vp0[:], [], ["SI0"])
+    dma("S", "s1", T.SI[24:32, :], T.act0[8:16, :], [], ["SI1"])
+    dma("S", "s2", T.SI[32:40, :], T.act0[0:8, :], [], ["SI2"])
+    dma("S", "dp", T.DI[0:1, :], T.dep0[:], [], ["DI"])
+    dma("S", "rf", T.RF[:, 0:NV], T.refs[:], [], ["RF0"])
+    dma("S", "rw", T.RF[:, NV:NV + 8], T.refs[:, 0:8], [], ["RF1"])
+    dma("S", "cs", T.CS[:], T.cases[:], [], ["CS"])
+    dma("S", "nd", T.NDi[64:64 + ST, :], T.need[:], [], ["NDi"])
+
+    ms(T.ONh[0:64, :], 1.0, ["ONh"])
+    ms(T.ONE[0:64, :], 1.0, ["ONE"])
+    iota(T.PI[:, 0:1], [[0, 1]], 0, 1, ["PI"], True)
+    iota(T.SR[:], [[0, 9], [1, 16]], 0, 0, ["SR"])
+    sel(T.WQ[0:64, :], T.ONh[0:64, :], [[128, 5], [1, 144]], -15, -16, ["ONh"], ["WQ"])
+    iota(T.XI[:, 0:144], [[1, 144]], 0, 0, ["XI"])
+    iota(T.GB[:], [[16, 8], [0, 16]], 0, 0, ["GB"])
+    iota(T.DM[:], [[1, 128]], 0, -1, ["DM"])
+    sel(T.EXP[0:64, :], T.ONE[0:64, :], [[-1, 64], [0, 16]], 0, 1, ["ONE"], ["EXP"])
+    for ch in range(3):
+        ms(W[ch][:, 24:36], 0.0, ["Wt%d" % ch])
+        ms(W[ch][:, 36:40], 1.0, ["Wk%d" % ch])
+        ms(W[ch][:, 40:44], 2.0, ["Wl%d" % ch])
+        ms(W[ch][:, 44:48], 0.0, ["Wv%d" % ch])
+    ms(T.TAB[:, NA:TW], 0.0, ["TABx"])
+    ms(T.CNs[64:128, :], 0.0, ["CNn"])
+    for j, (num, o) in enumerate(((15, A.bitwise_and), (112, A.bitwise_and), (3, A.bitwise_and), (4, A.logical_shift_right))):
+        ts(T.PJ[:, j:j + 1], T.PI[:, 0:1], num, None, o, None, ["PI"], ["PJ%d" % j])
+    ts(T.W2h[:], T.SR[:], 15.0, None, A.is_equal, None, ["SR"], ["W2h"])
+    cp(T.PF[:, 0:4], T.PJ[:, 0:4], ["PJ%d" % j for j in range(4)], ["PF"])
+    cp(T.SF[0:40, :], T.SI[0:40, :], ["SI0", "SI1", "SI2"], ["SF"])
+    cp(T.DF[0:1, :], T.DI[0:1, :], ["DI"], ["DF"])
+    cp(T.SH[0:40, :], T.SF[0:40, :], ["SF"], ["SH"])
+    cp(T.DH[0:1, :], T.DF[0:1, :], ["DF"], ["DH"])
+    for qq in (5, 0, 1, 2, 3, 4):
+        for r in range(16):
+            if qq < 5:
+                mm(T.PZ[:, 12 * qq:12 * qq + 12], T.WQ[0:40, 144 * qq + 15 - r:144 * qq + 143 - r], T.SH[0:40, r:L:16], r == 0, r == 15, ["WQ", "SH"], "#PZ")
+            else:
+                mm(T.PZ[:, 60:72], T.W2h[0:1, 15 - r:143 - r], T.DH[0:1, r:L:16], r == 0, r == 15, ["W2h", "DH"], "#PZ")
+    ts(T.DG[:], T.SR[:], r15, None, A.is_equal, None, ["SR", "PF"], ["DG"])
+    cp(T.IOT[:], T.XI[:, 0:16], ["XI"], ["IOT"])
+    ts(T.BD[:], T.GB[:], g16, None, A.is_equal, None, ["GB", "PF"], ["BD"])
+    ts(T.WS[:], T.XI[:, 0:144], -15.0, g16, A.add, A.is_equal, ["XI", "PF"], ["WS"])
+    ts(T.Ib[:], T.DM[:], 0.0, None, A.is_equal, None, ["DM"], ["Ib"])
+
+    def wk(ch):
+        return ["W%d_%d" % (ch, qq) for qq in range(6)]
+
+    def wall(ch):
+        return wk(ch) + [x + str(ch) for x in ("Wt", "Wk", "Wl", "Wv")]
+
+    def start_state(ch):
+        c0 = LO[ch] // 16
+        for qq in range(6):
+            act(W[ch][:, 4 * qq:4 * qq + 4], T.PZ[:, 12 * qq + c0:12 * qq + c0 + 4], F.Copy, ["#PZ"], [wk(ch)[qq]])
+        act(W[ch][:, 44:48], T.PZ[:, c0:c0 + 4], F.Identity, ["#PZ"], ["Wv%d" % ch], bias=1.0)
+
+    def convert(j):
+        ts(T.TAB[:, 1024 * j:1024 * j + 1024], T.GI[:, 1024 * j:1024 * j + 1024], -2048.0, None, A.add, None, ["GI%d" % j], [TABK[j]])
+
+    def turn_cases():
+        for ch in range(3):
+            mm(T.PS[0:64, 128 * ch:128 * ch + 128], T.CS[:, LO[ch]:LO[ch] + 64], T.Ib[:], True, True, ["CS", "Ib"], "#PS")
+        act(T.CNs[0:64, :], T.PS[0:64, 0:384], F.Copy, ["#PS"], ["CNc"])
+        cp(T.NDf[64:64 + ST, :], T.NDi[64:64 + ST, :], ["NDi"], ["NDf"])
+        ts(T.CNs[64:64 + ST, 0:L], T.NDf[64:64 + ST, :], 2.0, -1.0, A.mult, A.add, ["NDf"], ["CNn"])
+
+    def send_cases(t):
+        send(partner(t), T.CN[:, 2 * L * t:2 * L * (t + 1)], T.CNs[:], "cn%d" % t, ["CNc", "CNn"])
+
+    def later_constants():
+        ts(k2, r15, 2048.0, None, A.mult, None, ["PF"], ["K2"])
+        ts(dum, r15, float(NA + 1), None, A.add, None, ["PF"], ["dum"])
+        ts(T.NEG[:], T.SR[:, 0:128], -1.0, None, A.mult, None, ["SR"], ["NEG"])
+        ts(T.W2[:], T.SR[:], 15.0, -2.0, A.is_equal, A.mult, ["SR"], ["W2c"])
+        ts(T.BDh[:], T.GB[:], g16, None, A.is_equal, None, ["GB", "PF"], ["BDh"])
+        ts(T.BDq[:], T.GB[:], g16, 0.25, A.is_equal, A.mult, ["GB", "PF"], ["BDq"])
+        ts(T.BD8[:], T.GB[:], g16, 8192.0, A.is_equal, A.mult, ["GB", "PF"], ["BD8"])
+        ts(T.BD1[:], T.GB[:], g16, 1024.0, A.is_equal, A.mult, ["GB", "PF"], ["BD1"])
+        ts(T.TA[:], T.DM[:], 0.0, -2048.0, A.is_gt, A.mult, ["DM"], ["TA"])
+        ts(T.TC[:], T.DM[:], 0.0, 2048.0, A.is_equal, A.mult, ["DM"], ["TC"])
+        ts(T.NI[:], T.DM[:], 0.0, -1.0, A.is_equal, A.mult, ["DM"], ["NI"])
+        ts(T.Ih[:], T.DM[:], 0.0, None, A.is_equal, None, ["DM"], ["Ih"])
+        tt(T.TA[:], T.TA[:], T.TC[:], A.add, ["TA", "TC"], ["TA"])
+        ts(T.TRI[:], T.SR[:, 0:64], r15, 16384.0, A.is_gt, A.mult, ["SR", "PF"], ["TRI"])
+        ts(T.TD[:], T.DG[:, 0:128], -17.0, 1.0, A.mult, A.add, ["DG"], ["TD"])
+        tt(T.T1[:], T.TA[:], T.BD[:], A.mult, ["TA", "BD"], ["T1"])
+        ts(T.RZ[:], T.SR[:], 0.0, None, A.not_equal, None, ["SR"], ["RZ"])
+        ms(T.MON[64:72, :], 1.0, ["MON"])
+        ts(T.T3[:], T.T1[:], -1.0, None, A.mult, None, ["T1"], ["T3"])
+        tt(T.D0[:, 0:128], T.TD[:], T.RZ[:, 0:128], A.mult, ["TD", "RZ"], ["D0"])
+        for ch in range(3):
+            ms(T.TB[:, 256 * ch + 192:256 * ch + 256], 14336.0, ["TBc%d" % ch])
+            ms(T.TB[:, 256 * ch + 128:256 * ch + 192], 0.0, ["TBd%d" % ch])
+        ms(T.CC[:], 0.0, ["CC"])
+        ms(T.NO[0:1, :], -1.0, ["NO"])
+        sel(T.NS[64:72, :], T.MON[64:72, :], [[-1, ST], [0, 128]], 0, 1, ["MON"], ["NS"])
+
+    moves = ((0, 0, 11), (0, 1, 1), (0, 2, 2), (0, 3, 6), (0, 4, 6), (0, 5, 11), (1, 3, 11), (2, 4, 11),
+             (3, 4, 7), (3, 2, 8), (4, 3, 7), (4, 1, 8))
+
+    def update_lists():
+        iota(T.RT[:, 0:120], [[4, 5], [1, 4], [0, 6]], 0, 0, ["RT"])
+        iota(T.RT[:, 120:144], [[1, 4], [4, 3], [0, 2]], 32, 0, ["RTd"])
+        for n, (qq, slot, blk) in enumerate(moves):
+            ap = T.RT[:, 24 * qq + slot:24 * qq + 24:6]
+            act(ap, ap, F.Identity, ["RT"], ["RT%d" % n], bias=float(4 * (blk - qq)))
+        iota(T.CD[:], [[0, 24], [1, 6]], 0, 0, ["CD"])
+        iota(T.JT[:], [[16, 16]], 0, 0, ["JT"])
+        iota(T.LI[:, 0:12], [[4, 6], [0, 2]], 0, 0, ["LI"])
+        iota(T.BI[:], [[0, 6], [1, 8], [0, 4]], 0, 0, ["BI"])
+
+    def update_lists_2():
+        tt(T.RU[:], T.RT[:], T.DG[:], A.mult, ["DG", "RTd"] + ["RT%d" % n for n in range(len(moves))], ["RU"])
+        ts(T.JU[:], T.JT[:], r15, -2.5, A.add, A.add, ["JT", "PF"], ["JU"])
+        scan(T.RV[:], T.RZ[:], T.RU[:], ["RZ", "RU"], ["RV"])
+        ts(T.JI[:], T.JU[:], 1.0 / 6.0, None, A.mult, None, ["JU"], ["JI"])
+        ts(T.RS[:], T.CD[:], 0.0, None, A.not_equal, None, ["CD"], ["RS"])
+        cp(T.LC[:, 0:9], T.RV[:, 15:144:16], ["RV"], ["LC"])
+        ts(T.JK[:], T.JI[:], 3, None, A.bitwise_and, None, ["JI"], ["JK"])
+        ts(T.LO[:, 0:12], T.LI[:, 0:12], r3, None, A.add, None, ["LI", "PF"], ["LO"])
+        cp(T.LF[:], T.JK[:], ["JK"], ["LF"])
+        ts(T.BG[:], T.BI[:], gg, None, A.is_equal, None, ["BI", "PF"], ["BG"])
+        cp(T.DGh[:], T.DG[:, 0:16], ["DG"], ["DGh"])
+
+    def act_mask(ch, src, key, mt, name, on):
+        out = mt[0:64, 128 * ch:128 * ch + 128]
+        if on == "S":
+            mm(T.PC[0:64, 128:256], T.ONE[0:1, 0:64], T.NEG[0:1, :], True, False, ["ONE", "NEG"], "#PC")
+            mm(T.PC[0:64, 128:256], src, T.BD[:], False, True, [key, "BD"], "#PC")
+            act(T.XA[0:64, :], T.PC[0:64, 128:256], F.Abs, ["#PC"], ["XA"])
+            act(out, T.XA[0:64, :], F.Relu, ["XA"], [name], bias=1.0, scale=-1.0)
+            return lambda: None
+        mm(T.PC[0:64, 128:256], src, T.BD[:], True, True, [key, "BD"], "#PC")
+        return lambda: tt(out, T.PC[0:64, 128:256], T.SR[0:64, 0:128], A.is_equal, ["#PC", "SR"], [name])
+
+    def ask_ops(ch, t, on):
+        w, lo = W[ch], LO[ch]
+        c0, al = lo // 16, 24 * t + 8 * ch
+        later = []
+
+        def acts():
+            send(partner(t), T.AL[:, al:al + 8], w[:, 16:24], "a%d_%d" % (ch, t), wk(ch)[4:6], "l%d_%d" % (ch, t))
+            tt(T.RA[:, lo:lo + 64], w[:, 8:16].indirect(T.IOT[:, 4:8]), T.DG[:, 0:64], A.mult, wk(ch)[2:4] + ["IOT", "DG"], ["RA%d" % ch])
+            later.append(act_mask(ch, T.RA[:, lo:lo + 64], "RA%d" % ch, T.MT2, "MT2%d" % ch, on))
+        return [acts,
+                lambda: cp(T.VU[:, c0:c0 + 4], w[:, 0:4], wk(ch)[0:1], ["VU%d" % ch]),
+                lambda: cp(T.R16[:, lo:lo + 64], T.RF[:].indirect(T.VU[:, c0:c0 + 4]), ["RF0", "RF1", "VU%d" % ch], ["R16%d" % ch]),
+                lambda: later[0]()]
+
+    def serve_ops(ch, t, on):
+        al, key, lo = 24 * t + 8 * ch, "AL%d_%d" % (ch, t), LO[ch]
+        later = []
+
+        def first():
+            arrive("a%d_%d" % (ch, t), [key])
+            tt(T.RD[:, 128 * ch:128 * ch + 128], T.AL[:, al:al + 8].indirect(T.IOT[:, 0:8]), T.DG[:, 0:128], A.mult, [key, "IOT", "DG"], ["RD%d" % ch])
+            later.append(act_mask(ch, T.RD[:, 128 * ch:128 * ch + 64], "RD%d" % ch, T.MT1, "MT1%d" % ch, on))
+
+        def second():
+            later[0]()
+            mm(T.PU[:, 128:192], T.MT1[0:64, 128 * ch:128 * ch + 128], T.Ib[0:64, 0:64], True, True, ["MT1%d" % ch, "Ib"], "#PU")
+            lin(ON["NM"][ch], T.NM[:, lo:lo + 64], T.PU[:, 128:192], -1.0, 1.0, ["#PU"], ["NM%d" % ch])
+        return [first, second]
+
+    def gather(t, n, level, ch, p):
+        lo = LO[ch] + 32 * p
+        win, wkeys = T.TAB[:, 0:NA], TABK
+        if level == 1:
+            off, key = T.R16[:, lo:lo + 32], "R16%d" % ch
+        elif level == 2:
+            off, key = T.BL[:, L * t + lo:L * t + lo + 32], "BL%d_%d" % (t, ch)
+            if p == 0:
+                arrive("b%d_%d" % (ch, t), [key])
+        else:
+            off, key, win, wkeys = T.TU[:, lo:lo + 32], "TU%d" % ch, T.FX[:], ["FX"]
+        act(T.G[:, 512 * (n % 4):512 * (n % 4) + 512], win.indirect(off), F.Copy, wkeys + [key], ["G%d" % (n % 4)])
+
+    def widen(t, n, level, ch, p):
+        if level == 3:
+            if ch == 0 and p == 0:
+                arrive("cn%d" % t, ["CN%d" % t])
+            src, key = T.CN[0:64, 2 * L * t + 128 * ch:2 * L * t + 128 * ch + 128], "CN%d" % t
+        else:
+            src, key = (T.MT2, T.MT1)[level - 1][0:64, 128 * ch:128 * ch + 128], "MT%d%d" % (3 - level, ch)
+        mm(T["PM%d" % (n % 2)][:], src, T.EXP[0:64, 512 * p:512 * p + 512], True, True, [key, "EXP"], "#PM%d" % (n % 2))
+
+    def mask(t, n, level, ch, p):
+        m = ch
+        out, key, o = (T.CB, "CB", A.is_le) if level == 3 else (T.M, "M", A.mult)
+        tt(out[:, 1024 * m + 512 * p:1024 * m + 512 * p + 512], T.G[:, 512 * (n % 4):512 * (n % 4) + 512], T["PM%d" % (n % 2)][:], o,
+           ["G%d" % (n % 4), "#PM%d" % (n % 2)], ["%s%d_%d" % (key, m, p)])
+
+    def pick(level, ch):
+        m = ch
+        for k in range(16):
+            mm(T.PL[:, 0:64], T.WS[:, 15 - k:143 - k], T.M[:, 1024 * m + k:1024 * m + 1024:16], k == 0, k == 15,
+               ["WS", "M%d_0" % m, "M%d_1" % m], "#PL")
+
+    def send_b(t, ch):
+        o = L * t + LO[ch]
+        ts(T.BS[:, o:o + 64], T.PL[:, 0:64], 2048.0, None, A.add, None, ["#PL"], ["BS%d_%d" % (t, ch)])
+        send(partner(t), T.BL[:, o:o + 64], T.BS[:, o:o + 64], "b%d_%d" % (ch, t), ["BS%d_%d" % (t, ch)])
+
+    def take_t(t, ch):
+        lo, o = LO[ch], 256 * ch
+        ts(T.TU[:, lo:lo + 64], T.PL[:, 0:64], 2048.0, None, A.add, None, ["#PL"], ["TU%d" % ch])
+        ts(T.TB[:, o + 64:o + 128], T.BL[:, L * t + lo:L * t + lo + 64], k2, 14336.0, A.add, A.add, ["BL%d_%d" % (t, ch), "K2"], ["TBb%d" % ch])
+        lin(ON["TB"][ch], T.TB[:, o:o + 64], T.PL[:, 0:64], 1.0, k2, ["#PL", "K2"], ["TBa%d" % ch])
+        if t == ST - 1:
+            lin(ON["TB"][ch], T.YS[:, lo:lo + 64], T.PL[:, 0:64], 1.0, 2048.0, ["#PL"], ["YS%d" % ch])
+            send(asker(t), T.YL[:, lo:lo + 64], T.YS[:, lo:lo + 64], "yt%d" % ch, ["YS%d" % ch])
+
+    def count(t, ch):
+        lo, o, m = LO[ch], 256 * ch, ch
+        nd = 2 * L * t + lo
+        mm(T.PC[:, 0:64], T.NS[64:72, 128 * t:128 * t + 128], T.CN[64:72, nd:nd + 64], True, False, ["NS", "CN%d" % t], "#PC")
+        for k in range(16):
+            mm(T.PC[:, 0:64], T.W2[:, 15 - k:143 - k], T.CB[:, 1024 * m + k:1024 * m + 1024:16], False, k == 15,
+               ["W2c", "CB%d_0" % m, "CB%d_1" % m], "#PC")
+
+    def before(ch):
+        o = 256 * ch
+        z, zk = T[ZB[ch]], "#" + ZB[ch]
+        mm(z[:, 0:256], T.NI[:], T.TB[:, o:o + 256], True, False, ["NI"] + ["TB%s%d" % (x, ch) for x in "abcd"], zk)
+        mm(z[:, 128:192], T.NI[:], T.TB[:, o:o + 64], False, False, ["NI", "TBa%d" % ch], zk)
+        mm(z[:, 64:128], T.BD8[:], T.RD[:, 128 * ch + 64:128 * ch + 128], False, False, ["BD8", "RD%d" % ch], zk)
+
+    def signs(ch):
+        if ON["UN"][ch] == "S":
+            act(T.UN[:], T.PC[:, 0:64], F.Sign, ["#PC"], ["UN"])
+        else:
+            ts(T.UN[:], T.PC[:, 0:64], -1.0, 1.0, A.max, A.min, ["#PC"], ["UN"])
+        for j, (lt, key) in enumerate(((T.T1, "T1"), (T.T1, "T1"), (T.T3, "T3"), (T.BD1, "BD1"))):
+            mm(T[ZB[ch]][:, 64 * j:64 * j + 64], lt[:], T.UN[:], False, j == 3, [key, "UN"], "#" + ZB[ch])
+
+    def verdict(ch):
+        ts(T.X[:], T[ZB[ch]][:, 0:256], 0.0, -2048.0, A.max, A.add, ["#" + ZB[ch]], ["X"])
+        mm(T.PU[:, 0:64], T.Ih[:], T.TRI[:], True, False, ["Ih", "TRI"], "#PU")
+        mm(T.PU[:, 0:64], T.BDh[:], T.X[:, 64:128], False, False, ["BDh", "X"], "#PU")
+        mm(T.PU[:, 0:64], T.BDq[:], T.X[:, 192:256], False, True, ["BDq", "X"], "#PU")
+        mm(T.PU[:, 64:128], T.BDh[:], T.X[:, 128:192], True, True, ["BDh", "X"], "#PU")
+        for r in range(16):
+            mm(T.PS[:, 0:8], T.WS[:, 15 - r:143 - r], T.X[:, r:128:16], r == 0, r == 15, ["WS", "X"], "#PS")
+
+    def answer(t, ch):
+        lo = LO[ch]
+        o, c = 12 * t + lo // 16, (lo // 16 - 4) % 12
+        lin(ON["TH"][ch], T.TH[:, lo:lo + 64], T.PU[:, 64:128], -1.0, -30720.0, ["#PU"], ["TH%d" % ch])
+        lin(ON["TH"][ch], T.RB[:, lo:lo + 64], T.PU[:, 0:64], -1.0, -36864.0, ["#PU"], ["RB%d" % ch])
+        ts(T.OB[:, c:c + 4], T.PS[:, 4:8], -1.0, -28672.0, A.mult, A.add, ["#PS"], ["OB%d" % ch])
+        ts(T.RPs[:, o:o + 4], T.PS[:, 0:4], -1.0, -28672.0, A.mult, A.add, ["#PS"], ["RPs%d_%d" % (t, ch)])
+        send(asker(t), T.RPl[:, o:o + 4], T.RPs[:, o:o + 4], "r%d_%d" % (ch, t), ["RPs%d_%d" % (t, ch)])
+        lin(ON["BC"][ch], T.BCF[:, c:c + 4], T.PS[:, 4:8], -1.0, -28672.0, ["#PS"], ["BCF%d" % ch])
+        lin(ON["BC"][ch], T.BCS[:, c:c + 4], T.PS[:, 4:8], -1.0 / 8192.0, -2.5, ["#PS"], ["BCS%d" % ch])
+
+    def write_ops(chs):
+        C, lo, s = 4 * len(chs), LO[chs[-1]], str(chs[0])
+        ln = slice(lo, lo + 16 * C)
+        c0 = (lo // 16 - 4) % 12
+        cs = slice(c0, c0 + C)
+
+        def k(name):
+            return [name + str(ch) for ch in chs]
+        return [
+            lambda: tt(T.DD[:, ln], T.TAB[:].indirect(T.OB[:, cs]), T.TH[:, ln], A.subtract, TABK + ["TABx"] + k("OB") + k("TH"), ["DD" + s]),
+            lambda: tt(T.EQ[:, ln], T.BCF[:, cs].indirect(T.IOT[:, 0:C]), T.RB[:, ln], A.is_equal, ["IOT"] + k("BCF") + k("RB"), ["EQ" + s]),
+            lambda: tt(T.EE[:, ln], T.DD[:, ln], T.NM[:, ln], A.mult, ["DD" + s] + k("NM"), k("EE")),
+            lambda: scan(T.SC[:, ln], T.D0[:, 0:16 * C], T.EQ[:, ln], ["D0", "EQ" + s], ["SC" + s]),
+            lambda: tt(T.T2[:, cs], T.BCS[:, cs], T.SC[:, lo + 15:lo + 16 * C:16], A.subtract, k("BCS") + ["SC" + s], ["T2" + s]),
+            lambda: ts(T.OF[:, lo // 8:lo // 8 + 2 * C:2], T.T2[:, cs], 8192.0, dum, A.mult, A.min, ["T2" + s, "dum"], k("OF")),
+        ]
+
+    def scatter(c):
+        ch, ln = 2 - c // 4, slice(16 * c, 16 * c + 16)
+        return lambda: tt(T.TAB[:].indirect(T.OF[:, 2 * c:2 * c + 1]), T.TH[:, ln], T.EE[:, ln], A.add,
+                          ["OF%d" % ch, "EE%d" % ch, "TH%d" % ch], TABK + ["TABx"])
+
+    def update_ops(ch, t):
+        w, o = W[ch], 12 * t + LO[ch] // 16
+        rp, rk = T.RPl[:, o:o + 4], ["RPl%d_%d" % (t, ch)]
+
+        def first():
+            arrive("r%d_%d" % (ch, t), rk)
+            ts(T.U3[:, 0:4], rp, float(NA), 3.0, A.is_lt, A.mult, rk, ["U3"])
+
+        def back():
+            lin(ON["W"][ch], w[:, 0:24], T.SO[:, 5:144:6], 1.0, 0.0, ["SO"], wk(ch))
+            lin(ON["W"][ch], w[:, 44:48], T.SO[:, 5:24:6], 1.0, 1.0, ["SO"], ["Wv%d" % ch])
+        return [
+            first,
+            lambda: ts(T.TI[:, 0:4], rp, NV - 1, None, A.bitwise_and, None, rk, ["TI0"]),
+            lambda: ts(T.TI[:, 4:8], rp, 15, None, A.bitwise_and, None, rk, ["TI1"]),
+            lambda: tt(T.CC[:, 0:4], w[:, 20:24], T.U3[:, 0:4], A.add, [wk(ch)[5], "U3"], ["CC"]),
+            lambda: cp(w[:, 24:32], T.TI[:], ["TI0", "TI1"], ["Wt%d" % ch]),
+            lambda: tt(T.FF[:], T.CC[:].indirect(T.LF[:, 0:9]), T.CD[:], A.is_equal, ["CC", "LF", "CD"], ["FF"]),
+            lambda: tt(T.PP[:], w[:].indirect(T.LC[:, 0:9]), T.FF[:], A.mult, wall(ch) + ["LC", "FF"], ["PP"]),
+            lambda: scan(T.SO[:], T.RS[:], T.PP[:], ["RS", "PP"], ["SO"]),
+            back,
+        ]
+
+    def final_ops(ch):
+        w, o, lo = W[ch], L * ch, LO[ch]
+
+        def turn():
+            tt(T.RO[:, o:o + L], w[:].indirect(T.LO[:, 0:12]), T.BG[:], A.mult, wall(ch) + ["LO", "BG"], ["RO%d" % ch])
+            for c in range(4):
+                mm(T.PL[0:48, 16 * c:16 * c + 16], T.RO[:, o + c:o + L:4], T.DGh[:], True, True, ["RO%d" % ch, "DGh"], "#PL")
+            act(T.OUT[0:48, lo:lo + 64], T.PL[0:48, 0:64], F.Copy, ["#PL"], ["OUT%d" % ch])
+        return [
+            lambda: ts(T.MD[:], w[:, 0:12], float(NV), -float(NV), A.is_ge, A.mult, wk(ch)[0:3], ["MD"]),
+            lambda: tt(w[:, 0:12], w[:, 0:12], T.MD[:], A.add, wk(ch)[0:3] + ["MD"], wk(ch)[0:3]),
+            turn]
+
+    convert(0)
+    for ch in range(3):
+        start_state(ch)
+    convert(1)
+    run(ask_ops(0, 0, "V"))
+    convert(2)
+    turn_cases()
+    run(ask_ops(1, 0, "V"))
+    send_cases(0)
+    convert(3)
+    run(ask_ops(2, 0, "V"))
+    update_lists()
+
+    later_constants()
+    update_lists_2()
+    for t in range(ST):
+        more = t + 1 < ST
+        run(serve_ops(0, t, ON["serve"][0]))
+        run(serve_ops(1, t, ON["serve"][1]))
+        if t:
+            run(update_ops(2, t - 1) + ask_ops(2, t, ON["ask"][2]))
+        run(serve_ops(2, t, ON["serve"][2]))
+        if more:
+            send_cases(t + 1)
+        for n, name in enumerate(PIECES.split()):
+            level, ch, p = (int(x) for x in name)
+            gather(t, n, level, ch, p)
+            widen(t, n, level, ch, p)
+            mask(t, n, level, ch, p)
+            if p == 1 and level == 1:
+                pick(1, ch)
+                send_b(t, ch)
+            elif p == 1 and level == 2:
+                pick(2, ch)
+                take_t(t, ch)
+                if ch < 2:
+                    before(ch)
+            elif p == 1:
+                if ch == 2:
+                    before(ch)
+                count(t, ch)
+                signs(ch)
+                verdict(ch)
+                answer(t, ch)
+        for chs in WRITES:
+            run(write_ops(chs))
+        run([scatter(c) for c in range(11, -1, -1)])
+        for ch in (0, 1):
+            run(update_ops(ch, t) + (ask_ops(ch, t + 1, ON["ask"][ch]) if more else final_ops(ch)))
+
+    for ch in range(3):
+        arrive("yt%d" % ch, ["YL%d" % ch])
+    dma("Y", "oyt", T.yt[:], T.YL[:], ["YL0", "YL1", "YL2"], [])
+    ms(T.Y4[0:1, :], 32768.0, ["Y4"])
+    mm(T.PC[:, 0:256], T.NO[0:1, :], T.Y4[0:1, :], True, False, ["NO", "Y4"], "#PC")
+    for m in range(10):
+        mm(T.PC[:, 0:256], T.NI[:], T.TAB[:, 256 * m:256 * m + 256], False, m == 9, ["NI"] + TABK, "#PC")
+    tt(T.Y1[:, 0:768], T.TAB[:, 2560:3328], T.TAB[:, 3328:4096], A.add, TABK, ["Y1"])
+    run(update_ops(2, ST - 1) + final_ops(2))
+    outs = ["OUT0", "OUT1", "OUT2"]
+    dma("S", "o0", T.yvp[:], T.OUT[0:24, :], outs, [])
+    dma("Y", "o1", T.yact[8:16, :], T.OUT[24:32, :], outs, [])
+    dma("S", "o2", T.yact[0:8, :], T.OUT[32:40, :], outs, [])
+    dma("Y", "o3", T.ydep[:], T.OUT[40:41, :], outs, [])
+    tt(T.Y2[:, 0:256], T.Y1[:, 0:256], T.Y1[:, 256:512], A.add, ["Y1"], ["Y2"])
+    tt(T.Y3[:], T.Y2[:, 0:256], T.Y1[:, 512:768], A.add, ["Y1", "Y2"], ["Y3"])
+    tt(T.YG[:], T.Y3[:], T.PC[:, 0:256], A.subtract, ["Y3", "#PC"], ["YG"])
+    dma("Y", "oyg", T.yg[:], T.YG[:], ["YG"], [])
+    return ops

@@ -6,6 +6,8 @@ A, F = AluOpType, ActivationFunctionType
 L, ST, NA, NV = 192, 5, 4096, 512
 TW = NA + 32
 LO = (128, 64, 0)
+SET_OF = (0, 1, 2)
+SETS = (((0,), 4, 128), ((1,), 4, 64), ((2,), 4, 0))
 NE = 8
 
 f32, b16, h16, i32, u16 = "float32", "bfloat16", "float16", "int32", "uint16"
@@ -20,33 +22,33 @@ SCRATCH = {
     "CNs": _s(2 * L, b16), "CN": _s(ST * 2 * L, b16),
     "NDi": _s(L, i32), "NDf": _s(L, f32), "SI": _s(L, i32), "SF": _s(L, f32), "SH": _s(L, h16),
     "DI": _s(L, i32), "DF": _s(L, f32), "DH": _s(L, h16),
-    "WA": _s(48, f32), "WB": _s(48, f32), "WC": _s(48, f32), "AL": _s(ST * 24, f32),
+    "WA": _s(96, f32), "WB": _s(96, f32), "WC": _s(96, f32), "LA": _s(16, u16), "I8": _s(128, b16), "AL": _s(ST * 24, f32),
     "RPs": _s(ST * 12, i32), "RPl": _s(ST * 12, i32), "BS": _s(ST * L, u16), "BL": _s(ST * L, u16),
     "YS": _s(L, f32), "YL": _s(L, f32),
-    "G": _s(4 * 512, f32), "M": _s(3 * 1024, h16), "CB": _s(3 * 1024, b16),
+    "CX": _s(6 * 512, b16), "G": _s(4 * 512, f32), "M": _s(3 * 1024, h16), "CB": _s(3 * 1024, b16),
     "R16": _s(L, u16), "TU": _s(L, u16), "VU": _s(16, u16), "RA": _s(L, b16), "RD": _s(2 * L, b16),
     "XA": _s(128, f32), "MT1": _s(384, b16), "MT2": _s(384, b16), "NM": _s(L, f32),
-    "TB": _s(3 * 256, f32), "UN": _s(64, b16), "X": _s(256, h16),
+    "TB": _s(3 * 256, h16), "UN": _s(64, b16), "X": _s(256, h16),
     "OB": _s(16, u16), "BCF": _s(16, f32), "BCS": _s(16, f32), "RB": _s(L, f32), "TH": _s(L, f32),
-    "DD": _s(L, f32), "EE": _s(L, f32), "EQ": _s(L, f32), "SC": _s(L, f32), "T2": _s(16, f32), "OF": _s(24, u16),
-    "U3": _s(8, f32), "CC": _s(8, f32), "TI": _s(8, i32), "FF": _s(144, f32), "PP": _s(144, f32), "SO": _s(144, f32),
-    "MD": _s(12, f32), "RO": _s(576, h16), "OUT": _s(L, f32), "Y1": _s(1024, f32), "Y2": _s(512, f32), "Y3": _s(256, f32),
+    "DD": _s(L, f32), "EQ": _s(L, f32), "SC": _s(L, f32), "T2": _s(16, f32), "OF": _s(24, u16),
+    "U3": _s(8, f32), "CC": _s(8, f32), "TI": _s(16, i32), "FF": _s(288, f32), "PP": _s(288, f32), "SO": _s(288, f32),
+    "MD": _s(24, f32), "RO": _s(576, h16), "OUT": _s(L, f32), "Y1": _s(1024, f32), "Y2": _s(512, f32), "Y3": _s(256, f32),
     "Y4": _s(256, f32), "NO": _s(128, f32), "YG": _s(256, f32),
-    "PI": _s(4, i32), "PJ": _s(8, i32), "PF": _s(8, f32), "K2": _s(8, f32), "XI": _s(L, f32), "SR": _s(144, f32),
+    "PI": _s(4, i32), "PJ": _s(8, i32), "PF": _s(8, f32), "K2": _s(8, f32), "XI": _s(L, f32), "SR": _s(432, f32),
     "GB": _s(128, f32), "DM": _s(128, f32), "IOT": _s(16, u16), "ONE": _s(1024, b16), "EXP": _s(1024, b16),
     "WS": _s(144, h16), "W2": _s(144, b16), "W2h": _s(144, h16), "WQ": _s(5 * 144, h16), "ONh": _s(5 * 144, h16),
     "BD": _s(128, b16), "BDh": _s(128, h16), "BDq": _s(128, h16), "BD8": _s(128, b16), "BD1": _s(128, b16),
     "TA": _s(128, f32), "TC": _s(128, f32), "TD": _s(128, f32), "T1": _s(128, b16), "T3": _s(128, b16), "NI": _s(128, f32),
-    "Ih": _s(128, h16), "Ib": _s(128, b16), "NEG": _s(128, b16), "TRI": _s(64, h16), "DG": _s(144, f32), "DGh": _s(16, h16),
-    "D0": _s(L, f32), "NS": _s(640, b16), "MON": _s(640, b16), "RT": _s(144, f32), "RU": _s(144, f32), "RV": _s(144, f32),
-    "RZ": _s(144, f32), "LC": _s(16, u16), "LF": _s(16, u16), "JT": _s(16, f32), "JU": _s(16, f32), "JI": _s(16, i32), "JK": _s(16, i32),
-    "CD": _s(144, f32), "RS": _s(144, f32), "LI": _s(16, f32), "LO": _s(16, u16), "BI": _s(L, f32), "BG": _s(L, f32),
+    "Ih": _s(256, h16), "Ib": _s(128, b16), "NEG": _s(640, b16), "TRI": _s(64, h16), "DG": _s(432, f32), "DGh": _s(16, h16),
+    "D0": _s(L, f32), "NS": _s(640, b16), "MON": _s(640, b16), "RT": _s(432, f32), "RU": _s(432, f32), "RV": _s(432, f32),
+    "RZ": _s(432, f32), "LC": _s(32, u16), "LF": _s(32, u16), "JT": _s(18, f32), "JU": _s(18, f32), "JI": _s(18, i32), "JK": _s(32, i32),
+    "CD": _s(288, f32), "RS": _s(288, f32), "LI": _s(36, f32), "LO": _s(36, u16), "BI": _s(576, f32), "BG": _s(576, f32),
 }
 for _n in ("PM0", "PM1", "PL", "PC", "PZ", "PS", "PU", "PX"):
     SCRATCH[_n] = ("psum", [128, 512], f32)
 
-_LOCAL = ["g0", "g1", "g2", "g3", "fx", "rf", "rw", "cs", "nd", "s0", "s1", "s2", "dp", "oyt", "oyg", "o0", "o1", "o2", "o3"]
-SEMAPHORES = (["eV", "eS", "eT", "eP", "ls"] + _LOCAL + ["yt0", "yt1", "yt2"] + ["cn%d" % t for t in range(ST)]
+_LOCAL = ["g0", "g1", "g2", "g3", "fx", "rf", "rw", "cs", "nd", "s0", "s1", "s2", "dp", "oyt", "oyg", "o0", "o1", "o2", "o3", "ex"]
+SEMAPHORES = (["eV", "eS", "eT", "eP", "ls"] + _LOCAL + ["yt0", "yt1", "yt2"] + ["%s%d" % (n, t) for t in range(ST) for n in ("cn", "h")]
               + ["%s%d_%d" % (n, ch, t) for t in range(ST) for ch in range(3) for n in "albr"])
 
 
@@ -68,7 +70,10 @@ def shadow(T):
     return rec[0]
 
 
-CYC, GATHER, SCATTER, FIX, WAKE, FAR, NEAR, PEC = 1.04, 1.56, 3.8, 50.0, 100.0, 2500.0, 1900.0, 0.5
+CYC, GATHER, SCATTER, FIX, WAKE, FAR, NEAR, PEC = 0.85, 1.56, 3.8, 50.0, 100.0, 2300.0, 1900.0, 0.43
+
+
+ISSUE = 400.0
 
 
 def cost(eng, kind, aps, rd):
@@ -76,7 +81,7 @@ def cost(eng, kind, aps, rd):
     if kind == "d":
         return 60.0, NEAR
     if kind == "r":
-        return 300.0, FAR + aps[0].nbytes / 40.0
+        return ISSUE, FAR + aps[0].nbytes / 40.0
     if eng == "P":
         return 150.0 + 2 * n * CYC, 0.0
     if eng == "T":
@@ -84,11 +89,11 @@ def cost(eng, kind, aps, rd):
     if aps[0].dtype == np.complex64:
         return FIX + n * SCATTER * CYC, 0.0
     if len(aps) > 1 and aps[1].dtype == np.complex64:
-        return FIX + n * GATHER * CYC, 0.0
+        return FIX + 25.0 + n * GATHER * CYC, 0.0
     per = 0.5 if eng == "V" and all(a.itemsize == 2 for a in aps) else 1.0
     if len(aps) == 3 and not any(k[0] == "#" for k in rd):
         per = 2.0
-    return FIX + max(16, n * per) * CYC, 0.0
+    return FIX + (25.0 if eng == "S" else 10.0) + max(16, n * per) * CYC, 0.0
 
 
 def depends(ops):
@@ -161,7 +166,7 @@ def arrange(ops):
 def fill(ops, deps, users, dur, ahead, seed):
     n = len(ops)
     ahead = [a + (seed.get(o[0], 0.0) if d[0] < seed["short"] else 0.0) for a, o, d in zip(ahead, ops, dur)]
-    ahead = [a + (seed["hot"] if (o[3] and o[3][0].startswith(HOT)) or (o[0] == "P" and o[1][0] == "r") else 0.0) for a, o in zip(ahead, ops)]
+    ahead = [a + sum(v for k, v in seed["first"].items() if o[3] and o[3][0].startswith(k)) for a, o in zip(ahead, ops)]
     left = [len(d) for d in deps]
     ready, done, free, order = {}, [0.0] * n, {}, []
     pool = {e: [] for e in ("V", "S", "T", "P", "Y", None)}
@@ -181,7 +186,7 @@ def fill(ops, deps, users, dur, ahead, seed):
             if best is None or at < best[0]:
                 best = (at, e)
         at, e = best
-        i = max((j for j in pool[e] if ready[j] <= at + LEEWAY), key=lambda j: (ahead[j], -j))
+        i = max((j for j in pool[e] if ready[j] <= at + seed.get("wait" + str(e), 0.0)), key=lambda j: (ahead[j], -j))
         pool[e].remove(i)
         start = max(at, ready[i])
         if e is not None:
@@ -196,9 +201,15 @@ def fill(ops, deps, users, dur, ahead, seed):
 
 
 LEEWAY, JITTER = 0.0, 10000.0
-SEEDS = [{"short": 250.0, "S": s, "V": v, "hot": h} for s in (2000.0, 5000.0) for v in (0.0, 500.0, 1000.0, 2000.0) for h in (0.0, 1000.0, 2000.0, 4000.0, 8000.0)]
-HOT = ("#PS", "#PU", "#PZ", "#PX", "#PC", "X", "UN", "RPs", "OB", "U3", "CC", "FF", "PP", "SO", "TI", "W")
-PIECES = "100 101 110 111 120 121 200 201 210 300 211 301 220 221 310 311 320 321"
+SEEDS = [{'short': 250.0, 'S': 500.0, 'V': 1000.0, 'T': 1000.0, 'waitS': 200.0, 'first': {
+    'TAB': 4000.0, 'TI': -1000.0, 'M0': -1000.0, 'SC': -2000.0, 'EE': 200.0, 'OB': 2000.0, 'RA': -2000.0, '#PS': -200.0, 'CC': 2000.0,
+    'BC': -1000.0, '#PC': 500.0, 'NM': -2000.0, 'CB': -200.0, 'UN': -200.0, 'U3': 500.0, '#PL': 200.0, 'FF': -2000.0, 'RPs': 4000.0,
+    'M1': 200.0, 'T2': -200.0, 'TH': -2000.0, 'M2': 2000.0, 'G': -2000.0, 'XA': -1000.0, 'W': 2000.0, 'VU': -1000.0, 'OF': -1000.0,
+    'BS': 4000.0, 'RD': 500.0, 'TB': -200.0, '#PX': -1000.0, '#PZ': -2000.0, '#PM': -2000.0, 'PP': 200.0, 'TU': -200.0, 'R16': 200.0,
+    'CX': 2000.0, 'MT': -200.0, 'EQ': 4000.0, 'RB': 200.0}}]
+PIECES = "100 101 110 111 120 121 200 201 210 211 300 301 220 221 310 311 320 321"
+FUSED = ["301", "311", "321"]
+CUT = (0, 1280, 2560, 3584, 4096)
 WRITES = ((0, 1), (2,))
 ZB = ("PZ", "PX", "PZ")
 ON = {"TB": "VVV", "UN": "SSS", "TH": "SSS", "BC": "SSS", "NM": "SSS", "ask": "SSV", "serve": "VVV", "W": "SSS"}
@@ -348,12 +359,13 @@ def calls(g, core, rank, T, topo):
                     x[j]()
 
     W = (T.WA, T.WB, T.WC)
-    r15, g16, r3, gg = (T.PF[:, j:j + 1] for j in range(4))
+    r15, g16, r3, gg, r7 = (T.PF[:, j:j + 1] for j in range(5))
     k2, dum = T.K2[:, 0:1], T.K2[:, 4:5]
+    KEYS = ["KR%d" % j for j in range(5)]
     TABK = ["TAB0", "TAB1", "TAB2", "TAB3"]
 
     for j in range(4):
-        dma("Y", "g%d" % j, T.GI[:, 1024 * j:1024 * j + 1024], T.gloss[:, 1024 * j:1024 * j + 1024], [], ["GI%d" % j])
+        dma("Y", "g%d" % j, T.GI[:, CUT[j]:CUT[j + 1]], T.gloss[:, CUT[j]:CUT[j + 1]], [], ["GI%d" % j])
     dma("Y", "fx", T.FX[:], T.facts[:], [], ["FX"])
     dma("S", "s0", T.SI[0:24, :], T.vp0[:], [], ["SI0"])
     dma("S", "s1", T.SI[24:32, :], T.act0[8:16, :], [], ["SI1"])
@@ -367,23 +379,23 @@ def calls(g, core, rank, T, topo):
     ms(T.ONh[0:64, :], 1.0, ["ONh"])
     ms(T.ONE[0:64, :], 1.0, ["ONE"])
     iota(T.PI[:, 0:1], [[0, 1]], 0, 1, ["PI"], True)
-    iota(T.SR[:], [[0, 9], [1, 16]], 0, 0, ["SR"])
+    iota(T.SR[:], [[0, 27], [1, 16]], 0, 0, ["SR"])
     sel(T.WQ[0:64, :], T.ONh[0:64, :], [[128, 5], [1, 144]], -15, -16, ["ONh"], ["WQ"])
     iota(T.XI[:, 0:144], [[1, 144]], 0, 0, ["XI"])
     iota(T.GB[:], [[16, 8], [0, 16]], 0, 0, ["GB"])
     iota(T.DM[:], [[1, 128]], 0, -1, ["DM"])
     sel(T.EXP[0:64, :], T.ONE[0:64, :], [[-1, 64], [0, 16]], 0, 1, ["ONE"], ["EXP"])
-    for ch in range(3):
-        ms(W[ch][:, 24:36], 0.0, ["Wt%d" % ch])
-        ms(W[ch][:, 36:40], 1.0, ["Wk%d" % ch])
-        ms(W[ch][:, 40:44], 2.0, ["Wl%d" % ch])
-        ms(W[ch][:, 44:48], 0.0, ["Wv%d" % ch])
+    dma("S", "ex", T.EXP[64:128, :], T.EXP[0:64, :], ["EXP"], ["EXP2"])
+    for s, (chs, C, lo) in enumerate(SETS):
+        ms(W[s][:, 6 * C:9 * C], 0.0, ["Wt%d" % s])
+        ms(W[s][:, 9 * C:10 * C], 1.0, ["Wk%d" % s])
+        ms(W[s][:, 10 * C:11 * C], 2.0, ["Wl%d" % s])
     ms(T.TAB[:, NA:TW], 0.0, ["TABx"])
     ms(T.CNs[64:128, :], 0.0, ["CNn"])
-    for j, (num, o) in enumerate(((15, A.bitwise_and), (112, A.bitwise_and), (3, A.bitwise_and), (4, A.logical_shift_right))):
+    for j, (num, o) in enumerate(((15, A.bitwise_and), (112, A.bitwise_and), (3, A.bitwise_and), (4, A.logical_shift_right), (7, A.bitwise_and))):
         ts(T.PJ[:, j:j + 1], T.PI[:, 0:1], num, None, o, None, ["PI"], ["PJ%d" % j])
-    ts(T.W2h[:], T.SR[:], 15.0, None, A.is_equal, None, ["SR"], ["W2h"])
-    cp(T.PF[:, 0:4], T.PJ[:, 0:4], ["PJ%d" % j for j in range(4)], ["PF"])
+    ts(T.W2h[:], T.SR[:, 0:144], 15.0, None, A.is_equal, None, ["SR"], ["W2h"])
+    cp(T.PF[:, 0:5], T.PJ[:, 0:5], ["PJ%d" % j for j in range(5)], ["PF"])
     cp(T.SF[0:40, :], T.SI[0:40, :], ["SI0", "SI1", "SI2"], ["SF"])
     cp(T.DF[0:1, :], T.DI[0:1, :], ["DI"], ["DF"])
     cp(T.SH[0:40, :], T.SF[0:40, :], ["SF"], ["SH"])
@@ -406,14 +418,20 @@ def calls(g, core, rank, T, topo):
     def wall(ch):
         return wk(ch) + [x + str(ch) for x in ("Wt", "Wk", "Wl", "Wv")]
 
-    def start_state(ch):
-        c0 = LO[ch] // 16
-        for qq in range(6):
-            act(W[ch][:, 4 * qq:4 * qq + 4], T.PZ[:, 12 * qq + c0:12 * qq + c0 + 4], F.Copy, ["#PZ"], [wk(ch)[qq]])
-        act(W[ch][:, 44:48], T.PZ[:, c0:c0 + 4], F.Identity, ["#PZ"], ["Wv%d" % ch], bias=1.0)
+    def start_state(s):
+        C, c0 = SETS[s][1], SETS[s][2] // 16
+        for qq in (0, 3, 4, 5, 1, 2):
+            act(W[s][:, C * qq:C * qq + C], T.PZ[:, 12 * qq + c0:12 * qq + c0 + C], F.Copy, ["#PZ"], [wk(s)[qq]])
+        act(W[s][:, 11 * C:12 * C], T.PZ[:, c0:c0 + C], F.Identity, ["#PZ"], ["Wv%d" % s], bias=1.0)
+
+    def rows(ch):
+        return slice(64, 128) if LO[ch] > SETS[SET_OF[ch]][2] else slice(0, 64)
+
+    def lanes_first(mt, ch):
+        return mt[rows(ch), 128 * SET_OF[ch]:128 * SET_OF[ch] + 128]
 
     def convert(j):
-        ts(T.TAB[:, 1024 * j:1024 * j + 1024], T.GI[:, 1024 * j:1024 * j + 1024], -2048.0, None, A.add, None, ["GI%d" % j], [TABK[j]])
+        ts(T.TAB[:, CUT[j]:CUT[j + 1]], T.GI[:, CUT[j]:CUT[j + 1]], -2048.0, None, A.add, None, ["GI%d" % j], [TABK[j]])
 
     def turn_cases():
         for ch in range(3):
@@ -423,13 +441,13 @@ def calls(g, core, rank, T, topo):
         ts(T.CNs[64:64 + ST, 0:L], T.NDf[64:64 + ST, :], 2.0, -1.0, A.mult, A.add, ["NDf"], ["CNn"])
 
     def send_cases(t):
-        send(partner(t), T.CN[:, 2 * L * t:2 * L * (t + 1)], T.CNs[:], "cn%d" % t, ["CNc", "CNn"])
+        send(partner(t), T.CN[:, 2 * L * t:2 * L * (t + 1)], T.CNs[:], "cn%d" % t, ["CNc", "CNn"] + (["BS%d_2" % (t - 1)] if t else []))
 
     def later_constants():
-        ts(k2, r15, 2048.0, None, A.mult, None, ["PF"], ["K2"])
         ts(dum, r15, float(NA + 1), None, A.add, None, ["PF"], ["dum"])
-        ts(T.NEG[:], T.SR[:, 0:128], -1.0, None, A.mult, None, ["SR"], ["NEG"])
-        ts(T.W2[:], T.SR[:], 15.0, -2.0, A.is_equal, A.mult, ["SR"], ["W2c"])
+        ts(T.NEG[0:1, 0:128], T.SR[0:1, 0:128], -1.0, None, A.mult, None, ["SR"], ["NEG"])
+        ts(T.W2[:], T.SR[:, 0:144], 15.0, -2.0, A.is_equal, A.mult, ["SR"], ["W2c"])
+        ts(T.I8[:], T.DM[:], 0.0, -8192.0, A.is_equal, A.mult, ["DM"], ["I8"])
         ts(T.BDh[:], T.GB[:], g16, None, A.is_equal, None, ["GB", "PF"], ["BDh"])
         ts(T.BDq[:], T.GB[:], g16, 0.25, A.is_equal, A.mult, ["GB", "PF"], ["BDq"])
         ts(T.BD8[:], T.GB[:], g16, 8192.0, A.is_equal, A.mult, ["GB", "PF"], ["BD8"])
@@ -437,7 +455,7 @@ def calls(g, core, rank, T, topo):
         ts(T.TA[:], T.DM[:], 0.0, -2048.0, A.is_gt, A.mult, ["DM"], ["TA"])
         ts(T.TC[:], T.DM[:], 0.0, 2048.0, A.is_equal, A.mult, ["DM"], ["TC"])
         ts(T.NI[:], T.DM[:], 0.0, -1.0, A.is_equal, A.mult, ["DM"], ["NI"])
-        ts(T.Ih[:], T.DM[:], 0.0, None, A.is_equal, None, ["DM"], ["Ih"])
+        ts(T.Ih[:, 0:128], T.DM[:], 0.0, None, A.is_equal, None, ["DM"], ["Ih"])
         tt(T.TA[:], T.TA[:], T.TC[:], A.add, ["TA", "TC"], ["TA"])
         ts(T.TRI[:], T.SR[:, 0:64], r15, 16384.0, A.is_gt, A.mult, ["SR", "PF"], ["TRI"])
         ts(T.TD[:], T.DG[:, 0:128], -17.0, 1.0, A.mult, A.add, ["DG"], ["TD"])
@@ -446,9 +464,9 @@ def calls(g, core, rank, T, topo):
         ms(T.MON[64:72, :], 1.0, ["MON"])
         ts(T.T3[:], T.T1[:], -1.0, None, A.mult, None, ["T1"], ["T3"])
         tt(T.D0[:, 0:128], T.TD[:], T.RZ[:, 0:128], A.mult, ["TD", "RZ"], ["D0"])
-        for ch in range(3):
-            ms(T.TB[:, 256 * ch + 192:256 * ch + 256], 14336.0, ["TBc%d" % ch])
-            ms(T.TB[:, 256 * ch + 128:256 * ch + 192], 0.0, ["TBd%d" % ch])
+        ts(T.Ih[:, 128:256], T.DM[:], 0.0, -1.0, A.is_equal, A.mult, ["DM"], ["NIh"])
+        for key, (a, b, val) in zip(KEYS, ((128, 320, 2048.0), (320, 448, 0.0), (448, 512, -16384.0), (512, 576, 0.0), (576, 640, -14336.0))):
+            ms(T.NEG[0:1, a:b], val, [key])
         ms(T.CC[:], 0.0, ["CC"])
         ms(T.NO[0:1, :], -1.0, ["NO"])
         sel(T.NS[64:72, :], T.MON[64:72, :], [[-1, ST], [0, 128]], 0, 1, ["MON"], ["NS"])
@@ -457,90 +475,99 @@ def calls(g, core, rank, T, topo):
              (3, 4, 7), (3, 2, 8), (4, 3, 7), (4, 1, 8))
 
     def update_lists():
-        iota(T.RT[:, 0:120], [[4, 5], [1, 4], [0, 6]], 0, 0, ["RT"])
-        iota(T.RT[:, 120:144], [[1, 4], [4, 3], [0, 2]], 32, 0, ["RTd"])
-        for n, (qq, slot, blk) in enumerate(moves):
-            ap = T.RT[:, 24 * qq + slot:24 * qq + 24:6]
-            act(ap, ap, F.Identity, ["RT"], ["RT%d" % n], bias=float(4 * (blk - qq)))
-        iota(T.CD[:], [[0, 24], [1, 6]], 0, 0, ["CD"])
-        iota(T.JT[:], [[16, 16]], 0, 0, ["JT"])
-        iota(T.LI[:, 0:12], [[4, 6], [0, 2]], 0, 0, ["LI"])
-        iota(T.BI[:], [[0, 6], [1, 8], [0, 4]], 0, 0, ["BI"])
+        for C, o in ((8, 0), (4, 288)):
+            iota(T.RT[:, o:o + 30 * C], [[C, 5], [1, C], [0, 6]], 0, 0, ["RT%d" % C])
+            iota(T.RT[:, o + 30 * C:o + 36 * C], [[1, C], [C, 3], [0, 2]], 8 * C, 0, ["RTd%d" % C])
+            for n, (qq, slot, blk) in enumerate(moves):
+                ap = T.RT[:, o + 6 * C * qq + slot:o + 6 * C * (qq + 1):6]
+                act(ap, ap, F.Identity, ["RT%d" % C], ["RT%d_%d" % (C, n)], bias=float(C * (blk - qq)))
+        iota(T.CD[:], [[0, 48], [1, 6]], 0, 0, ["CD"])
+        iota(T.JT[:], [[16, 18]], 0, 0, ["JT"])
+        iota(T.LI[:, 0:24], [[8, 6], [0, 4]], 0, 0, ["LI8"])
+        iota(T.LI[:, 24:36], [[4, 6], [0, 2]], 0, 0, ["LI4"])
+        iota(T.BI[:, 0:384], [[0, 6], [1, 8], [0, 8]], 0, 0, ["BI8"])
+        iota(T.BI[:, 384:576], [[0, 6], [1, 8], [0, 4]], 0, 0, ["BI4"])
 
     def update_lists_2():
-        tt(T.RU[:], T.RT[:], T.DG[:], A.mult, ["DG", "RTd"] + ["RT%d" % n for n in range(len(moves))], ["RU"])
+        tt(T.RU[:], T.RT[:], T.DG[:], A.mult, ["DG", "RTd8", "RTd4"] + ["RT%d_%d" % (C, n) for C in (8, 4) for n in range(len(moves))], ["RU"])
         ts(T.JU[:], T.JT[:], r15, -2.5, A.add, A.add, ["JT", "PF"], ["JU"])
         scan(T.RV[:], T.RZ[:], T.RU[:], ["RZ", "RU"], ["RV"])
         ts(T.JI[:], T.JU[:], 1.0 / 6.0, None, A.mult, None, ["JU"], ["JI"])
         ts(T.RS[:], T.CD[:], 0.0, None, A.not_equal, None, ["CD"], ["RS"])
-        cp(T.LC[:, 0:9], T.RV[:, 15:144:16], ["RV"], ["LC"])
-        ts(T.JK[:], T.JI[:], 3, None, A.bitwise_and, None, ["JI"], ["JK"])
-        ts(T.LO[:, 0:12], T.LI[:, 0:12], r3, None, A.add, None, ["LI", "PF"], ["LO"])
-        cp(T.LF[:], T.JK[:], ["JK"], ["LF"])
-        ts(T.BG[:], T.BI[:], gg, None, A.is_equal, None, ["BI", "PF"], ["BG"])
+        cp(T.LC[:, 0:27], T.RV[:, 15:432:16], ["RV"], ["LC"])
+        ts(T.JK[:, 0:18], T.JI[:], 7, None, A.bitwise_and, None, ["JI"], ["JK8"])
+        ts(T.JK[:, 18:27], T.JI[:, 0:9], 3, None, A.bitwise_and, None, ["JI"], ["JK4"])
+        ts(T.LO[:, 0:24], T.LI[:, 0:24], r7, None, A.add, None, ["LI8", "PF"], ["LO0"])
+        ts(T.LO[:, 24:36], T.LI[:, 24:36], r3, None, A.add, None, ["LI4", "PF"], ["LO1"])
+        cp(T.LF[:, 0:27], T.JK[:, 0:27], ["JK8", "JK4"], ["LF"])
+        ts(T.BG[:], T.BI[:], gg, None, A.is_equal, None, ["BI8", "BI4", "PF"], ["BG"])
         cp(T.DGh[:], T.DG[:, 0:16], ["DG"], ["DGh"])
+        for C in sorted({s[1] for s in SETS}):
+            ts(T.LA[:, C:2 * C], T.XI[:, 0:C], 6.0, 18.0 * C + 5.0, A.mult, A.add, ["XI"], ["LA"])
 
     def act_mask(ch, src, key, mt, name, on):
-        out = mt[0:64, 128 * ch:128 * ch + 128]
+        n = 16 * SETS[ch][1]
+        out, x = mt[0:n, 128 * ch:128 * ch + 128], T.PC[0:n, 128:256]
         if on == "S":
-            mm(T.PC[0:64, 128:256], T.ONE[0:1, 0:64], T.NEG[0:1, :], True, False, ["ONE", "NEG"], "#PC")
-            mm(T.PC[0:64, 128:256], src, T.BD[:], False, True, [key, "BD"], "#PC")
-            act(T.XA[0:64, :], T.PC[0:64, 128:256], F.Abs, ["#PC"], ["XA"])
-            act(out, T.XA[0:64, :], F.Relu, ["XA"], [name], bias=1.0, scale=-1.0)
-            return lambda: None
-        mm(T.PC[0:64, 128:256], src, T.BD[:], True, True, [key, "BD"], "#PC")
-        return lambda: tt(out, T.PC[0:64, 128:256], T.SR[0:64, 0:128], A.is_equal, ["#PC", "SR"], [name])
+            mm(x, T.ONE[0:1, 0:n], T.NEG[0:1, 0:128], True, False, ["ONE", "NEG"], "#PC")
+            mm(x, src, T.BD[:], False, True, [key, "BD"], "#PC")
+            act(T.XA[0:n, :], x, F.Abs, ["#PC"], ["XA"])
+            act(out, T.XA[0:n, :], F.Relu, ["XA"], [name], bias=1.0, scale=-1.0)
+        else:
+            mm(x, src, T.BD[:], True, True, [key, "BD"], "#PC")
+            tt(out, x, T.SR[0:n, 0:128], A.is_equal, ["#PC", "SR"], [name])
 
-    def ask_ops(ch, t, on):
-        w, lo = W[ch], LO[ch]
-        c0, al = lo // 16, 24 * t + 8 * ch
-        later = []
+    def ask(s, t, on):
+        chs, C, lo = SETS[s]
+        w, c0, al, ln = W[s], lo // 16, 24 * t + lo // 8, slice(lo, lo + 16 * C)
+        w0 = 3 * C // 8 * 8
+        send(partner(t), T.AL[:, al:al + 2 * C], w[:, 4 * C:6 * C], "a%d_%d" % (s, t), wk(s)[4:6], "l%d_%d" % (s, t))
+        if t:
+            cp(T.VU[:, c0:c0 + C], T.SO[:, 5:6 * C:6], ["SO"], ["VU%d" % s])
+        else:
+            cp(T.VU[:, c0:c0 + C], w[:, 0:C], wk(s)[0:1], ["VU%d" % s])
+        cp(T.R16[:, ln], T.RF[:].indirect(T.VU[:, c0:c0 + C]), ["RF0", "RF1", "VU%d" % s], ["R16%d" % s])
+        if t:
+            tt(T.RA[:, ln], T.SO[:, 0:36 * C].indirect(T.LA[:, C:2 * C]), T.DG[:, 0:16 * C], A.mult, ["SO", "LA", "DG"], ["RA%d" % s])
+        else:
+            tt(T.RA[:, ln], w[:, w0:4 * C].indirect(T.IOT[:, 3 * C - w0:4 * C - w0]), T.DG[:, 0:16 * C], A.mult,
+               wk(s)[w0 // C:4] + ["IOT", "DG"], ["RA%d" % s])
+        act_mask(s, T.RA[:, ln], "RA%d" % s, T.MT2, "MT2%d" % s, on)
 
-        def acts():
-            send(partner(t), T.AL[:, al:al + 8], w[:, 16:24], "a%d_%d" % (ch, t), wk(ch)[4:6], "l%d_%d" % (ch, t))
-            tt(T.RA[:, lo:lo + 64], w[:, 8:16].indirect(T.IOT[:, 4:8]), T.DG[:, 0:64], A.mult, wk(ch)[2:4] + ["IOT", "DG"], ["RA%d" % ch])
-            later.append(act_mask(ch, T.RA[:, lo:lo + 64], "RA%d" % ch, T.MT2, "MT2%d" % ch, on))
-        return [acts,
-                lambda: cp(T.VU[:, c0:c0 + 4], w[:, 0:4], wk(ch)[0:1], ["VU%d" % ch]),
-                lambda: cp(T.R16[:, lo:lo + 64], T.RF[:].indirect(T.VU[:, c0:c0 + 4]), ["RF0", "RF1", "VU%d" % ch], ["R16%d" % ch]),
-                lambda: later[0]()]
-
-    def serve_ops(ch, t, on):
-        al, key, lo = 24 * t + 8 * ch, "AL%d_%d" % (ch, t), LO[ch]
-        later = []
-
-        def first():
-            arrive("a%d_%d" % (ch, t), [key])
-            tt(T.RD[:, 128 * ch:128 * ch + 128], T.AL[:, al:al + 8].indirect(T.IOT[:, 0:8]), T.DG[:, 0:128], A.mult, [key, "IOT", "DG"], ["RD%d" % ch])
-            later.append(act_mask(ch, T.RD[:, 128 * ch:128 * ch + 64], "RD%d" % ch, T.MT1, "MT1%d" % ch, on))
-
-        def second():
-            later[0]()
-            mm(T.PU[:, 128:192], T.MT1[0:64, 128 * ch:128 * ch + 128], T.Ib[0:64, 0:64], True, True, ["MT1%d" % ch, "Ib"], "#PU")
-            lin(ON["NM"][ch], T.NM[:, lo:lo + 64], T.PU[:, 128:192], -1.0, 1.0, ["#PU"], ["NM%d" % ch])
-        return [first, second]
+    def serve(s, t, on):
+        chs, C, lo = SETS[s]
+        al, key, o, n = 24 * t + lo // 8, "AL%d_%d" % (s, t), 2 * lo, 16 * C
+        arrive("a%d_%d" % (s, t), [key])
+        tt(T.RD[:, o:o + 2 * n], T.AL[:, al:al + 2 * C].indirect(T.IOT[:, 0:2 * C]), T.DG[:, 0:2 * n], A.mult, [key, "IOT", "DG"], ["RD%d" % s])
+        act_mask(s, T.RD[:, o:o + n], "RD%d" % s, T.MT1, "MT1%d" % s, on)
+        for ch in chs:
+            a = 128 + LO[ch] - lo
+            mm(T.PU[:, a:a + 64], lanes_first(T.MT1, ch), T.Ib[rows(ch), rows(ch)], True, True, ["MT1%d" % s, "Ib"], "#PU")
+        lin(ON["NM"][s], T.NM[:, lo:lo + n], T.PU[:, 128:128 + n], -16384.0, 8192.0, ["#PU"], ["NM%d" % ch for ch in chs])
 
     def gather(t, n, level, ch, p):
         lo = LO[ch] + 32 * p
         win, wkeys = T.TAB[:, 0:NA], TABK
         if level == 1:
-            off, key = T.R16[:, lo:lo + 32], "R16%d" % ch
+            off, key = T.R16[:, lo:lo + 32], "R16%d" % SET_OF[ch]
         elif level == 2:
             off, key = T.BL[:, L * t + lo:L * t + lo + 32], "BL%d_%d" % (t, ch)
             if p == 0:
                 arrive("b%d_%d" % (ch, t), [key])
+            elif ch == 0:
+                key = "BH%d" % t
+                arrive("h%d" % t, [key])
         else:
             off, key, win, wkeys = T.TU[:, lo:lo + 32], "TU%d" % ch, T.FX[:], ["FX"]
         act(T.G[:, 512 * (n % 4):512 * (n % 4) + 512], win.indirect(off), F.Copy, wkeys + [key], ["G%d" % (n % 4)])
 
     def widen(t, n, level, ch, p):
         if level == 3:
-            if ch == 0 and p == 0:
-                arrive("cn%d" % t, ["CN%d" % t])
             src, key = T.CN[0:64, 2 * L * t + 128 * ch:2 * L * t + 128 * ch + 128], "CN%d" % t
         else:
-            src, key = (T.MT2, T.MT1)[level - 1][0:64, 128 * ch:128 * ch + 128], "MT%d%d" % (3 - level, ch)
-        mm(T["PM%d" % (n % 2)][:], src, T.EXP[0:64, 512 * p:512 * p + 512], True, True, [key, "EXP"], "#PM%d" % (n % 2))
+            src, key = lanes_first((T.MT2, T.MT1)[level - 1], ch), "MT%d%d" % (3 - level, SET_OF[ch])
+        at = rows(ch) if level < 3 else slice(0, 64)
+        mm(T["PM%d" % (n % 2)][:], src, T.EXP[at, 512 * p:512 * p + 512], True, True, [key, "EXP2" if at.start else "EXP"], "#PM%d" % (n % 2))
 
     def mask(t, n, level, ch, p):
         m = ch
@@ -548,11 +575,30 @@ def calls(g, core, rank, T, topo):
         tt(out[:, 1024 * m + 512 * p:1024 * m + 512 * p + 512], T.G[:, 512 * (n % 4):512 * (n % 4) + 512], T["PM%d" % (n % 2)][:], o,
            ["G%d" % (n % 4), "#PM%d" % (n % 2)], ["%s%d_%d" % (key, m, p)])
 
+    def wide_cases(t, n):
+        arrive("cn%d" % t, ["CN%d" % t])
+        for j, name in enumerate(FUSED):
+            widen(t, n + j, 3, int(name[1]), int(name[2]))
+            bank = "PM%d" % ((n + j) % 2)
+            act(T.CX[:, 512 * j:512 * j + 512], T[bank][:], F.Copy, ["#" + bank], ["CX%d" % j])
+
+    def compare(t, ch, p):
+        j, lo = FUSED.index("3%d%d" % (ch, p)), LO[ch] + 32 * p
+        tt(T.CB[:, 1024 * ch + 512 * p:1024 * ch + 512 * p + 512], T.FX[:].indirect(T.TU[:, lo:lo + 32]), T.CX[:, 512 * j:512 * j + 512],
+           A.is_le, ["FX", "TU%d" % ch, "CX%d" % j], ["CB%d_%d" % (ch, p)])
+
     def pick(level, ch):
         m = ch
         for k in range(16):
             mm(T.PL[:, 0:64], T.WS[:, 15 - k:143 - k], T.M[:, 1024 * m + k:1024 * m + 1024:16], k == 0, k == 15,
                ["WS", "M%d_0" % m, "M%d_1" % m], "#PL")
+
+    def send_half(t, p):
+        o, key = L * t + LO[0] + 32 * p, "BS%d_0%d" % (t, p)
+        for k in range(16):
+            mm(T.PL[:, 0:32], T.WS[:, 15 - k:143 - k], T.M[:, 512 * p + k:512 * p + 512:16], k == 0, k == 15, ["WS", "M0_%d" % p], "#PL")
+        ts(T.BS[:, o:o + 32], T.PL[:, 0:32], 2048.0, None, A.add, None, ["#PL"], [key])
+        send(partner(t), T.BL[:, o:o + 32], T.BS[:, o:o + 32], ("h%d" if p else "b0_%d") % t, [key])
 
     def send_b(t, ch):
         o = L * t + LO[ch]
@@ -562,8 +608,8 @@ def calls(g, core, rank, T, topo):
     def take_t(t, ch):
         lo, o = LO[ch], 256 * ch
         ts(T.TU[:, lo:lo + 64], T.PL[:, 0:64], 2048.0, None, A.add, None, ["#PL"], ["TU%d" % ch])
-        ts(T.TB[:, o + 64:o + 128], T.BL[:, L * t + lo:L * t + lo + 64], k2, 14336.0, A.add, A.add, ["BL%d_%d" % (t, ch), "K2"], ["TBb%d" % ch])
-        lin(ON["TB"][ch], T.TB[:, o:o + 64], T.PL[:, 0:64], 1.0, k2, ["#PL", "K2"], ["TBa%d" % ch])
+        ts(T.TB[:, o + 64:o + 128], T.BL[:, L * t + lo:L * t + lo + 64], -2048.0, None, A.add, None, ["BL%d_%d" % (t, ch), "BH%d" % t], ["TBb%d" % ch])
+        cp(T.TB[:, o:o + 64], T.PL[:, 0:64], ["#PL"], ["TBa%d" % ch])
         if t == ST - 1:
             lin(ON["TB"][ch], T.YS[:, lo:lo + 64], T.PL[:, 0:64], 1.0, 2048.0, ["#PL"], ["YS%d" % ch])
             send(asker(t), T.YL[:, lo:lo + 64], T.YS[:, lo:lo + 64], "yt%d" % ch, ["YS%d" % ch])
@@ -579,9 +625,12 @@ def calls(g, core, rank, T, topo):
     def before(ch):
         o = 256 * ch
         z, zk = T[ZB[ch]], "#" + ZB[ch]
-        mm(z[:, 0:256], T.NI[:], T.TB[:, o:o + 256], True, False, ["NI"] + ["TB%s%d" % (x, ch) for x in "abcd"], zk)
-        mm(z[:, 128:192], T.NI[:], T.TB[:, o:o + 64], False, False, ["NI", "TBa%d" % ch], zk)
-        mm(z[:, 64:128], T.BD8[:], T.RD[:, 128 * ch + 64:128 * ch + 128], False, False, ["BD8", "RD%d" % ch], zk)
+        mm(z[:, 0:256], T.NEG[0:1, 0:128], T.NEG[0:1, 128:384], True, False, ["NEG"] + KEYS, zk)
+        mm(z[:, 0:256], T.ONE[0:1, 0:128], T.NEG[0:1, 384:640], False, False, ["ONE"] + KEYS, zk)
+        mm(z[:, 0:128], T.Ih[:, 128:256], T.TB[:, o:o + 128], False, False, ["NIh", "TBa%d" % ch, "TBb%d" % ch], zk)
+        mm(z[:, 128:192], T.Ih[:, 128:256], T.TB[:, o:o + 64], False, False, ["NIh", "TBa%d" % ch], zk)
+        d = SETS[SET_OF[ch]][2] + 16 * SETS[SET_OF[ch]][1] + LO[ch]
+        mm(z[:, 64:128], T.BD8[:], T.RD[:, d:d + 64], False, False, ["BD8", "RD%d" % SET_OF[ch]], zk)
 
     def signs(ch):
         if ON["UN"][ch] == "S":
@@ -593,17 +642,18 @@ def calls(g, core, rank, T, topo):
 
     def verdict(ch):
         ts(T.X[:], T[ZB[ch]][:, 0:256], 0.0, -2048.0, A.max, A.add, ["#" + ZB[ch]], ["X"])
-        mm(T.PU[:, 0:64], T.Ih[:], T.TRI[:], True, False, ["Ih", "TRI"], "#PU")
+        mm(T.PU[:, 0:64], T.Ih[:, 0:128], T.TRI[:], True, False, ["Ih", "TRI"], "#PU")
         mm(T.PU[:, 0:64], T.BDh[:], T.X[:, 64:128], False, False, ["BDh", "X"], "#PU")
         mm(T.PU[:, 0:64], T.BDq[:], T.X[:, 192:256], False, True, ["BDq", "X"], "#PU")
-        mm(T.PU[:, 64:128], T.BDh[:], T.X[:, 128:192], True, True, ["BDh", "X"], "#PU")
+        mm(T.PU[:, 64:128], lanes_first(T.MT1, ch), T.I8[rows(ch), rows(ch)], True, False, ["MT1%d" % SET_OF[ch], "I8"], "#PU")
+        mm(T.PU[:, 64:128], T.BDh[:], T.X[:, 128:192], False, True, ["BDh", "X"], "#PU")
         for r in range(16):
             mm(T.PS[:, 0:8], T.WS[:, 15 - r:143 - r], T.X[:, r:128:16], r == 0, r == 15, ["WS", "X"], "#PS")
 
     def answer(t, ch):
         lo = LO[ch]
         o, c = 12 * t + lo // 16, (lo // 16 - 4) % 12
-        lin(ON["TH"][ch], T.TH[:, lo:lo + 64], T.PU[:, 64:128], -1.0, -30720.0, ["#PU"], ["TH%d" % ch])
+        lin(ON["TH"][ch], T.TH[:, lo:lo + 64], T.PU[:, 64:128], -1.0, -38912.0, ["#PU"], ["TH%d" % ch])
         lin(ON["TH"][ch], T.RB[:, lo:lo + 64], T.PU[:, 0:64], -1.0, -36864.0, ["#PU"], ["RB%d" % ch])
         ts(T.OB[:, c:c + 4], T.PS[:, 4:8], -1.0, -28672.0, A.mult, A.add, ["#PS"], ["OB%d" % ch])
         ts(T.RPs[:, o:o + 4], T.PS[:, 0:4], -1.0, -28672.0, A.mult, A.add, ["#PS"], ["RPs%d_%d" % (t, ch)])
@@ -620,9 +670,8 @@ def calls(g, core, rank, T, topo):
         def k(name):
             return [name + str(ch) for ch in chs]
         return [
-            lambda: tt(T.DD[:, ln], T.TAB[:].indirect(T.OB[:, cs]), T.TH[:, ln], A.subtract, TABK + ["TABx"] + k("OB") + k("TH"), ["DD" + s]),
+            lambda: tt(T.DD[:, ln], T.TAB[:].indirect(T.OB[:, cs]), T.NM[:, ln], A.min, TABK + ["TABx"] + k("OB") + k("NM"), k("EE")),
             lambda: tt(T.EQ[:, ln], T.BCF[:, cs].indirect(T.IOT[:, 0:C]), T.RB[:, ln], A.is_equal, ["IOT"] + k("BCF") + k("RB"), ["EQ" + s]),
-            lambda: tt(T.EE[:, ln], T.DD[:, ln], T.NM[:, ln], A.mult, ["DD" + s] + k("NM"), k("EE")),
             lambda: scan(T.SC[:, ln], T.D0[:, 0:16 * C], T.EQ[:, ln], ["D0", "EQ" + s], ["SC" + s]),
             lambda: tt(T.T2[:, cs], T.BCS[:, cs], T.SC[:, lo + 15:lo + 16 * C:16], A.subtract, k("BCS") + ["SC" + s], ["T2" + s]),
             lambda: ts(T.OF[:, lo // 8:lo // 8 + 2 * C:2], T.T2[:, cs], 8192.0, dum, A.mult, A.min, ["T2" + s, "dum"], k("OF")),
@@ -630,77 +679,74 @@ def calls(g, core, rank, T, topo):
 
     def scatter(c):
         ch, ln = 2 - c // 4, slice(16 * c, 16 * c + 16)
-        return lambda: tt(T.TAB[:].indirect(T.OF[:, 2 * c:2 * c + 1]), T.TH[:, ln], T.EE[:, ln], A.add,
+        return lambda: tt(T.TAB[:].indirect(T.OF[:, 2 * c:2 * c + 1]), T.TH[:, ln], T.DD[:, ln], A.max,
                           ["OF%d" % ch, "EE%d" % ch, "TH%d" % ch], TABK + ["TABx"])
 
-    def update_ops(ch, t):
-        w, o = W[ch], 12 * t + LO[ch] // 16
-        rp, rk = T.RPl[:, o:o + 4], ["RPl%d_%d" % (t, ch)]
+    def update(s, t):
+        chs, C, lo = SETS[s]
+        w, o, n = W[s], 12 * t + lo // 16, 36 * C
+        rp, rk, ls = T.RPl[:, o:o + C], ["RPl%d_%d" % (t, ch) for ch in chs], slice(0, 18) if C == 8 else slice(18, 27)
+        for ch in chs:
+            arrive("r%d_%d" % (ch, t), ["RPl%d_%d" % (t, ch)])
+        ts(T.U3[:, 0:C], rp, float(NA), 3.0, A.is_lt, A.mult, rk, ["U3"])
+        ts(T.TI[:, 0:C], rp, NV - 1, None, A.bitwise_and, None, rk, ["TI0"])
+        ts(T.TI[:, C:2 * C], rp, 15, None, A.bitwise_and, None, rk, ["TI1"])
+        tt(T.CC[:, 0:C], w[:, 5 * C:6 * C], T.U3[:, 0:C], A.add, [wk(s)[5], "U3"], ["CC"])
+        cp(w[:, 6 * C:8 * C], T.TI[:, 0:2 * C], ["TI0", "TI1"], ["Wt%d" % s])
+        tt(T.FF[:, 0:n], T.CC[:].indirect(T.LF[:, ls]), T.CD[:, 0:n], A.is_equal, ["CC", "LF", "CD"], ["FF"])
+        tt(T.PP[:, 0:n], w[:, 0:12 * C].indirect(T.LC[:, ls]), T.FF[:, 0:n], A.mult, wall(s) + ["LC", "FF"], ["PP"])
+        scan(T.SO[:, 0:n], T.RS[:, 0:n], T.PP[:, 0:n], ["RS", "PP"], ["SO"])
+        lin(ON["W"][s], w[:, 0:6 * C], T.SO[:, 5:n:6], 1.0, 0.0, ["SO"], wk(s))
+        lin(ON["W"][s], w[:, 11 * C:12 * C], T.SO[:, 5:6 * C:6], 1.0, 1.0, ["SO"], ["Wv%d" % s])
 
-        def first():
-            arrive("r%d_%d" % (ch, t), rk)
-            ts(T.U3[:, 0:4], rp, float(NA), 3.0, A.is_lt, A.mult, rk, ["U3"])
+    def final(s):
+        chs, C, lo = SETS[s]
+        w, o, n, k = W[s], 3 * lo, 48 * C, int(C == 4)
+        ts(T.MD[:, 0:3 * C], w[:, 0:3 * C], float(NV), -float(NV), A.is_ge, A.mult, wk(s)[0:3], ["MD"])
+        tt(w[:, 0:3 * C], w[:, 0:3 * C], T.MD[:, 0:3 * C], A.add, wk(s)[0:3] + ["MD"], wk(s)[0:3])
+        tt(T.RO[:, o:o + n], w[:, 0:12 * C].indirect(T.LO[:, 24 * k:24 * k + 3 * C]), T.BG[:, 384 * k:384 * k + n], A.mult, wall(s) + ["LO%d" % k, "BG"], ["RO%d" % s])
+        for c in range(C):
+            mm(T.PL[0:48, 16 * c:16 * c + 16], T.RO[:, o + c:o + n:C], T.DGh[:], True, True, ["RO%d" % s, "DGh"], "#PL")
+        act(T.OUT[0:48, lo:lo + 16 * C], T.PL[0:48, 0:16 * C], F.Copy, ["#PL"], ["OUT%d" % s])
 
-        def back():
-            lin(ON["W"][ch], w[:, 0:24], T.SO[:, 5:144:6], 1.0, 0.0, ["SO"], wk(ch))
-            lin(ON["W"][ch], w[:, 44:48], T.SO[:, 5:24:6], 1.0, 1.0, ["SO"], ["Wv%d" % ch])
-        return [
-            first,
-            lambda: ts(T.TI[:, 0:4], rp, NV - 1, None, A.bitwise_and, None, rk, ["TI0"]),
-            lambda: ts(T.TI[:, 4:8], rp, 15, None, A.bitwise_and, None, rk, ["TI1"]),
-            lambda: tt(T.CC[:, 0:4], w[:, 20:24], T.U3[:, 0:4], A.add, [wk(ch)[5], "U3"], ["CC"]),
-            lambda: cp(w[:, 24:32], T.TI[:], ["TI0", "TI1"], ["Wt%d" % ch]),
-            lambda: tt(T.FF[:], T.CC[:].indirect(T.LF[:, 0:9]), T.CD[:], A.is_equal, ["CC", "LF", "CD"], ["FF"]),
-            lambda: tt(T.PP[:], w[:].indirect(T.LC[:, 0:9]), T.FF[:], A.mult, wall(ch) + ["LC", "FF"], ["PP"]),
-            lambda: scan(T.SO[:], T.RS[:], T.PP[:], ["RS", "PP"], ["SO"]),
-            back,
-        ]
-
-    def final_ops(ch):
-        w, o, lo = W[ch], L * ch, LO[ch]
-
-        def turn():
-            tt(T.RO[:, o:o + L], w[:].indirect(T.LO[:, 0:12]), T.BG[:], A.mult, wall(ch) + ["LO", "BG"], ["RO%d" % ch])
-            for c in range(4):
-                mm(T.PL[0:48, 16 * c:16 * c + 16], T.RO[:, o + c:o + L:4], T.DGh[:], True, True, ["RO%d" % ch, "DGh"], "#PL")
-            act(T.OUT[0:48, lo:lo + 64], T.PL[0:48, 0:64], F.Copy, ["#PL"], ["OUT%d" % ch])
-        return [
-            lambda: ts(T.MD[:], w[:, 0:12], float(NV), -float(NV), A.is_ge, A.mult, wk(ch)[0:3], ["MD"]),
-            lambda: tt(w[:, 0:12], w[:, 0:12], T.MD[:], A.add, wk(ch)[0:3] + ["MD"], wk(ch)[0:3]),
-            turn]
-
-    convert(0)
-    for ch in range(3):
-        start_state(ch)
-    convert(1)
-    run(ask_ops(0, 0, "V"))
-    convert(2)
+    for j in range(4):
+        convert(j)
+    last = len(SETS) - 1
+    for s in range(last + 1):
+        start_state(s)
+        ask(s, 0, "V")
     turn_cases()
-    run(ask_ops(1, 0, "V"))
     send_cases(0)
-    convert(3)
-    run(ask_ops(2, 0, "V"))
     update_lists()
 
     later_constants()
     update_lists_2()
     for t in range(ST):
         more = t + 1 < ST
-        run(serve_ops(0, t, ON["serve"][0]))
-        run(serve_ops(1, t, ON["serve"][1]))
         if t:
-            run(update_ops(2, t - 1) + ask_ops(2, t, ON["ask"][2]))
-        run(serve_ops(2, t, ON["serve"][2]))
-        if more:
-            send_cases(t + 1)
-        for n, name in enumerate(PIECES.split()):
+            update(last, t - 1)
+            ask(last, t, ON["ask"][last])
+        for s in range(last + 1):
+            serve(s, t, ON["serve"][s])
+        n = 0
+        for name in PIECES.split():
             level, ch, p = (int(x) for x in name)
-            gather(t, n, level, ch, p)
-            widen(t, n, level, ch, p)
-            mask(t, n, level, ch, p)
-            if p == 1 and level == 1:
+            if t == 0 and name == "200":
+                wide_cases(0, n)
+            if name in FUSED:
+                compare(t, ch, p)
+            else:
+                gather(t, n, level, ch, p)
+                widen(t, n, level, ch, p)
+                mask(t, n, level, ch, p)
+                n += 1
+            if level == 1 and ch == 0:
+                send_half(t, p)
+            elif p == 1 and level == 1:
                 pick(1, ch)
                 send_b(t, ch)
+                if ch == 2 and more:
+                    send_cases(t + 1)
             elif p == 1 and level == 2:
                 pick(2, ch)
                 take_t(t, ch)
@@ -713,28 +759,36 @@ def calls(g, core, rank, T, topo):
                 signs(ch)
                 verdict(ch)
                 answer(t, ch)
+        if more:
+            wide_cases(t + 1, n)
         for chs in WRITES:
             run(write_ops(chs))
         run([scatter(c) for c in range(11, -1, -1)])
-        for ch in (0, 1):
-            run(update_ops(ch, t) + (ask_ops(ch, t + 1, ON["ask"][ch]) if more else final_ops(ch)))
+        for s in range(last):
+            update(s, t)
+            if more:
+                ask(s, t + 1, ON["ask"][s])
+            else:
+                final(s)
 
     for ch in range(3):
         arrive("yt%d" % ch, ["YL%d" % ch])
     dma("Y", "oyt", T.yt[:], T.YL[:], ["YL0", "YL1", "YL2"], [])
     ms(T.Y4[0:1, :], 32768.0, ["Y4"])
     mm(T.PC[:, 0:256], T.NO[0:1, :], T.Y4[0:1, :], True, False, ["NO", "Y4"], "#PC")
-    for m in range(10):
-        mm(T.PC[:, 0:256], T.NI[:], T.TAB[:, 256 * m:256 * m + 256], False, m == 9, ["NI"] + TABK, "#PC")
-    tt(T.Y1[:, 0:768], T.TAB[:, 2560:3328], T.TAB[:, 3328:4096], A.add, TABK, ["Y1"])
-    run(update_ops(2, ST - 1) + final_ops(2))
-    outs = ["OUT0", "OUT1", "OUT2"]
+    for m in range(9):
+        mm(T.PC[:, 0:256], T.NI[:], T.TAB[:, 256 * m:256 * m + 256], False, False, ["NI"] + TABK, "#PC")
+    tt(T.Y1[:, 0:768], T.TAB[:, 2560:3328], T.TAB[:, 3328:4096], A.add, TABK, ["Y1a"])
+    tt(T.Y2[:, 0:256], T.TAB[:, 2304:2560], T.Y1[:, 0:256], A.add, TABK + ["Y1a"], ["Y2a"])
+    tt(T.Y2[:, 256:512], T.Y1[:, 256:512], T.Y1[:, 512:768], A.add, ["Y1a"], ["Y2b"])
+    mm(T.PC[:, 0:256], T.NI[:], T.Y2[:, 0:256], False, True, ["NI", "Y2a"], "#PC")
+    update(last, ST - 1)
+    final(last)
+    outs = ["OUT%d" % s for s in range(last + 1)]
     dma("S", "o0", T.yvp[:], T.OUT[0:24, :], outs, [])
     dma("Y", "o1", T.yact[8:16, :], T.OUT[24:32, :], outs, [])
     dma("S", "o2", T.yact[0:8, :], T.OUT[32:40, :], outs, [])
     dma("Y", "o3", T.ydep[:], T.OUT[40:41, :], outs, [])
-    tt(T.Y2[:, 0:256], T.Y1[:, 0:256], T.Y1[:, 256:512], A.add, ["Y1"], ["Y2"])
-    tt(T.Y3[:], T.Y2[:, 0:256], T.Y1[:, 512:768], A.add, ["Y1", "Y2"], ["Y3"])
-    tt(T.YG[:], T.Y3[:], T.PC[:, 0:256], A.subtract, ["Y3", "#PC"], ["YG"])
+    tt(T.YG[:], T.Y2[:, 256:512], T.PC[:, 0:256], A.subtract, ["Y2b", "#PC"], ["YG"])
     dma("Y", "oyg", T.yg[:], T.YG[:], ["YG"], [])
     return ops

@@ -4,343 +4,422 @@ from concourse.mybir import AluOpType, ActivationFunctionType
 A, F = AluOpType, ActivationFunctionType
 
 L, ST, NA, NV = 192, 5, 4096, 512
-TW = NA + 32
-LO = (128, 64, 0)
-SET_OF = (0, 1, 2)
-SETS = (((0,), 4, 128), ((1,), 4, 64), ((2,), 4, 0))
+SP = 40
+CHS = (2, 1, 0)
 NE = 8
+WW = 160
+CUT = (0, 1280, 2560, 3584, 4096)
+AT = {"v": (0, 7), "a2": (28, 5), "a1": (48, 6), "d": (72, 6), "p1": (96, 6), "p2": (120, 6)}
+END = {"v": (5, 7), "w": (6, 7), "a2": (32, 5), "a1": (53, 6), "d": (77, 6), "p1": (101, 6), "p2": (125, 6),
+       "tf": (144, 1), "code": (148, 1), "one": (158, 0), "six": (159, 0)}
+CELLS = (2050, 2048, 2052, 2048, 2052, 2050, 1, 6)
+MOVES = (("v", 0, "tf"), ("v", 1, "w"), ("v", 2, "tf"), ("v", 3, "p1"), ("v", 4, "w"), ("v", 5, "p2"), ("v", 6, "one"),
+         ("a2", 2, "tf"), ("a1", 0, "tf"), ("p1", 0, "w"), ("p2", 2, "w"))
 
 f32, b16, h16, i32, u16 = "float32", "bfloat16", "float16", "int32", "uint16"
 
 
 def _s(n, dt):
-    return ("sbuf", [128, n], dt)
+    return ("sbuf", [128] + (n if isinstance(n, list) else [n]), dt)
 
 
 SCRATCH = {
-    "GI": _s(NA, i32), "TAB": _s(TW, f32), "FX": _s(NA, b16), "RF": _s(NV + 8, i32), "CS": _s(L, b16),
-    "CNs": _s(2 * L, b16), "CN": _s(ST * 2 * L, b16),
-    "NDi": _s(L, i32), "NDf": _s(L, f32), "SI": _s(L, i32), "SF": _s(L, f32), "SH": _s(L, h16),
-    "DI": _s(L, i32), "DF": _s(L, f32), "DH": _s(L, h16),
-    "WA": _s(96, f32), "WB": _s(96, f32), "WC": _s(96, f32), "LA": _s(16, u16), "I8": _s(128, b16), "AL": _s(ST * 24, f32),
-    "RPs": _s(ST * 12, i32), "RPl": _s(ST * 12, i32), "BS": _s(ST * L, u16), "BL": _s(ST * L, u16),
-    "YS": _s(L, f32), "YL": _s(L, f32),
-    "CX": _s(6 * 512, b16), "G": _s(4 * 512, f32), "M": _s(3 * 1024, h16), "CB": _s(3 * 1024, b16),
-    "R16": _s(L, u16), "TU": _s(L, u16), "VU": _s(16, u16), "RA": _s(L, b16), "RD": _s(2 * L, b16),
-    "XA": _s(128, f32), "MT1": _s(384, b16), "MT2": _s(384, b16), "NM": _s(L, f32),
-    "TB": _s(3 * 256, h16), "UN": _s(64, b16), "X": _s(256, h16),
-    "OB": _s(16, u16), "BCF": _s(16, f32), "BCS": _s(16, f32), "RB": _s(L, f32), "TH": _s(L, f32),
-    "DD": _s(L, f32), "EQ": _s(L, f32), "SC": _s(L, f32), "T2": _s(16, f32), "OF": _s(24, u16),
-    "U3": _s(8, f32), "CC": _s(8, f32), "TI": _s(16, i32), "FF": _s(288, f32), "PP": _s(288, f32), "SO": _s(288, f32),
-    "MD": _s(24, f32), "RO": _s(576, h16), "OUT": _s(L, f32), "Y1": _s(1024, f32), "Y2": _s(512, f32), "Y3": _s(256, f32),
-    "Y4": _s(256, f32), "NO": _s(128, f32), "YG": _s(256, f32),
-    "PI": _s(4, i32), "PJ": _s(8, i32), "PF": _s(8, f32), "K2": _s(8, f32), "XI": _s(L, f32), "SR": _s(432, f32),
-    "GB": _s(128, f32), "DM": _s(128, f32), "IOT": _s(16, u16), "ONE": _s(1024, b16), "EXP": _s(1024, b16),
-    "WS": _s(144, h16), "W2": _s(144, b16), "W2h": _s(144, h16), "WQ": _s(5 * 144, h16), "ONh": _s(5 * 144, h16),
-    "BD": _s(128, b16), "BDh": _s(128, h16), "BDq": _s(128, h16), "BD8": _s(128, b16), "BD1": _s(128, b16),
-    "TA": _s(128, f32), "TC": _s(128, f32), "TD": _s(128, f32), "T1": _s(128, b16), "T3": _s(128, b16), "NI": _s(128, f32),
-    "Ih": _s(256, h16), "Ib": _s(128, b16), "NEG": _s(640, b16), "TRI": _s(64, h16), "DG": _s(432, f32), "DGh": _s(16, h16),
-    "D0": _s(L, f32), "NS": _s(640, b16), "MON": _s(640, b16), "RT": _s(432, f32), "RU": _s(432, f32), "RV": _s(432, f32),
-    "RZ": _s(432, f32), "LC": _s(32, u16), "LF": _s(32, u16), "JT": _s(18, f32), "JU": _s(18, f32), "JI": _s(18, i32), "JK": _s(32, i32),
-    "CD": _s(288, f32), "RS": _s(288, f32), "LI": _s(36, f32), "LO": _s(36, u16), "BI": _s(576, f32), "BG": _s(576, f32),
+    "GI": _s(NA, i32), "TAB": _s(SP + NA, f32), "FX": _s(NA, b16), "RF": _s(NV + 8, i32),
+    "CNs": _s(320, b16), "CN": _s(ST * 320, b16), "CX": _s([3 * ST, 512], b16), "NDi": _s(16, i32),
+    "SI": _s(L, i32), "SH": _s(L, h16), "DI": _s(L, i32), "DH": _s(L, h16),
+    "W": _s([3 * (ST + 1), WW], i32), "BS": _s(ST * 240, u16), "BL": _s(ST * 240, u16),
+    "RP": _s(ST * 24, i32), "YS": _s(L, f32), "YL": _s(L, f32),
+    "R16": _s(L, u16), "TU": _s(L, u16), "G1": _s(3072, h16), "G2": _s(3072, h16), "CB": _s(3072, b16),
+    "MK1": _s(L, b16), "MK2": _s(L, b16), "MX1": _s(1536, b16), "MX2": _s(1536, b16), "XA": _s(384, h16), "XB": _s(384, h16),
+    "BB": _s(216, h16), "SG": _s(384, b16), "ST": _s(384, i32), "SB": _s([3, 144], h16),
+    "D1": _s(L, h16), "OB": _s(12, u16), "EE": _s(L, f32), "SC": _s(L, f32), "OF": _s(24, u16), "DD": _s(L, f32), "TH": _s(L, f32),
+    "FF": _s(432, f32), "PP": _s(432, f32), "FM": _s(96, i32), "RO": _s(576, h16), "OUT": _s(L, f32), "YH": _s(NA, h16), "YG": _s(256, f32),
+    "PI": _s(4, i32), "PJ": _s(8, i32), "PF": _s(8, f32), "PG": _s(8, f32), "SR": _s(512, f32), "DM": _s(128, f32), "XI": _s(240, f32),
+    "ONE": _s(720, b16), "Ib": _s(128, b16), "I32": _s(128, b16), "MKT": _s(512, b16), "DG": _s(416, f32), "DGh": _s(16, h16),
+    "LXi": _s(4, f32), "LX": _s(4, u16), "LN": _s(8, u16), "S2": _s(128, b16), "RM": _s(260, b16), "RA": _s(64, f32), "RB": _s(64, f32),
+    "RC": _s(64, f32), "RE": _s(64, f32), "CE": _s(64, f32), "CR": _s(260, b16), "CS": _s(4, h16), "RS1": _s(128, f32), "RS2": _s(132, f32), "TRI": _s(L, b16),
+    "GB": _s(128, f32), "BD": _s(128, b16), "NI": _s(128, b16), "SEL": _s(2048, b16), "SED": _s(2048, b16), "EW": _s(960, b16), "M2": _s(8, b16), "WQ": _s(720, b16), "W2": _s(144, b16),
+    "WY": _s(960, b16), "RT": _s(416, f32), "RU": _s(416, f32), "RV": _s(416, f32), "RZ": _s(416, f32), "LS": _s(26, u16),
+    "CD": _s(144, f32), "RS": _s(144, f32), "LI": _s(12, f32), "LO": _s(12, u16), "BI": _s(L, f32), "BG": _s(L, f32),
 }
-for _n in ("PM0", "PM1", "PL", "PC", "PZ", "PS", "PU", "PX"):
+BANKS = ("PA0", "PA1", "PB0", "PB1", "PC", "PZ0", "PZ1", "PD")
+for _n in BANKS:
     SCRATCH[_n] = ("psum", [128, 512], f32)
+IO = {"refs": [128, NV], "gloss": [128, NA], "facts": [128, NA], "cases": [128, L], "need": [ST, L], "vp0": [24, L],
+      "act0": [16, L], "dep0": [1, L], "yt": [128, L], "yg": [128, 256], "yvp": [24, L], "yact": [16, L], "ydep": [1, L]}
 
-_LOCAL = ["g0", "g1", "g2", "g3", "fx", "rf", "rw", "cs", "nd", "s0", "s1", "s2", "dp", "oyt", "oyg", "o0", "o1", "o2", "o3", "ex"]
-SEMAPHORES = (["eV", "eS", "eT", "eP", "ls"] + _LOCAL + ["yt0", "yt1", "yt2"] + ["%s%d" % (n, t) for t in range(ST) for n in ("cn", "h")]
-              + ["%s%d_%d" % (n, ch, t) for t in range(ST) for ch in range(3) for n in "albr"])
-
-
-class Shape(np.ndarray):
-    def indirect(self, off):
-        return np.zeros((128, 16 * off.shape[1]), np.complex64)
+SEMAPHORES = (["eV", "eS", "eT", "eP", "ls", "g0", "g1", "g2", "g3", "fx", "rf", "rw", "cs", "nd", "s0", "s1", "s2", "dp",
+               "oyt", "oyg", "o0", "o1", "o2", "yt0", "yt1", "yt2"]
+              + ["%s%d" % (n, t) for t in range(ST) for n in ("cn",)]
+              + ["%s%d_%d" % (n, ch, t) for t in range(ST) for ch in range(3) for n in "abhr"])
 
 
-def shadow(T):
-    io = {"refs": (128, NV), "gloss": (128, NA), "facts": (128, NA), "cases": (128, L), "need": (ST, L), "vp0": (24, L),
-          "act0": (16, L), "dep0": (1, L), "yt": (128, L), "yg": (128, 256), "yvp": (24, L), "yact": (16, L), "ydep": (1, L)}
-    wide = {f32: np.float32, i32: np.float32}
-    fields = {k: np.zeros(v, np.float16 if k in ("facts", "cases") else np.float32).view(Shape) for k, v in io.items()}
-    fields.update({k: np.zeros(v[1], wide.get(v[2], np.float16)).view(Shape) for k, v in SCRATCH.items()})
-    fields["cores"] = list(T.cores)
-    rec = np.zeros(1, [(k, "O") for k in fields]).view(np.recarray)
-    for k, v in fields.items():
-        rec[k][0] = v
-    return rec[0]
+def at(name, c0=None, c1=None, step=None, p=(0, 128)):
+    return (name, (slice(p[0], p[1]), slice(c0, c1, step)))
 
 
-CYC, GATHER, SCATTER, FIX, WAKE, FAR, NEAR, PEC = 0.85, 1.56, 3.8, 50.0, 100.0, 2300.0, 1900.0, 0.43
+def at3(name, k, c0=None, c1=None, step=None):
+    return (name, (slice(0, 128), k, slice(c0, c1, step)))
 
 
-ISSUE = 400.0
+def by(win, off):
+    return win + (off,)
 
 
-def cost(eng, kind, aps, rd):
-    n = int(np.prod(aps[0].shape[1:]))
-    if kind == "d":
-        return 60.0, NEAR
-    if kind == "r":
-        return ISSUE, FAR + aps[0].nbytes / 40.0
-    if eng == "P":
-        return 150.0 + 2 * n * CYC, 0.0
-    if eng == "T":
-        return max(min(64, aps[1].shape[1]), aps[2].shape[1]) * PEC * (4 if aps[1].itemsize == 4 else 1), 60.0
-    if aps[0].dtype == np.complex64:
-        return FIX + n * SCATTER * CYC, 0.0
-    if len(aps) > 1 and aps[1].dtype == np.complex64:
-        return FIX + 25.0 + n * GATHER * CYC, 0.0
-    per = 0.5 if eng == "V" and all(a.itemsize == 2 for a in aps) else 1.0
-    if len(aps) == 3 and not any(k[0] == "#" for k in rd):
-        per = 2.0
-    return FIX + (25.0 if eng == "S" else 10.0) + max(16, n * per) * CYC, 0.0
+CYC, GATHER, SCATTER, FIX, WAKE, FAR, NEAR, PEC, ISSUE = 0.85, 1.56, 3.8, 50.0, 140.0, 2500.0, 1900.0, 0.43, 400.0
+PEFIX = 4.0
+SIZE = {f32: 4, i32: 4, b16: 2, h16: 2, u16: 2}
+
+
+def cells(ap):
+    shape = SCRATCH[ap[0]][1]
+    return np.arange(int(np.prod(shape[1:]))).reshape(shape[1:])[ap[1][1:]].ravel()
+
+
+def count(ap):
+    return 16 * len(cells(ap[2])) if len(ap) == 3 else len(cells(ap))
+
+
+def foot(ap, memo={}):
+    key = (ap[0], str(ap[1]))
+    if key not in memo:
+        bits = np.zeros(int(np.prod(SCRATCH[ap[0]][1][1:])), bool)
+        bits[cells(ap)] = True
+        memo[key] = (ap[0], ap[1][0].start, ap[1][0].stop, int.from_bytes(np.packbits(bits, bitorder="little").tobytes(), "little"))
+    return memo[key]
+
+
+def sides(op):
+    kind, args = op[1], op[2]
+    if kind == "mm":
+        rd, wr = [x for m in args for x in m[1:3]], [m[0] for m in args]
+    elif kind == "send":
+        rd, wr = [args[2]], []
+    else:
+        rd, wr = [x for x in args[1:] if isinstance(x, tuple)], [args[0]]
+    rd = rd + [x[2] for x in rd + wr if len(x) == 3]
+    return [list({foot(x) for x in s if x[0] in SCRATCH}) for s in (rd, wr)]
 
 
 def depends(ops):
-    writer, readers, last, out = {}, {}, {}, []
-    for i, (eng, fn, rd, wr, ev) in enumerate(ops):
-        deps = set()
-        for k in list(rd) + list(wr):
-            if k in writer:
-                deps.add(writer[k])
-            if k[0] == "#":
-                if k in last and ops[last[k]][0] != eng:
-                    deps.add(last[k])
-                last[k] = i
-        for k in wr:
-            deps.update(readers.get(k, ()))
-        for k in rd:
-            readers.setdefault(k, []).append(i)
-        for k in wr:
-            writer[k] = i
-            readers[k] = []
-        out.append(deps - {i})
+    log, out = {}, []
+    for i, op in enumerate(ops):
+        rd, wr = sides(op)
+        raw, other = set(), set()
+        for mine, writes in ((rd, False), (wr, True)):
+            for name, p0, p1, bits in mine:
+                for j, q0, q1, theirs, wrote in log.get(name, ()):
+                    if (wrote or writes) and q0 < p1 and p0 < q1 and bits & theirs:
+                        (other if writes and wrote else raw).add(j)
+        for name, p0, p1, bits in wr:
+            log[name] = [e for e in log.get(name, ()) if not (p0 <= e[1] and e[2] <= p1 and e[3] & ~bits == 0)]
+        for mine, writes in ((rd, False), (wr, True)):
+            for name, p0, p1, bits in mine:
+                log.setdefault(name, []).append((i, p0, p1, bits, writes))
+        out.append({j: j in raw or ops[j][0] != op[0] or op[0] != IN_ORDER or "dma" in (op[1], ops[j][1]) for j in (raw | other) - {i}})
     return out
 
 
-def arrange(ops):
-    single, groups, head = depends(ops), [], {}
+IN_ORDER = "T"
+
+
+def banks(op):
+    rd, wr = sides(op)
+    return {x[0] for x in rd + wr if x[0] in BANKS}
+
+
+def cost(op):
+    eng, kind, args = op[:3]
+    if kind == "arr":
+        return 100.0 + count(args[0]) * SIZE[SCRATCH[args[0][0]][2]] * 128 / 40.0, FAR - 100.0
+    if kind == "dma":
+        sb = args[0] if args[0][0] in SCRATCH else args[1]
+        return 60.0, NEAR + count(sb) * SIZE[SCRATCH[sb[0]][2]] * 128 / 200.0
+    if kind == "send":
+        return ISSUE, -WAKE
+    if kind == "mm":
+        return sum(max(min(64, count(m[1])), count(m[2])) * PEC + PEFIX for m in args), 60.0
+    n = count(args[0])
+    if eng == "P":
+        return 150.0 + 2 * n * CYC, 0.0
+    if len(args[0]) == 3:
+        return FIX + n * SCATTER * CYC, 0.0
+    fix = FIX + (20.0 if eng == "S" else 5.0)
+    if kind != "ms" and len(args[1]) == 3:
+        return fix + n * GATHER * CYC, 0.0
+    full = [x for x in args if isinstance(x, tuple) and count(x) == n]
+    per = 0.5 if eng == "V" and all(SIZE[SCRATCH[x[0]][2]] == 2 for x in full) else 1.0
+    if kind == "tt" and not any(x[0] in BANKS for x in full[1:]):
+        per = 2.0
+    return fix + max(16, n * per) * CYC, 0.0
+
+
+def network(ops):
+    n, deps, dur = len(ops), depends(ops), [cost(o) for o in ops]
+    sender = {o[2][3]: i for i, o in enumerate(ops) if o[1] == "send"}
+    loaded, before = 1200.0, {}
+    first = [0.0] * n
     for i, o in enumerate(ops):
-        if not (i and o[0] == ops[i - 1][0] == "T" and o[3] == ops[i - 1][3]):
-            groups.append([])
-        groups[-1].append(i)
-        head[i] = len(groups) - 1
-    deps = [{head[j] for i in gr for j in single[i]} - {k} for k, gr in enumerate(groups)]
-    each = [cost(o[0], o[1][0], o[1][2], o[2]) if o[0] else (0.0, 0.0) for o in ops]
-    dur = [(sum(each[i][0] for i in gr), each[gr[0]][1]) for gr in groups]
-    ops = [ops[gr[0]] for gr in groups]
-    n = len(ops)
-    sender = {o[1][3]: i for i, o in enumerate(ops) if o[0] and o[1][0] == "r"}
-    loaded, before_load, issue = 1200.0, {}, []
-    for i, o in enumerate(ops):
-        if o[0] is None:
-            deps[i].add(sender[o[4][0]])
-        elif o[1][0] == "d" and not o[2]:
-            if o[0] in before_load:
-                issue.append((before_load[o[0]], i))
-            before_load[o[0]] = i
-            loaded += o[1][2][0].nbytes / 250.0 if o[0] == "Y" else 0.0
+        if o[1] == "arr":
+            deps[i][sender[o[2][1]]] = True
+        elif o[1] == "dma" and o[2][1][0] in IO:
+            first[i] = 1e6 - i
+            loaded += dur[i][1] - NEAR if o[0] == "Y" else 0.0
             dur[i] = (60.0, NEAR + (loaded if o[0] == "Y" else 600.0))
-    users = [[] for o in ops]
+    eng, bank, busy = [o[0] or "link" for o in ops], [banks(o) for o in ops], [d[0] for d in dur]
+    back, ahead = [[] for o in ops], [[] for o in ops]
     for i in range(n):
-        for j in deps[i]:
-            users[j].append(i)
-    left = [len(d) for d in deps]
-    topo_order, stack = [], [i for i in range(n) if not left[i]]
-    while stack:
-        i = stack.pop()
-        topo_order.append(i)
-        for u in users[i]:
-            left[u] -= 1
-            if not left[u]:
-                stack.append(u)
-    ahead = [0.0] * n
-    for i in reversed(topo_order):
-        ahead[i] = sum(dur[i]) + max([ahead[u] + (0.0 if ops[u][0] == ops[i][0] == "T" else WAKE) for u in users[i]], default=0.0)
-    for a, b in reversed(issue):
-        ahead[a] = max(ahead[a], ahead[b] + 2 * JITTER + 1.0)
-    best_plan = min(fill(ops, deps, users, dur, ahead, seed) for seed in SEEDS)
-    return [i for k in best_plan[1] for i in groups[k]]
+        for j in set(deps[i]) | ({before[eng[i]]} if first[i] and eng[i] in before else set()):
+            lag = 0.0 if (not deps[i].get(j) or eng[j] == eng[i] == "T") else dur[j][1] + (WAKE if eng[i] else 0.0)
+            back[i].append((j, lag))
+            ahead[j].append((i, lag))
+        if first[i]:
+            before[eng[i]] = i
+    for t in range(1, ST):
+        back[sender["cn%d" % t]].append((sender["b0_%d" % (t - 1)], 0.0))
+        ahead[sender["b0_%d" % (t - 1)]].append((sender["cn%d" % t], 0.0))
+    return ops, deps, dur, eng, bank, busy, back, ahead
 
 
-def fill(ops, deps, users, dur, ahead, seed):
+def arrange(ops, net=None):
+    ops, deps, dur, eng, bank, busy, back, ahead = net or network(ops)
     n = len(ops)
-    ahead = [a + (seed.get(o[0], 0.0) if d[0] < seed["short"] else 0.0) for a, o, d in zip(ahead, ops, dur)]
-    ahead = [a + sum(v for k, v in seed["first"].items() if o[3] and o[3][0].startswith(k)) for a, o in zip(ahead, ops)]
-    left = [len(d) for d in deps]
-    ready, done, free, order = {}, [0.0] * n, {}, []
-    pool = {e: [] for e in ("V", "S", "T", "P", "Y", None)}
+    inside, rank = [0.0] * n, [None] * n
+    for i, o in enumerate(ops):
+        if len(o) > 3:
+            inside[i] = max([inside[j] + busy[j] + lag for j, lag in back[i] if ops[j][3:] == o[3:]], default=0.0)
+            rank[i] = o[3][0] * PERIOD + WHEN[o[3][1]][o[3][2]] + inside[i]
+        elif any(rank[j] is not None for j, lag in back[i]):
+            rank[i] = max(rank[j] + busy[j] + lag for j, lag in back[i] if rank[j] is not None)
+    for i in reversed(range(n)):
+        if rank[i] is None:
+            rank[i] = min([rank[u] - lag - (EARLY if len(ops[u]) > 3 else 0.0) for u, lag in ahead[i]], default=0.0) - busy[i]
+    left, start, ready, free, held, order = [len(b) for b in back], [0.0] * n, {}, {}, {}, []
+    pool = {e: [] for e in sorted(set(eng))}
 
     def release(i):
-        ready[i] = max([done[j] + (-60.0 if ops[j][0] == ops[i][0] == "T" else 0.0 if ops[i][0] is None else WAKE) for j in deps[i]], default=0.0)
-        pool[ops[i][0]].append(i)
+        ready[i] = max([0.0] + [start[j] + busy[j] + lag for j, lag in back[i]])
+        pool[eng[i]].append((ready[i] if eng[i] == "link" else rank[i], i))
+        pool[eng[i]].sort()
+        first.pop(eng[i], None)
+
+    def when(i):
+        t = ready[i]
+        for b in bank[i]:
+            if b in held and held[b][0] != eng[i] and held[b][1] > t:
+                t = held[b][1]
+        return t
+    first = {}
     for i in range(n):
         if not left[i]:
             release(i)
     while len(order) < n:
-        best = None
-        for e, cand in pool.items():
-            if not cand:
-                continue
-            at = max(free.get(e, 0.0), min(ready[i] for i in cand))
-            if best is None or at < best[0]:
-                best = (at, e)
-        at, e = best
-        i = max((j for j in pool[e] if ready[j] <= at + seed.get("wait" + str(e), 0.0)), key=lambda j: (ahead[j], -j))
-        pool[e].remove(i)
-        start = max(at, ready[i])
-        if e is not None:
-            free[e] = start + dur[i][0]
-        done[i] = start + sum(dur[i])
-        order.append(i)
-        for u in users[i]:
+        for e, c in pool.items():
+            if e not in first:
+                first[e] = min([when(i) for r, i in c], default=1e18)
+        now, e = min((max(free.get(e, 0.0), t), e) for e, t in first.items())
+        soon, strict, pick = 1e18, 1e18, None
+        for r, i in pool[e]:
+            if when(i) > now + 1.0:
+                soon = min(soon, when(i))
+                if len(ops[i]) > 3 and ops[i][3][1] in URGENT:
+                    strict = min(strict, when(i) + URGENT[ops[i][3][1]])
+            elif now + busy[i] * PATIENCE <= soon and now + busy[i] <= strict:
+                pick = i
+                break
+        if pick is None:
+            free[e] = soon
+            continue
+        pool[e].remove((r, pick))
+        order.append(pick)
+        start[pick], free[e] = now, now + busy[pick]
+        first.pop(e)
+        for b in bank[pick]:
+            held[b] = (e, now + sum(dur[pick]) + WAKE)
+            first.clear()
+        for u, lag in ahead[pick]:
             left[u] -= 1
             if not left[u]:
                 release(u)
-    return max(done), order
+    return order, deps, start, [s + sum(d) for s, d in zip(start, dur)]
 
 
-LEEWAY, JITTER = 0.0, 10000.0
-SEEDS = [{'short': 250.0, 'S': 500.0, 'V': 1000.0, 'T': 1000.0, 'waitS': 200.0, 'first': {
-    'TAB': 4000.0, 'TI': -1000.0, 'M0': -1000.0, 'SC': -2000.0, 'EE': 200.0, 'OB': 2000.0, 'RA': -2000.0, '#PS': -200.0, 'CC': 2000.0,
-    'BC': -1000.0, '#PC': 500.0, 'NM': -2000.0, 'CB': -200.0, 'UN': -200.0, 'U3': 500.0, '#PL': 200.0, 'FF': -2000.0, 'RPs': 4000.0,
-    'M1': 200.0, 'T2': -200.0, 'TH': -2000.0, 'M2': 2000.0, 'G': -2000.0, 'XA': -1000.0, 'W': 2000.0, 'VU': -1000.0, 'OF': -1000.0,
-    'BS': 4000.0, 'RD': 500.0, 'TB': -200.0, '#PX': -1000.0, '#PZ': -2000.0, '#PM': -2000.0, 'PP': 200.0, 'TU': -200.0, 'R16': 200.0,
-    'CX': 2000.0, 'MT': -200.0, 'EQ': 4000.0, 'RB': 200.0}}]
-PIECES = "100 101 110 111 120 121 200 201 210 211 300 301 220 221 310 311 320 321"
-FUSED = ["301", "311", "321"]
-CUT = (0, 1280, 2560, 3584, 4096)
-WRITES = ((0, 1), (2,))
-ZB = ("PZ", "PX", "PZ")
-ON = {"TB": "VVV", "UN": "SSS", "TH": "SSS", "BC": "SSS", "NM": "SSS", "ask": "SSV", "serve": "VVV", "W": "SSS"}
-ORDER = []
+PERIOD, EARLY, PATIENCE = 20000.0, 3000.0, 0.3
+URGENT = {}
+WHEN = {'one': [21000, 9300, 2450], 'acts': [14850, 2200, 11950], 'two': [14300, 13200, 3500], 'before': [10350, 9500, 36300], 'three': [17250, 9500, 13100], 'reply': [17700, 19600, -5050], 'writes': [-8600, 13150, 9750], 'scatter': [18800, 17350, 23000], 'update': [28900, 23050, 21950], 'ask': [17500, 16250, 16650], 'cases': [15150, 12550, 5450], 'yt': [43800, 14150, 14050], 'old': [-4350, 36500, -13850], 'keys': [-2500, 9450, -6250], 'found': [10700, 24900, 12200], 'count': [5000, -100, -1900], 'XA': [-3200, 14700, -5700], 'XB': [9800, -5250, -11650], 'mask': [22000, 25850, 25850]}
 
 
-def emit(g, T, ops):
+PLAN = []
+
+
+def waits_of(ops, order, deps):
+    place = {i: k for k, i in enumerate(order)}
+    known = {e: ({}, set()) for e in "VSTPY"}
+    clock, waits, need, held = {}, {}, set(), {}
+    for i in order:
+        eng = ops[i][0]
+        if eng is None:
+            clock[i] = ({}, set())
+            continue
+        mine, all_deps = [], {j for j, hard in deps[i].items() if hard}
+        for b in banks(ops[i]):
+            if b in held and ops[held[b]][0] != eng:
+                all_deps.add(held[b])
+            held[b] = i
+        kc, ks = known[eng]
+        for j in sorted(all_deps, key=lambda j: -place[j]):
+            ej = ops[j][0]
+            if ops[j][1] in ("dma", "arr"):
+                if j in ks:
+                    continue
+                ks.add(j)
+            else:
+                if ej == eng == "T" or kc.get(ej, -1) >= place[j]:
+                    continue
+                kc[ej] = place[j]
+                need.add(j)
+            mine.append(j)
+            for e, k in clock[j][0].items():
+                kc[e] = max(kc.get(e, -1), k)
+            ks.update(clock[j][1])
+        clock[i] = (dict(kc), set(ks))
+        waits[i] = mine
+    return waits, need
+
+
+def emit(g, core, T, topo, ops, order, waits, need):
     q = {"V": g.vector, "S": g.scalar, "T": g.tensor, "P": g, "Y": g.sync}
-    known = {e: ({}, set()) for e in q}
-    clock, waits, need = [], [], set()
-    every = depends(ops)
-    for i, (eng, fn, rd, wr, ev) in enumerate(ops):
-        deps = every[i]
-        mine = []
-        if eng is not None:
-            kc, ks = known[eng]
-            for j in sorted(deps - {i}, reverse=True):
-                ej, evj = ops[j][0], ops[j][4]
-                if evj is None:
-                    if (ej == eng == "T") or kc.get(ej, -1) >= j:
-                        continue
-                    kc[ej] = j
-                    need.add(j)
-                else:
-                    if j in ks:
-                        continue
-                    ks.add(j)
-                mine.append(j)
-                for e, n in clock[j][0].items():
-                    if kc.get(e, -1) < n:
-                        kc[e] = n
-                ks.update(clock[j][1])
-            clock.append((dict(kc), set(ks)))
-        else:
-            clock.append(({}, set()))
-        waits.append(mine)
-    count, num, sent, seen = {}, {}, 0, set()
-    for i in sorted(need):
-        count[ops[i][0]] = count.get(ops[i][0], 0) + 1
-        num[i] = count[ops[i][0]]
-    for i, (eng, fn, rd, wr, ev) in enumerate(ops):
+
+    def real(x):
+        if not isinstance(x, tuple):
+            return x
+        ap = T[x[0]][x[1]]
+        return ap.indirect(real(x[2])) if len(x) == 3 else ap
+    tick, num, seen, sent = {}, {}, set(), 0
+    for i in order:
+        if i in need:
+            tick[ops[i][0]] = num[i] = tick.get(ops[i][0], 0) + 1
+    for i in order:
+        eng, kind, args = ops[i][:3]
         if eng is None:
             continue
+        e = q[eng]
         for j in waits[i]:
-            if ops[j][4] is None:
-                q[eng].wait_ge(T.sem["e" + ops[j][0]], num[j])
-            else:
-                q[eng].wait_ge(T.sem[ops[j][4][0]], ops[j][4][1])
+            if ops[j][1] in ("dma", "arr"):
+                e.wait_ge(T.sem[ops[j][2][-1]], 16 if ops[j][1] == "dma" else NE)
                 seen.add(j)
-        ins = fn[1]()
-        if fn[0] == "d":
-            ins.then_inc(T.sem[ev[0]], 16)
-        elif fn[0] == "r":
-            sent += NE if ev[0] == "ls" else 0
-        elif i in need:
+            else:
+                e.wait_ge(T.sem["e" + ops[j][0]], num[j])
+        if kind == "send":
+            dst = T.cores[args[0]]
+            rid, pid = topo.addr(dst)[:2]
+            e.remote_dma(real(args[1]), real(args[2]), T.sem[args[3]], T.sem.ls, pid, rid, sum(1 << k for k in topo.engines(core, dst)[:NE]))
+            sent += NE
+            continue
+        if kind == "dma":
+            e.dma_start(real(args[0]), real(args[1])).then_inc(T.sem[args[2]], 16)
+            continue
+        a = [real(x) for x in args] if kind != "mm" else None
+        if kind == "mm":
+            for m in args:
+                ins = e.matmul(real(m[0]), real(m[1]), real(m[2]), m[3], m[4])
+        elif kind == "ts":
+            ins = e.tensor_scalar(*(a if a[5] is not None else a[:5]))
+        elif kind == "tt":
+            ins = e.tensor_tensor(*a)
+        elif kind == "cp":
+            ins = e.tensor_copy(*a)
+        elif kind == "ms":
+            ins = e.memset(*a)
+        elif kind == "scan":
+            ins = e.tensor_tensor_scan(*a)
+        elif kind == "act":
+            ins = e.activation(a[0], a[1], a[2], bias=a[3], scale=a[4])
+        elif kind == "iota":
+            ins = e.iota(*a) if SCRATCH[args[0][0]][2] == i32 else e.iota(*a, allow_small_or_imprecise_dtypes=True)
+        else:
+            ins = e.affine_select(*a)
+        if i in need:
             ins.then_inc(T.sem["e" + eng], 1)
-    for i, (eng, fn, rd, wr, ev) in enumerate(ops):
-        if ev is not None and ev[0] != "ls" and i not in seen:
-            g.wait_ge(T.sem[ev[0]], ev[1])
-    g.wait_ge(T.sem["ls"], sent)
+    for i in order:
+        if ops[i][1] in ("dma", "arr") and i not in seen:
+            g.wait_ge(T.sem[ops[i][2][-1]], 16 if ops[i][1] == "dma" else NE)
+    for eng, k in tick.items():
+        g.wait_ge(T.sem["e" + eng], k)
+    g.wait_ge(T.sem.ls, sent)
 
 
 def rank_program(g, core, T, topo):
     rank = T.rank_of(core)
     if rank is None:
         return
-    if not ORDER:
-        ORDER.extend(arrange(calls(g, core, rank, shadow(T), topo)))
-    ops = calls(g, core, rank, T, topo)
-    emit(g, T, [ops[i] for i in ORDER])
+    ops = calls(rank, len(T.cores))
+    if not PLAN:
+        order, deps = arrange(ops)[:2]
+        PLAN.extend((order,) + waits_of(ops, order, deps))
+    emit(g, core, T, topo, ops, *PLAN)
 
 
-def calls(g, core, rank, T, topo):
-    n_ranks = len(T.cores)
-    ops = []
-    V, S, PE = g.vector, g.scalar, g.tensor
+AHEAD = (2, 1, 0)
+WRITES = ((1, 3), (0, 1))
+HALVED = (0, 1, 2)
+PARTS = {2: ((0, 4),), 1: ((0, 4),), 0: ((0, 4),)}
+FACTS = [256, 256, 256]
+ON = {"cx": "SSSS", "G1": ["V1S1V1S1", "V1S1S1S1", "V1S1V1S1"], "G2": ["S1S1S1S1", "V1S1S1S1", "V1S1V1S1"], "XA": "SSS", "XB": "SSS", "SG": "SSS"}
 
-    def op(eng, fn, aps, rd, wr):
-        ops.append((eng, ("c", fn, aps), rd, wr, None))
 
-    def ts(out, in0, s1, s2, o0, o1, rd, wr):
-        if o1 is None:
-            op("V", lambda: V.tensor_scalar(out, in0, s1, None, o0), (out, in0), rd, wr)
-        else:
-            op("V", lambda: V.tensor_scalar(out, in0, s1, s2, o0, o1), (out, in0), rd, wr)
+def calls(rank, n_ranks):
+    ops, marks = [], []
 
-    def tt(out, a, b, o, rd, wr):
-        op("V", lambda: V.tensor_tensor(out, a, b, o), (out, a, b), rd, wr)
+    def part(*tag):
+        marks.append((len(ops), tag))
 
-    def cp(out, a, rd, wr):
-        op("V", lambda: V.tensor_copy(out, a), (out, a), rd, wr)
+    def ts(out, a, s1, s2, o0, o1=None):
+        ops.append(("V", "ts", (out, a, s1, s2, o0, o1)))
 
-    def ms(out, val, wr):
-        op("V", lambda: V.memset(out, val), (out,), [], wr)
+    def tt(out, a, b, o):
+        ops.append(("V", "tt", (out, a, b, o)))
 
-    def scan(out, d0, d1, rd, wr):
-        op("V", lambda: V.tensor_tensor_scan(out, d0, d1, 0.0, A.mult, A.add), (out, d0), rd, wr)
+    def cp(out, a):
+        ops.append(("V", "cp", (out, a)))
 
-    def act(out, a, fn, rd, wr, bias=0.0, scale=1.0):
-        op("S", lambda: S.activation(out, a, fn, bias=bias, scale=scale), (out, a), rd, wr)
+    def ms(out, val):
+        ops.append(("V", "ms", (out, val)))
 
-    def lin(on, out, a, scale, bias, rd, wr):
+    def scan(out, d0, d1, o0, o1):
+        ops.append(("V", "scan", (out, d0, d1, 0.0, o0, o1)))
+
+    def act(out, a, fn=F.Identity, bias=0.0, scale=1.0):
+        ops.append(("S", "act", (out, a, fn, bias, scale)))
+
+    def move(on, out, a):
         if on == "S":
-            act(out, a, F.Identity, rd, wr, bias=bias, scale=scale)
+            act(out, a, F.Copy)
+        elif on == "P":
+            sel(out, a, [[0, count(out)]], 0, 0)
         else:
-            ts(out, a, scale, bias, A.mult, A.add, rd, wr)
+            cp(out, a)
 
-    def mm(out, lt, rhs, start, stop, rd, bank):
-        op("T", lambda: PE.matmul(out, lt, rhs, start, stop), (out, lt, rhs), rd, [bank])
+    def mm(*group):
+        ops.append(("T", "mm", group))
 
-    def iota(out, pat, base, cm, wr, integer=False):
-        if integer:
-            op("P", lambda: g.iota(out, pat, base, cm), (out,), [], wr + ["pool"])
-        else:
-            op("P", lambda: g.iota(out, pat, base, cm, allow_small_or_imprecise_dtypes=True), (out,), [], wr + ["pool"])
+    def chain(items, first=True, last=True):
+        mm(*[m + (first and k == 0, last and k == len(items) - 1) for k, m in enumerate(items)])
 
-    def sel(out, a, pat, base, cm, rd, wr):
-        op("P", lambda: g.affine_select(out, a, pat, A.is_equal, 0.0, base, cm), (out,), rd, wr + ["pool"])
+    def iota(out, pat, base=0, cm=0):
+        ops.append(("P", "iota", (out, pat, base, cm)))
 
-    def dma(eng, sem, out, a, rd, wr):
-        e = {"Y": g.sync, "S": S}[eng]
-        ops.append((eng, ("d", lambda: e.dma_start(out, a), (out,)), rd, wr, (sem, 16)))
+    def sel(out, a, pat, base, cm, o=A.is_equal, other=0.0):
+        ops.append(("P", "sel", (out, a, pat, o, other, base, cm)))
 
-    def send(dst_rank, out, a, sem, rd, local="ls"):
-        dst = T.cores[dst_rank]
-        rid, pid = topo.addr(dst)[:2]
-        bits = sum(1 << e for e in topo.engines(core, dst)[:NE])
-        ops.append(("P", ("r", lambda: g.remote_dma(out, a, T.sem[sem], T.sem[local], pid, rid, bits), (out,), sem), rd, [], (local, NE)))
+    def dma(eng, sem, out, a):
+        ops.append((eng, "dma", (out, a, sem)))
 
-    def arrive(sem, wr):
-        ops.append((None, None, [], wr, (sem, NE)))
+    def send(dst, out, a, sem):
+        ops.append(("P", "send", (dst, out, a, sem)))
+
+    def arrive(out, sem):
+        ops.append((None, "arr", (out, sem)))
 
     def partner(t):
         return (rank + 1 + t % (n_ranks - 1)) % n_ranks
@@ -348,447 +427,332 @@ def calls(g, core, rank, T, topo):
     def asker(t):
         return (rank - 1 - t % (n_ranks - 1)) % n_ranks
 
-    def run(fs):
-        for fn in fs:
-            fn()
+    def rows(name, r0, r1, c0=None, c1=None):
+        return (name, (slice(r0, r1), slice(c0, c1)))
 
-    def weave(a, b):
-        for j in range(max(len(a), len(b))):
-            for x in (a, b):
-                if j < len(x):
-                    x[j]()
+    x16, grp, x4, x32 = (at("PF", j, j + 1) for j in range(4))
+    spare, place = at("PG", 0, 1), at("PG", 1, 2)
+    table, whole = at("TAB", SP, SP + NA), at("TAB")
+    LC, LF, LV, LA, LB = at("LS", 0, 9), at("LS", 10, 19), at("LS", 20, 21), at("LS", 22, 23), at("LS", 24, 25)
+    Ib = at("Ib")
+    turn = [0, 0]
 
-    W = (T.WA, T.WB, T.WC)
-    r15, g16, r3, gg, r7 = (T.PF[:, j:j + 1] for j in range(5))
-    k2, dum = T.K2[:, 0:1], T.K2[:, 4:5]
-    KEYS = ["KR%d" % j for j in range(5)]
-    TABK = ["TAB0", "TAB1", "TAB2", "TAB3"]
+    def bank(k):
+        turn[k] += 1
+        return ("PA", "PB")[k] + str(turn[k] % 2)
 
     for j in range(4):
-        dma("Y", "g%d" % j, T.GI[:, CUT[j]:CUT[j + 1]], T.gloss[:, CUT[j]:CUT[j + 1]], [], ["GI%d" % j])
-    dma("Y", "fx", T.FX[:], T.facts[:], [], ["FX"])
-    dma("S", "s0", T.SI[0:24, :], T.vp0[:], [], ["SI0"])
-    dma("S", "s1", T.SI[24:32, :], T.act0[8:16, :], [], ["SI1"])
-    dma("S", "s2", T.SI[32:40, :], T.act0[0:8, :], [], ["SI2"])
-    dma("S", "dp", T.DI[0:1, :], T.dep0[:], [], ["DI"])
-    dma("S", "rf", T.RF[:, 0:NV], T.refs[:], [], ["RF0"])
-    dma("S", "rw", T.RF[:, NV:NV + 8], T.refs[:, 0:8], [], ["RF1"])
-    dma("S", "cs", T.CS[:], T.cases[:], [], ["CS"])
-    dma("S", "nd", T.NDi[64:64 + ST, :], T.need[:], [], ["NDi"])
+        dma("Y", "g%d" % j, at("GI", CUT[j], CUT[j + 1]), rows("gloss", 0, 128, CUT[j], CUT[j + 1]))
+    dma("Y", "fx", at("FX"), rows("facts", 0, 128))
+    dma("S", "s0", at("SI", p=(0, 24)), rows("vp0", 0, 24))
+    dma("S", "s1", at("SI", p=(24, 32)), rows("act0", 8, 16))
+    dma("S", "s2", at("SI", p=(32, 40)), rows("act0", 0, 8))
+    dma("S", "dp", at("DI", p=(0, 1)), rows("dep0", 0, 1))
+    dma("S", "rf", at("RF", 0, NV), rows("refs", 0, 128))
+    dma("S", "rw", at("RF", NV, NV + 8), rows("refs", 0, 128, 0, 8))
+    dma("S", "cs", at("CNs", 0, L), rows("cases", 0, 128))
+    ms(at("NDi"), 1)
+    dma("S", "nd", at("NDi", p=(0, 12 * ST)), rows("need", 0, ST))
 
-    ms(T.ONh[0:64, :], 1.0, ["ONh"])
-    ms(T.ONE[0:64, :], 1.0, ["ONE"])
-    iota(T.PI[:, 0:1], [[0, 1]], 0, 1, ["PI"], True)
-    iota(T.SR[:], [[0, 27], [1, 16]], 0, 0, ["SR"])
-    sel(T.WQ[0:64, :], T.ONh[0:64, :], [[128, 5], [1, 144]], -15, -16, ["ONh"], ["WQ"])
-    iota(T.XI[:, 0:144], [[1, 144]], 0, 0, ["XI"])
-    iota(T.GB[:], [[16, 8], [0, 16]], 0, 0, ["GB"])
-    iota(T.DM[:], [[1, 128]], 0, -1, ["DM"])
-    sel(T.EXP[0:64, :], T.ONE[0:64, :], [[-1, 64], [0, 16]], 0, 1, ["ONE"], ["EXP"])
-    dma("S", "ex", T.EXP[64:128, :], T.EXP[0:64, :], ["EXP"], ["EXP2"])
-    for s, (chs, C, lo) in enumerate(SETS):
-        ms(W[s][:, 6 * C:9 * C], 0.0, ["Wt%d" % s])
-        ms(W[s][:, 9 * C:10 * C], 1.0, ["Wk%d" % s])
-        ms(W[s][:, 10 * C:11 * C], 2.0, ["Wl%d" % s])
-    ms(T.TAB[:, NA:TW], 0.0, ["TABx"])
-    ms(T.CNs[64:128, :], 0.0, ["CNn"])
-    for j, (num, o) in enumerate(((15, A.bitwise_and), (112, A.bitwise_and), (3, A.bitwise_and), (4, A.logical_shift_right), (7, A.bitwise_and))):
-        ts(T.PJ[:, j:j + 1], T.PI[:, 0:1], num, None, o, None, ["PI"], ["PJ%d" % j])
-    ts(T.W2h[:], T.SR[:, 0:144], 15.0, None, A.is_equal, None, ["SR"], ["W2h"])
-    cp(T.PF[:, 0:5], T.PJ[:, 0:5], ["PJ%d" % j for j in range(5)], ["PF"])
-    cp(T.SF[0:40, :], T.SI[0:40, :], ["SI0", "SI1", "SI2"], ["SF"])
-    cp(T.DF[0:1, :], T.DI[0:1, :], ["DI"], ["DF"])
-    cp(T.SH[0:40, :], T.SF[0:40, :], ["SF"], ["SH"])
-    cp(T.DH[0:1, :], T.DF[0:1, :], ["DF"], ["DH"])
-    for qq in (5, 0, 1, 2, 3, 4):
-        for r in range(16):
-            if qq < 5:
-                mm(T.PZ[:, 12 * qq:12 * qq + 12], T.WQ[0:40, 144 * qq + 15 - r:144 * qq + 143 - r], T.SH[0:40, r:L:16], r == 0, r == 15, ["WQ", "SH"], "#PZ")
-            else:
-                mm(T.PZ[:, 60:72], T.W2h[0:1, 15 - r:143 - r], T.DH[0:1, r:L:16], r == 0, r == 15, ["W2h", "DH"], "#PZ")
-    ts(T.DG[:], T.SR[:], r15, None, A.is_equal, None, ["SR", "PF"], ["DG"])
-    cp(T.IOT[:], T.XI[:, 0:16], ["XI"], ["IOT"])
-    ts(T.BD[:], T.GB[:], g16, None, A.is_equal, None, ["GB", "PF"], ["BD"])
-    ts(T.WS[:], T.XI[:, 0:144], -15.0, g16, A.add, A.is_equal, ["XI", "PF"], ["WS"])
-    ts(T.Ib[:], T.DM[:], 0.0, None, A.is_equal, None, ["DM"], ["Ib"])
-
-    def wk(ch):
-        return ["W%d_%d" % (ch, qq) for qq in range(6)]
-
-    def wall(ch):
-        return wk(ch) + [x + str(ch) for x in ("Wt", "Wk", "Wl", "Wv")]
-
-    def start_state(s):
-        C, c0 = SETS[s][1], SETS[s][2] // 16
-        for qq in (0, 3, 4, 5, 1, 2):
-            act(W[s][:, C * qq:C * qq + C], T.PZ[:, 12 * qq + c0:12 * qq + c0 + C], F.Copy, ["#PZ"], [wk(s)[qq]])
-        act(W[s][:, 11 * C:12 * C], T.PZ[:, c0:c0 + C], F.Identity, ["#PZ"], ["Wv%d" % s], bias=1.0)
-
-    def rows(ch):
-        return slice(64, 128) if LO[ch] > SETS[SET_OF[ch]][2] else slice(0, 64)
-
-    def lanes_first(mt, ch):
-        return mt[rows(ch), 128 * SET_OF[ch]:128 * SET_OF[ch] + 128]
-
-    def convert(j):
-        ts(T.TAB[:, CUT[j]:CUT[j + 1]], T.GI[:, CUT[j]:CUT[j + 1]], -2048.0, None, A.add, None, ["GI%d" % j], [TABK[j]])
-
-    def turn_cases():
-        for ch in range(3):
-            mm(T.PS[0:64, 128 * ch:128 * ch + 128], T.CS[:, LO[ch]:LO[ch] + 64], T.Ib[:], True, True, ["CS", "Ib"], "#PS")
-        act(T.CNs[0:64, :], T.PS[0:64, 0:384], F.Copy, ["#PS"], ["CNc"])
-        cp(T.NDf[64:64 + ST, :], T.NDi[64:64 + ST, :], ["NDi"], ["NDf"])
-        ts(T.CNs[64:64 + ST, 0:L], T.NDf[64:64 + ST, :], 2.0, -1.0, A.mult, A.add, ["NDf"], ["CNn"])
-
-    def send_cases(t):
-        send(partner(t), T.CN[:, 2 * L * t:2 * L * (t + 1)], T.CNs[:], "cn%d" % t, ["CNc", "CNn"] + (["BS%d_2" % (t - 1)] if t else []))
-
-    def later_constants():
-        ts(dum, r15, float(NA + 1), None, A.add, None, ["PF"], ["dum"])
-        ts(T.NEG[0:1, 0:128], T.SR[0:1, 0:128], -1.0, None, A.mult, None, ["SR"], ["NEG"])
-        ts(T.W2[:], T.SR[:, 0:144], 15.0, -2.0, A.is_equal, A.mult, ["SR"], ["W2c"])
-        ts(T.I8[:], T.DM[:], 0.0, -8192.0, A.is_equal, A.mult, ["DM"], ["I8"])
-        ts(T.BDh[:], T.GB[:], g16, None, A.is_equal, None, ["GB", "PF"], ["BDh"])
-        ts(T.BDq[:], T.GB[:], g16, 0.25, A.is_equal, A.mult, ["GB", "PF"], ["BDq"])
-        ts(T.BD8[:], T.GB[:], g16, 8192.0, A.is_equal, A.mult, ["GB", "PF"], ["BD8"])
-        ts(T.BD1[:], T.GB[:], g16, 1024.0, A.is_equal, A.mult, ["GB", "PF"], ["BD1"])
-        ts(T.TA[:], T.DM[:], 0.0, -2048.0, A.is_gt, A.mult, ["DM"], ["TA"])
-        ts(T.TC[:], T.DM[:], 0.0, 2048.0, A.is_equal, A.mult, ["DM"], ["TC"])
-        ts(T.NI[:], T.DM[:], 0.0, -1.0, A.is_equal, A.mult, ["DM"], ["NI"])
-        ts(T.Ih[:, 0:128], T.DM[:], 0.0, None, A.is_equal, None, ["DM"], ["Ih"])
-        tt(T.TA[:], T.TA[:], T.TC[:], A.add, ["TA", "TC"], ["TA"])
-        ts(T.TRI[:], T.SR[:, 0:64], r15, 16384.0, A.is_gt, A.mult, ["SR", "PF"], ["TRI"])
-        ts(T.TD[:], T.DG[:, 0:128], -17.0, 1.0, A.mult, A.add, ["DG"], ["TD"])
-        tt(T.T1[:], T.TA[:], T.BD[:], A.mult, ["TA", "BD"], ["T1"])
-        ts(T.RZ[:], T.SR[:], 0.0, None, A.not_equal, None, ["SR"], ["RZ"])
-        ms(T.MON[64:72, :], 1.0, ["MON"])
-        ts(T.T3[:], T.T1[:], -1.0, None, A.mult, None, ["T1"], ["T3"])
-        tt(T.D0[:, 0:128], T.TD[:], T.RZ[:, 0:128], A.mult, ["TD", "RZ"], ["D0"])
-        ts(T.Ih[:, 128:256], T.DM[:], 0.0, -1.0, A.is_equal, A.mult, ["DM"], ["NIh"])
-        for key, (a, b, val) in zip(KEYS, ((128, 320, 2048.0), (320, 448, 0.0), (448, 512, -16384.0), (512, 576, 0.0), (576, 640, -14336.0))):
-            ms(T.NEG[0:1, a:b], val, [key])
-        ms(T.CC[:], 0.0, ["CC"])
-        ms(T.NO[0:1, :], -1.0, ["NO"])
-        sel(T.NS[64:72, :], T.MON[64:72, :], [[-1, ST], [0, 128]], 0, 1, ["MON"], ["NS"])
-
-    moves = ((0, 0, 11), (0, 1, 1), (0, 2, 2), (0, 3, 6), (0, 4, 6), (0, 5, 11), (1, 3, 11), (2, 4, 11),
-             (3, 4, 7), (3, 2, 8), (4, 3, 7), (4, 1, 8))
-
-    def update_lists():
-        for C, o in ((8, 0), (4, 288)):
-            iota(T.RT[:, o:o + 30 * C], [[C, 5], [1, C], [0, 6]], 0, 0, ["RT%d" % C])
-            iota(T.RT[:, o + 30 * C:o + 36 * C], [[1, C], [C, 3], [0, 2]], 8 * C, 0, ["RTd%d" % C])
-            for n, (qq, slot, blk) in enumerate(moves):
-                ap = T.RT[:, o + 6 * C * qq + slot:o + 6 * C * (qq + 1):6]
-                act(ap, ap, F.Identity, ["RT%d" % C], ["RT%d_%d" % (C, n)], bias=float(C * (blk - qq)))
-        iota(T.CD[:], [[0, 48], [1, 6]], 0, 0, ["CD"])
-        iota(T.JT[:], [[16, 18]], 0, 0, ["JT"])
-        iota(T.LI[:, 0:24], [[8, 6], [0, 4]], 0, 0, ["LI8"])
-        iota(T.LI[:, 24:36], [[4, 6], [0, 2]], 0, 0, ["LI4"])
-        iota(T.BI[:, 0:384], [[0, 6], [1, 8], [0, 8]], 0, 0, ["BI8"])
-        iota(T.BI[:, 384:576], [[0, 6], [1, 8], [0, 4]], 0, 0, ["BI4"])
-
-    def update_lists_2():
-        tt(T.RU[:], T.RT[:], T.DG[:], A.mult, ["DG", "RTd8", "RTd4"] + ["RT%d_%d" % (C, n) for C in (8, 4) for n in range(len(moves))], ["RU"])
-        ts(T.JU[:], T.JT[:], r15, -2.5, A.add, A.add, ["JT", "PF"], ["JU"])
-        scan(T.RV[:], T.RZ[:], T.RU[:], ["RZ", "RU"], ["RV"])
-        ts(T.JI[:], T.JU[:], 1.0 / 6.0, None, A.mult, None, ["JU"], ["JI"])
-        ts(T.RS[:], T.CD[:], 0.0, None, A.not_equal, None, ["CD"], ["RS"])
-        cp(T.LC[:, 0:27], T.RV[:, 15:432:16], ["RV"], ["LC"])
-        ts(T.JK[:, 0:18], T.JI[:], 7, None, A.bitwise_and, None, ["JI"], ["JK8"])
-        ts(T.JK[:, 18:27], T.JI[:, 0:9], 3, None, A.bitwise_and, None, ["JI"], ["JK4"])
-        ts(T.LO[:, 0:24], T.LI[:, 0:24], r7, None, A.add, None, ["LI8", "PF"], ["LO0"])
-        ts(T.LO[:, 24:36], T.LI[:, 24:36], r3, None, A.add, None, ["LI4", "PF"], ["LO1"])
-        cp(T.LF[:, 0:27], T.JK[:, 0:27], ["JK8", "JK4"], ["LF"])
-        ts(T.BG[:], T.BI[:], gg, None, A.is_equal, None, ["BI8", "BI4", "PF"], ["BG"])
-        cp(T.DGh[:], T.DG[:, 0:16], ["DG"], ["DGh"])
-        for C in sorted({s[1] for s in SETS}):
-            ts(T.LA[:, C:2 * C], T.XI[:, 0:C], 6.0, 18.0 * C + 5.0, A.mult, A.add, ["XI"], ["LA"])
-
-    def act_mask(ch, src, key, mt, name, on):
-        n = 16 * SETS[ch][1]
-        out, x = mt[0:n, 128 * ch:128 * ch + 128], T.PC[0:n, 128:256]
-        if on == "S":
-            mm(x, T.ONE[0:1, 0:n], T.NEG[0:1, 0:128], True, False, ["ONE", "NEG"], "#PC")
-            mm(x, src, T.BD[:], False, True, [key, "BD"], "#PC")
-            act(T.XA[0:n, :], x, F.Abs, ["#PC"], ["XA"])
-            act(out, T.XA[0:n, :], F.Relu, ["XA"], [name], bias=1.0, scale=-1.0)
+    ms(at("ONE"), 1.0)
+    iota(at("PI", 0, 1), [[0, 1]], 0, 1)
+    iota(at("SR"), [[0, 32], [1, 16]])
+    sel(at("WQ", p=(0, 64)), at("ONE", p=(0, 64)), [[128, 5], [1, 144]], -15, -16)
+    iota(at("DM"), [[1, 128]], 0, -1)
+    for j, (num, o) in enumerate(((15, A.bitwise_and), (4, A.logical_shift_right), (3, A.bitwise_and), (31, A.bitwise_and),
+                                  (5, A.logical_shift_right))):
+        ts(at("PJ", j, j + 1), at("PI", 0, 1), num, None, o)
+    cp(at("PF", 0, 5), at("PJ", 0, 5))
+    ts(at("W2", p=(0, 1)), at("SR", 0, 144, p=(0, 1)), 15.0, None, A.is_equal)
+    cp(at("SH", p=(0, 40)), at("SI", p=(0, 40)))
+    ts(at("DH", p=(0, 1)), at("DI", p=(0, 1)), 2.0, 2048.0, A.mult, A.add)
+    for qq, name in enumerate(("v", "p1", "p2", "a2", "a1", "d")):
+        out = at("PZ1", 12 * qq, 12 * qq + 12)
+        if name == "d":
+            chain([(out, at("W2", 15 - r, 143 - r, p=(0, 1)), at("DH", r, L, 16, p=(0, 1))) for r in range(16)])
         else:
-            mm(x, src, T.BD[:], True, True, [key, "BD"], "#PC")
-            tt(out, x, T.SR[0:n, 0:128], A.is_equal, ["#PC", "SR"], [name])
+            chain([(out, at("WQ", 144 * qq + 15 - r, 144 * qq + 143 - r, p=(0, 40)), at("SH", r, L, 16, p=(0, 40))) for r in range(16)])
+    ms(at3("W", slice(0, 3), 0, 144), 0)
+    for qq, name in enumerate(("v", "p1", "p2", "a2", "a1", "d")):
+        for nm, add in ((name, 0.0),) + ((("w", 1.0),) if name == "v" else ()):
+            o, s = END[nm]
+            ts(at3("W", slice(0, 3), o, o + 3 * s + 1, s), at("PZ1", 12 * qq, 12 * qq + 12), add, None, A.add)
+    for k, val in enumerate(CELLS):
+        ms(at3("W", slice(0, 3 * ST), 152 + k, 153 + k), val)
+    ts(at("DG"), at("SR", 0, 416), x16, None, A.is_equal)
+    ts(at("RZ"), at("SR", 0, 416), 0.0, None, A.not_equal)
+    ts(at("MKT"), at("SR"), x16, 8192.0, A.is_equal, A.mult)
+    ts(Ib, at("DM"), 0.0, None, A.is_equal)
+    ts(at("LN"), at("SR", 0, 128, 16), x16, None, A.add)
+    ts(at("CNs", L, 320), by(at("NDi"), at("LN")), 2.0, -1.0, A.mult, A.add)
+    ts(spare, x16, -2.0, -2050.0, A.mult, A.add)
+    ts(place, x16, 8.0, grp, A.mult, A.add)
+    iota(at("LXi"), [[128, 4]])
+    ts(at("LX"), at("LXi"), place, None, A.add)
+    ms(at("TAB", 0, SP), 0.0)
+    for name in ("MX2", "MX1"):
+        ms(at(name), 0.0)
+    for name in ("PA0", "PA1"):
+        ms(at(name, 0, 128), 0.0)
+    sel(at("S2", 0, 64), at("ONE", 0, 64), [[-1, 16], [-32, 4]], 0, 1)
+    sel(at("S2", 64, 128), at("ONE", 0, 64), [[-32, 4], [-1, 16]], 0, 1)
 
-    def ask(s, t, on):
-        chs, C, lo = SETS[s]
-        w, c0, al, ln = W[s], lo // 16, 24 * t + lo // 8, slice(lo, lo + 16 * C)
-        w0 = 3 * C // 8 * 8
-        send(partner(t), T.AL[:, al:al + 2 * C], w[:, 4 * C:6 * C], "a%d_%d" % (s, t), wk(s)[4:6], "l%d_%d" % (s, t))
-        if t:
-            cp(T.VU[:, c0:c0 + C], T.SO[:, 5:6 * C:6], ["SO"], ["VU%d" % s])
+    ms(at("RT"), 0.0)
+    for name in ("a2", "a1", "p1", "p2"):
+        o, s = AT[name]
+        iota(at("RT", o, o + 4 * s), [[END[name][1], 4], [0, s]], END[name][0])
+    iota(at("RT", 72, 96), [[0, 4], [1, 6]], 152)
+    for name, case, src in MOVES:
+        o, s = AT[name]
+        iota(at("RT", o + case, o + case + 3 * s + 1, s), [[END[src][1], 4]], END[src][0])
+    for o, s, blocks in ((0, 7, 1), (28, 5, 1), (48, 6, 4)):
+        iota(at("RT", 160 + o, 160 + o + 4 * s * blocks), [[0, blocks], [1, 4], [0, s]], END["code"][0])
+        iota(at("CD", o, o + 4 * s * blocks), [[0, 4 * blocks], [1, s]])
+    iota(at("RT", 166, 188, 7), [[0, 4]], END["six"][0])
+    iota(at("RT", 211, 230, 6), [[0, 4]], END["six"][0])
+    for o, names in ((320, ("v", "a2", "a1", "d")), (352, ("v", "p1", "p2", "d")), (384, ("a1", "a2"))):
+        for k, name in enumerate(names):
+            iota(at("RT", o + 4 * k, o + 4 * k + 4), [[END[name][1], 4]], END[name][0])
+    for a, b in ((320, 336), (0, 160), (160, 320), (336, 416)):
+        tt(at("RU", a, b), at("RT", a, b), at("DG", a, b), A.mult)
+        scan(at("RV", a, b), at("RZ", a, b), at("RU", a, b), A.mult, A.add)
+        cp(at("LS", a // 16, b // 16), at("RV", a + 15, b, 16))
+    ts(at("RS"), at("CD"), 0.0, None, A.not_equal)
+
+    top = (0, 64)
+    iota(at("RA", p=top), [[1, 4], [4, 16]], 0, -1)
+    iota(at("RB", p=top), [[1, 4], [0, 16]])
+    ts(at("CE", p=top), at("RB", p=top), at("PF", 2, 3, p=top), None, A.is_equal)
+    ts(at("RC", p=top), at("RA", p=top), 0.0, 16384.0, A.is_equal, A.mult)
+    ts(at("RE", p=top), at("RA", p=top), 0.0, -8192.0, A.is_ge, A.mult)
+    tt(at("RC", p=top), at("RC", p=top), at("RE", p=top), A.add)
+    tt(at("RM", 0, 64, p=top), at("RC", p=top), at("CE", p=top), A.mult)
+    ms(at("RM", 64, 128, p=top), 0.0)
+    ts(at("RM", 79, 128, 16, p=top), at("CE", 0, 64, 16, p=top), -1.0, None, A.mult)
+    cp(at("RM", 128, 192, p=top), at("RM", 0, 64, p=top))
+    ts(at("RM", 192, 256, p=top), at("RM", 0, 64, p=top), -1.0, None, A.mult)
+    ts(at("RM", 256, 260, p=top), at("CE", 0, 64, 16, p=top), -2080.0, None, A.mult)
+    row = (0, 1)
+    ts(at("CR", 0, 64, p=row), at("SR", 0, 64, p=row), -8192.0, -4096.0, A.mult, A.add)
+    ts(at("CR", 64, 128, p=row), at("SR", 0, 64, p=row), 15.0, -15.0, A.is_equal, A.mult)
+    ts(at("CR", 128, 256, p=row), at("SR", 0, 128, p=row), -8192.0, -8192.0, A.mult, A.add)
+    ms(at("CR", 256, 260, p=row), -131072.0)
+    ms(at("CS", p=row), 31168.0)
+    ts(at("I32"), at("DM"), 0.0, 32768.0, A.is_equal, A.mult)
+    ts(at("RS1"), at("SR", 0, 128), 0.0, None, A.not_equal)
+    ts(at("RS2", 0, 128), at("SR", 0, 128), 60000.0, spare, A.mult, A.add)
+    ts(at("RS2", 128, 132), at("SR", 0, 64, 16), spare, None, A.add)
+    ts(at("D1"), at("SR", 0, L), 0.0, spare, A.mult, A.add)
+    ts(at("TRI"), at("SR", 0, L), x16, 8192.0, A.is_gt, A.mult)
+    ms(at("M2"), -2.0)
+    for j in range(3):
+        sel(at("EW", 320 * j, 320 * j + 320, p=top), at("ONE", 0, 320, p=top), [[-4, 5], [0, 16], [-1, 4]], -20 * j, 1)
+    iota(at("GB"), [[1, 8], [0, 16]])
+    ts(at("BD"), at("GB"), grp, None, A.is_equal)
+    ts(at("NI"), at("DM"), 0.0, -1.0, A.is_equal, A.mult)
+    for r in range(16):
+        act(at("SEL", 128 * r, 128 * r + 128), at("BD"), scale=at("DG", r, r + 1))
+    for j in range(4):
+        chain([(at("PC"), Ib, at("SEL", 512 * j, 512 * j + 512))] + [(at("PC", 128 * r, 128 * r + 128), Ib, at("NI")) for r in range(4)])
+        act(at("SED", 512 * j, 512 * j + 512), at("PC"), F.Copy)
+    iota(at("XI"), [[1, 240]], -112)
+    ts(at("PG", 4, 8), at("SR", 0, 4), at("PF", 4, 5), None, A.is_equal)
+    for q in range(4):
+        ts(at("WY", 240 * q, 240 * q + 240), at("XI"), x32, at("PG", 4 + q, 5 + q), A.is_equal, A.mult)
+    iota(at("LI"), [[4, 6], [0, 2]])
+    iota(at("BI"), [[0, 6], [1, 8], [0, 4]])
+    ts(at("LO"), at("LI"), x4, None, A.add)
+    ts(at("BG"), at("BI"), grp, None, A.is_equal)
+    ts(at("BG", 96, 128), at("BI", 96, 128), grp, 0.5, A.is_equal, A.mult)
+    cp(at("DGh"), at("DG", 0, 16))
+    for j in range(4):
+        ts(at("TAB", SP + CUT[j], SP + CUT[j + 1]), at("GI", CUT[j], CUT[j + 1]), -2048.0, None, A.add)
+
+    def cases(t):
+        part(t - 1, "cases", 0)
+        send(partner(t), at("CN", 320 * t, 320 * t + 320), at("CNs"), "cn%d" % t)
+        arrive(at("CN", 320 * t, 320 * t + 320), "cn%d" % t)
+        k = slice(3 * t, 3 * t + 3)
+        part(t - 1, "cases", 1)
+        on = ON["cx"] if t else "SSSS"
+        move(on[0], at3("CX", k, 0, 64), at("CN", 320 * t, 320 * t + L))
+        for w in (64, 128):
+            move(on[w // 64], at3("CX", k, w, 2 * w), at3("CX", k, 0, w))
+        part(t - 1, "cases", 2)
+        for ch in CHS:
+            if FACTS[ch] == 512:
+                move(on[3], at3("CX", 3 * t + ch, 256, 512), at3("CX", 3 * t + ch, 0, 256))
+
+    def masks(name, ch, acts):
+        act(at("MK" + name, 64 * ch, 64 * ch + 64), by(at("MKT"), acts), F.Copy)
+        cp(by(at("MX" + name, 512 * ch, 512 * ch + 512), at("LX")), at("MK" + name, 64 * ch, 64 * ch + 64))
+
+    def pick(t, level, ch, q0, q1, x):
+        pa, g, mx, lists = bank(0), "G%d" % level, "MX%d" % (3 - level), ("R16", 64 * ch) if level == 1 else ("BL", 240 * t + 80 * ch + 16)
+        plan, q = ON[g][ch], 0
+        for on, blocks in zip(plan[::2], plan[1::2]):
+            a, q = q, q + int(blocks)
+            if q0 <= a < q1:
+                move(on, at(g, 1024 * ch + 256 * a, 1024 * ch + 256 * q), by(table, at(lists[0], lists[1] + 16 * a, lists[1] + 16 * q)))
+                group = []
+                for lane in range(16 * a, 16 * q):
+                    o, r, p0 = 1024 * ch + lane // 16 * 256, lane % 16, lane // 16 * 32
+                    lt = at(g, o + 16 * r, o + 16 * r + 16) if level == 1 else at(g, o + r, o + 256, 16)
+                    group.append((at(pa, r, 128, 16, p=(p0, p0 + 16)), lt, at(mx, 512 * ch + 8 * lane, 512 * ch + 8 * lane + 8), True, True))
+                mm(*group)
+        p = (32 * q0, 32 * q1)
+        part(t, x, ch)
+        if ON[x][ch] == "S":
+            act(at(x, 128 * ch, 128 * ch + 128, p=p), at(pa, 0, 128, p=p), scale=1.0 / 8192.0)
         else:
-            cp(T.VU[:, c0:c0 + C], w[:, 0:C], wk(s)[0:1], ["VU%d" % s])
-        cp(T.R16[:, ln], T.RF[:].indirect(T.VU[:, c0:c0 + C]), ["RF0", "RF1", "VU%d" % s], ["R16%d" % s])
-        if t:
-            tt(T.RA[:, ln], T.SO[:, 0:36 * C].indirect(T.LA[:, C:2 * C]), T.DG[:, 0:16 * C], A.mult, ["SO", "LA", "DG"], ["RA%d" % s])
-        else:
-            tt(T.RA[:, ln], w[:, w0:4 * C].indirect(T.IOT[:, 3 * C - w0:4 * C - w0]), T.DG[:, 0:16 * C], A.mult,
-               wk(s)[w0 // C:4] + ["IOT", "DG"], ["RA%d" % s])
-        act_mask(s, T.RA[:, ln], "RA%d" % s, T.MT2, "MT2%d" % s, on)
+            ts(at(x, 128 * ch, 128 * ch + 128, p=p), at(pa, 0, 128, p=p), 1.0 / 8192.0, None, A.mult)
+        return at(x, 128 * ch, 128 * ch + 128, p=p), p
 
-    def serve(s, t, on):
-        chs, C, lo = SETS[s]
-        al, key, o, n = 24 * t + lo // 8, "AL%d_%d" % (s, t), 2 * lo, 16 * C
-        arrive("a%d_%d" % (s, t), [key])
-        tt(T.RD[:, o:o + 2 * n], T.AL[:, al:al + 2 * C].indirect(T.IOT[:, 0:2 * C]), T.DG[:, 0:2 * n], A.mult, [key, "IOT", "DG"], ["RD%d" % s])
-        act_mask(s, T.RD[:, o:o + n], "RD%d" % s, T.MT1, "MT1%d" % s, on)
-        for ch in chs:
-            a = 128 + LO[ch] - lo
-            mm(T.PU[:, a:a + 64], lanes_first(T.MT1, ch), T.Ib[rows(ch), rows(ch)], True, True, ["MT1%d" % s, "Ib"], "#PU")
-        lin(ON["NM"][s], T.NM[:, lo:lo + n], T.PU[:, 128:128 + n], -16384.0, 8192.0, ["#PU"], ["NM%d" % ch for ch in chs])
+    def ask(t, ch):
+        o = 240 * t + 80 * ch
+        cp(at("BS", o, o + 16), by(at3("W", 3 * t + ch, 0, 144), LV))
+        if ch in AHEAD:
+            send(partner(t), at("BL", o + 8, o + 16), at("BS", o + 8, o + 16), "a%d_%d" % (ch, t))
+        cp(at("R16", 64 * ch, 64 * ch + 64), by(at("RF"), at("BS", o, o + 4)))
+        part(t - 1, "mask", ch)
+        masks("2", ch, at("BS", o + 4, o + 8))
 
-    def gather(t, n, level, ch, p):
-        lo = LO[ch] + 32 * p
-        win, wkeys = T.TAB[:, 0:NA], TABK
-        if level == 1:
-            off, key = T.R16[:, lo:lo + 32], "R16%d" % SET_OF[ch]
-        elif level == 2:
-            off, key = T.BL[:, L * t + lo:L * t + lo + 32], "BL%d_%d" % (t, ch)
-            if p == 0:
-                arrive("b%d_%d" % (ch, t), [key])
-            elif ch == 0:
-                key = "BH%d" % t
-                arrive("h%d" % t, [key])
-        else:
-            off, key, win, wkeys = T.TU[:, lo:lo + 32], "TU%d" % ch, T.FX[:], ["FX"]
-        act(T.G[:, 512 * (n % 4):512 * (n % 4) + 512], win.indirect(off), F.Copy, wkeys + [key], ["G%d" % (n % 4)])
+    def message(t, ch, q0, q1):
+        o = 240 * t + 80 * ch + 16
+        return o + 16 * q0 - (8 if q0 == 0 and ch not in AHEAD else 0), o + 16 * q1
 
-    def widen(t, n, level, ch, p):
-        if level == 3:
-            src, key = T.CN[0:64, 2 * L * t + 128 * ch:2 * L * t + 128 * ch + 128], "CN%d" % t
-        else:
-            src, key = lanes_first((T.MT2, T.MT1)[level - 1], ch), "MT%d%d" % (3 - level, SET_OF[ch])
-        at = rows(ch) if level < 3 else slice(0, 64)
-        mm(T["PM%d" % (n % 2)][:], src, T.EXP[at, 512 * p:512 * p + 512], True, True, [key, "EXP2" if at.start else "EXP"], "#PM%d" % (n % 2))
+    def level1(t, ch):
+        for n, (q0, q1) in enumerate(PARTS[ch]):
+            part(t, "one", ch)
+            x, p = pick(t, 1, ch, q0, q1, "XA")
+            pb, o, w = bank(1), 240 * t + 80 * ch + 16 + 16 * q0, 16 * (q1 - q0)
+            mm((at(pb, 0, w), x, at("S2", 64 + 16 * q0, 64 + 16 * q1, p=p), True, True))
+            ts(at("BS", o, o + w), at(pb, 0, w), 2048.0, None, A.add)
+            send(partner(t), at("BL", *message(t, ch, q0, q1)), at("BS", *message(t, ch, q0, q1)), "%s%d_%d" % ("bh"[n], ch, t))
 
-    def mask(t, n, level, ch, p):
-        m = ch
-        out, key, o = (T.CB, "CB", A.is_le) if level == 3 else (T.M, "M", A.mult)
-        tt(out[:, 1024 * m + 512 * p:1024 * m + 512 * p + 512], T.G[:, 512 * (n % 4):512 * (n % 4) + 512], T["PM%d" % (n % 2)][:], o,
-           ["G%d" % (n % 4), "#PM%d" % (n % 2)], ["%s%d_%d" % (key, m, p)])
-
-    def wide_cases(t, n):
-        arrive("cn%d" % t, ["CN%d" % t])
-        for j, name in enumerate(FUSED):
-            widen(t, n + j, 3, int(name[1]), int(name[2]))
-            bank = "PM%d" % ((n + j) % 2)
-            act(T.CX[:, 512 * j:512 * j + 512], T[bank][:], F.Copy, ["#" + bank], ["CX%d" % j])
-
-    def compare(t, ch, p):
-        j, lo = FUSED.index("3%d%d" % (ch, p)), LO[ch] + 32 * p
-        tt(T.CB[:, 1024 * ch + 512 * p:1024 * ch + 512 * p + 512], T.FX[:].indirect(T.TU[:, lo:lo + 32]), T.CX[:, 512 * j:512 * j + 512],
-           A.is_le, ["FX", "TU%d" % ch, "CX%d" % j], ["CB%d_%d" % (ch, p)])
-
-    def pick(level, ch):
-        m = ch
-        for k in range(16):
-            mm(T.PL[:, 0:64], T.WS[:, 15 - k:143 - k], T.M[:, 1024 * m + k:1024 * m + 1024:16], k == 0, k == 15,
-               ["WS", "M%d_0" % m, "M%d_1" % m], "#PL")
-
-    def send_half(t, p):
-        o, key = L * t + LO[0] + 32 * p, "BS%d_0%d" % (t, p)
-        for k in range(16):
-            mm(T.PL[:, 0:32], T.WS[:, 15 - k:143 - k], T.M[:, 512 * p + k:512 * p + 512:16], k == 0, k == 15, ["WS", "M0_%d" % p], "#PL")
-        ts(T.BS[:, o:o + 32], T.PL[:, 0:32], 2048.0, None, A.add, None, ["#PL"], [key])
-        send(partner(t), T.BL[:, o:o + 32], T.BS[:, o:o + 32], ("h%d" if p else "b0_%d") % t, [key])
-
-    def send_b(t, ch):
-        o = L * t + LO[ch]
-        ts(T.BS[:, o:o + 64], T.PL[:, 0:64], 2048.0, None, A.add, None, ["#PL"], ["BS%d_%d" % (t, ch)])
-        send(partner(t), T.BL[:, o:o + 64], T.BS[:, o:o + 64], "b%d_%d" % (ch, t), ["BS%d_%d" % (t, ch)])
-
-    def take_t(t, ch):
-        lo, o = LO[ch], 256 * ch
-        ts(T.TU[:, lo:lo + 64], T.PL[:, 0:64], 2048.0, None, A.add, None, ["#PL"], ["TU%d" % ch])
-        ts(T.TB[:, o + 64:o + 128], T.BL[:, L * t + lo:L * t + lo + 64], -2048.0, None, A.add, None, ["BL%d_%d" % (t, ch), "BH%d" % t], ["TBb%d" % ch])
-        cp(T.TB[:, o:o + 64], T.PL[:, 0:64], ["#PL"], ["TBa%d" % ch])
+    def level2(t, ch):
+        o = 240 * t + 80 * ch + 16
+        part(t, "acts", ch)
+        if ch in AHEAD:
+            arrive(at("BL", o - 8, o), "a%d_%d" % (ch, t))
+        for n, (q0, q1) in enumerate(PARTS[ch]):
+            arrive(at("BL", *message(t, ch, q0, q1)), "%s%d_%d" % ("bh"[n], ch, t))
+        masks("1", ch, at("BL", o - 8, o - 4))
+        part(t, "keys", ch)
+        ts(at("BB", 72 * ch, 72 * ch + 68), at("BL", o - 4, o + 64), -2048.0, None, A.add)
+        part(t, "two", ch)
+        x, p = pick(t, 2, ch, 0, 4, "XB")
+        pb, ln = bank(1), (64 * ch, 64 * ch + 64)
+        mm((at(pb, 0, 64), x, at("S2", 0, 64), True, True))
+        ts(at("TU", *ln), at(pb, 0, 64), 2048.0, None, A.add)
+        part(t, "yt", ch)
         if t == ST - 1:
-            lin(ON["TB"][ch], T.YS[:, lo:lo + 64], T.PL[:, 0:64], 1.0, 2048.0, ["#PL"], ["YS%d" % ch])
-            send(asker(t), T.YL[:, lo:lo + 64], T.YS[:, lo:lo + 64], "yt%d" % ch, ["YS%d" % ch])
+            for q in range(4):
+                chain([(at("PD", 256 + 16 * q, 272 + 16 * q), at("WY", 240 * q + 112 - 16 * g, 240 * q + 240 - 16 * g),
+                        at("XB", 128 * ch + 16 * g, 128 * ch + 16 * g + 16)) for g in range(8)])
+            act(at("YS", *ln), at("PD", 256, 320), bias=2048.0)
+            send(asker(t), at("YL", *ln), at("YS", *ln), "yt%d" % ch)
 
-    def count(t, ch):
-        lo, o, m = LO[ch], 256 * ch, ch
-        nd = 2 * L * t + lo
-        mm(T.PC[:, 0:64], T.NS[64:72, 128 * t:128 * t + 128], T.CN[64:72, nd:nd + 64], True, False, ["NS", "CN%d" % t], "#PC")
-        for k in range(16):
-            mm(T.PC[:, 0:64], T.W2[:, 15 - k:143 - k], T.CB[:, 1024 * m + k:1024 * m + 1024:16], False, k == 15,
-               ["W2c", "CB%d_0" % m, "CB%d_1" % m], "#PC")
-
-    def before(ch):
-        o = 256 * ch
-        z, zk = T[ZB[ch]], "#" + ZB[ch]
-        mm(z[:, 0:256], T.NEG[0:1, 0:128], T.NEG[0:1, 128:384], True, False, ["NEG"] + KEYS, zk)
-        mm(z[:, 0:256], T.ONE[0:1, 0:128], T.NEG[0:1, 384:640], False, False, ["ONE"] + KEYS, zk)
-        mm(z[:, 0:128], T.Ih[:, 128:256], T.TB[:, o:o + 128], False, False, ["NIh", "TBa%d" % ch, "TBb%d" % ch], zk)
-        mm(z[:, 128:192], T.Ih[:, 128:256], T.TB[:, o:o + 64], False, False, ["NIh", "TBa%d" % ch], zk)
-        d = SETS[SET_OF[ch]][2] + 16 * SETS[SET_OF[ch]][1] + LO[ch]
-        mm(z[:, 64:128], T.BD8[:], T.RD[:, d:d + 64], False, False, ["BD8", "RD%d" % SET_OF[ch]], zk)
-
-    def signs(ch):
-        if ON["UN"][ch] == "S":
-            act(T.UN[:], T.PC[:, 0:64], F.Sign, ["#PC"], ["UN"])
+    def level3(t, ch):
+        z, x, d2 = "PZ%d" % (ch % 2), at("XB", 128 * ch, 128 * ch + 128), at("BB", 72 * ch, 72 * ch + 4)
+        part(t, "before", ch)
+        chain([(at(z, 0, 260), at("ONE", 0, 128, p=row), at("CR", p=row)), (at(z, 128, 192), Ib, at("BB", 72 * ch + 4, 72 * ch + 68)),
+               (at(z, 78, 128, 16), Ib, d2), (at(z, 79, 128, 16), Ib, d2), (at(z, 256, 260), at("I32"), d2),
+               (at(z, 256, 260), at("ONE", 0, 128, p=row), at("CS", p=row)),
+               (at(z, 0, 64), x, at("S2", 64, 128)), (at(z, 192, 256), x, at("S2", 64, 128))], last=False)
+        part(t, "three", ch)
+        for o in range(1024 * ch, 1024 * ch + 1024, FACTS[ch]):
+            tt(at("CB", o, o + FACTS[ch]), by(at("FX"), at("TU", o // 16, (o + FACTS[ch]) // 16)), at3("CX", 3 * t + ch, 0, FACTS[ch]), A.is_le)
+        part(t, "count", ch)
+        for r0, r1 in ((0, 32), (32, 64)) if ch in HALVED else ((0, 64),):
+            o, e = 1024 * ch + 16 * r0, 64 * (3 * t + ch)
+            chain([(at("PC", 0, 128, p=(r0, r1)), at("EW", e + r0, e + r1, p=(0, 12 * ST)), at("CN", 320 * t + L, 320 * t + 320, p=(0, 12 * ST)))]
+                  + [(at("PC", r, 128, 16, p=(r0, r1)), at("CB", o + r, o + 16 * (r1 - r0), 16), at("M2")) for r in range(16)])
+        sg = at("SG", 128 * ch, 128 * ch + 128, p=top)
+        if ON["SG"][ch] == "S":
+            act(sg, at("PC", 0, 128, p=top), F.Sign)
         else:
-            ts(T.UN[:], T.PC[:, 0:64], -1.0, 1.0, A.max, A.min, ["#PC"], ["UN"])
-        for j, (lt, key) in enumerate(((T.T1, "T1"), (T.T1, "T1"), (T.T3, "T3"), (T.BD1, "BD1"))):
-            mm(T[ZB[ch]][:, 64 * j:64 * j + 64], lt[:], T.UN[:], False, j == 3, [key, "UN"], "#" + ZB[ch])
+            ts(sg, at("PC", 0, 128, p=top), -1.0, 1.0, A.max, A.min)
+        chain([(at(z, 0, 260), sg, at("RM", p=top))], first=False)
+        o, a = 128 * ch, 24 * t + 8 * ch
+        part(t, "reply", ch)
+        scan(at("ST", o, o + 128), at("RS1"), at(z, 0, 128), A.mult, A.max)
+        ts(at("RP", a, a + 8), at("ST", o + 15, o + 128, 16), NV - 1, None, A.bitwise_and)
+        send(asker(t), at3("W", 3 * t + ch, 144, 152), at("RP", a, a + 8), "r%d_%d" % (ch, t))
+        part(t, "found", ch)
+        scan(at3("SB", ch, 0, 132), at("RS2"), at(z, 128, 260), A.min, A.max)
 
-    def verdict(ch):
-        ts(T.X[:], T[ZB[ch]][:, 0:256], 0.0, -2048.0, A.max, A.add, ["#" + ZB[ch]], ["X"])
-        mm(T.PU[:, 0:64], T.Ih[:, 0:128], T.TRI[:], True, False, ["Ih", "TRI"], "#PU")
-        mm(T.PU[:, 0:64], T.BDh[:], T.X[:, 64:128], False, False, ["BDh", "X"], "#PU")
-        mm(T.PU[:, 0:64], T.BDq[:], T.X[:, 192:256], False, True, ["BDq", "X"], "#PU")
-        mm(T.PU[:, 64:128], lanes_first(T.MT1, ch), T.I8[rows(ch), rows(ch)], True, False, ["MT1%d" % SET_OF[ch], "I8"], "#PU")
-        mm(T.PU[:, 64:128], T.BDh[:], T.X[:, 128:192], False, True, ["BDh", "X"], "#PU")
-        for r in range(16):
-            mm(T.PS[:, 0:8], T.WS[:, 15 - r:143 - r], T.X[:, r:128:16], r == 0, r == 15, ["WS", "X"], "#PS")
-
-    def answer(t, ch):
-        lo = LO[ch]
-        o, c = 12 * t + lo // 16, (lo // 16 - 4) % 12
-        lin(ON["TH"][ch], T.TH[:, lo:lo + 64], T.PU[:, 64:128], -1.0, -38912.0, ["#PU"], ["TH%d" % ch])
-        lin(ON["TH"][ch], T.RB[:, lo:lo + 64], T.PU[:, 0:64], -1.0, -36864.0, ["#PU"], ["RB%d" % ch])
-        ts(T.OB[:, c:c + 4], T.PS[:, 4:8], -1.0, -28672.0, A.mult, A.add, ["#PS"], ["OB%d" % ch])
-        ts(T.RPs[:, o:o + 4], T.PS[:, 0:4], -1.0, -28672.0, A.mult, A.add, ["#PS"], ["RPs%d_%d" % (t, ch)])
-        send(asker(t), T.RPl[:, o:o + 4], T.RPs[:, o:o + 4], "r%d_%d" % (ch, t), ["RPs%d_%d" % (t, ch)])
-        lin(ON["BC"][ch], T.BCF[:, c:c + 4], T.PS[:, 4:8], -1.0, -28672.0, ["#PS"], ["BCF%d" % ch])
-        lin(ON["BC"][ch], T.BCS[:, c:c + 4], T.PS[:, 4:8], -1.0 / 8192.0, -2.5, ["#PS"], ["BCS%d" % ch])
-
-    def write_ops(chs):
-        C, lo, s = 4 * len(chs), LO[chs[-1]], str(chs[0])
-        ln = slice(lo, lo + 16 * C)
-        c0 = (lo // 16 - 4) % 12
-        cs = slice(c0, c0 + C)
-
-        def k(name):
-            return [name + str(ch) for ch in chs]
-        return [
-            lambda: tt(T.DD[:, ln], T.TAB[:].indirect(T.OB[:, cs]), T.NM[:, ln], A.min, TABK + ["TABx"] + k("OB") + k("NM"), k("EE")),
-            lambda: tt(T.EQ[:, ln], T.BCF[:, cs].indirect(T.IOT[:, 0:C]), T.RB[:, ln], A.is_equal, ["IOT"] + k("BCF") + k("RB"), ["EQ" + s]),
-            lambda: scan(T.SC[:, ln], T.D0[:, 0:16 * C], T.EQ[:, ln], ["D0", "EQ" + s], ["SC" + s]),
-            lambda: tt(T.T2[:, cs], T.BCS[:, cs], T.SC[:, lo + 15:lo + 16 * C:16], A.subtract, k("BCS") + ["SC" + s], ["T2" + s]),
-            lambda: ts(T.OF[:, lo // 8:lo // 8 + 2 * C:2], T.T2[:, cs], 8192.0, dum, A.mult, A.min, ["T2" + s, "dum"], k("OF")),
-        ]
+    def writes(t, lo, hi):
+        ln, w, k = (64 * lo, 64 * hi), 64 * (hi - lo), slice(lo, hi)
+        art = at("D1", ln[0], ln[1], 16)
+        part(t, "writes", lo)
+        tt(art, at3("SB", k, 15, 64, 16), at3("SB", k, 128, 132), A.min)
+        chain([(at("PD", 0, w), Ib, at("TRI", 0, w))]
+              + [(at("PD", r + 1, w, 16), at("SED", 128 * r, 128 * r + 128), art) for r in range(15)])
+        ts(at("EE", *ln), at("PD", 0, w), 0.0, -8192.0, A.is_equal, A.mult)
+        scan(at("SC", *ln), at("EE", *ln), at("D1", *ln), A.add, A.max)
+        ts(at("OF", 8 * lo, 8 * hi, 2), at("SC", ln[0] + 15, ln[1], 16), 2048.0 + SP, None, A.add)
+        part(t, "old", lo)
+        ts(at("OB", 4 * lo, 4 * hi), art, 2048.0 + SP, None, A.add)
+        pb = bank(1)
+        chain([(at(pb, 0, w), Ib, at("MK1", *ln))]
+              + [(at(pb, r, w, 16), at("SEL", 128 * r, 128 * r + 128), at3("SB", k, 79, 128, 16)) for r in range(16)])
+        act(at("TH", *ln), at(pb, 0, w), bias=-8192.0)
+        tt(at("DD", *ln), by(whole, at("OB", 4 * lo, 4 * hi)), at("MK1", *ln), A.subtract)
 
     def scatter(c):
-        ch, ln = 2 - c // 4, slice(16 * c, 16 * c + 16)
-        return lambda: tt(T.TAB[:].indirect(T.OF[:, 2 * c:2 * c + 1]), T.TH[:, ln], T.DD[:, ln], A.max,
-                          ["OF%d" % ch, "EE%d" % ch, "TH%d" % ch], TABK + ["TABx"])
+        ln = (16 * c, 16 * c + 16)
+        tt(by(whole, at("OF", 2 * c, 2 * c + 1)), at("TH", *ln), at("DD", *ln), A.max)
 
-    def update(s, t):
-        chs, C, lo = SETS[s]
-        w, o, n = W[s], 12 * t + lo // 16, 36 * C
-        rp, rk, ls = T.RPl[:, o:o + C], ["RPl%d_%d" % (t, ch) for ch in chs], slice(0, 18) if C == 8 else slice(18, 27)
-        for ch in chs:
-            arrive("r%d_%d" % (ch, t), ["RPl%d_%d" % (t, ch)])
-        ts(T.U3[:, 0:C], rp, float(NA), 3.0, A.is_lt, A.mult, rk, ["U3"])
-        ts(T.TI[:, 0:C], rp, NV - 1, None, A.bitwise_and, None, rk, ["TI0"])
-        ts(T.TI[:, C:2 * C], rp, 15, None, A.bitwise_and, None, rk, ["TI1"])
-        tt(T.CC[:, 0:C], w[:, 5 * C:6 * C], T.U3[:, 0:C], A.add, [wk(s)[5], "U3"], ["CC"])
-        cp(w[:, 6 * C:8 * C], T.TI[:, 0:2 * C], ["TI0", "TI1"], ["Wt%d" % s])
-        tt(T.FF[:, 0:n], T.CC[:].indirect(T.LF[:, ls]), T.CD[:, 0:n], A.is_equal, ["CC", "LF", "CD"], ["FF"])
-        tt(T.PP[:, 0:n], w[:, 0:12 * C].indirect(T.LC[:, ls]), T.FF[:, 0:n], A.mult, wall(s) + ["LC", "FF"], ["PP"])
-        scan(T.SO[:, 0:n], T.RS[:, 0:n], T.PP[:, 0:n], ["RS", "PP"], ["SO"])
-        lin(ON["W"][s], w[:, 0:6 * C], T.SO[:, 5:n:6], 1.0, 0.0, ["SO"], wk(s))
-        lin(ON["W"][s], w[:, 11 * C:12 * C], T.SO[:, 5:6 * C:6], 1.0, 1.0, ["SO"], ["Wv%d" % s])
+    def update(t, ch):
+        k, ln = 3 * t + ch, (144 * ch, 144 * ch + 144)
+        arrive(at3("W", k, 144, 152), "r%d_%d" % (ch, t))
+        tt(at("FF", *ln), by(at3("W", k), LF), at("CD"), A.is_equal)
+        tt(at("PP", *ln), by(at3("W", k), LC), at("FF", *ln), A.mult)
+        scan(at3("W", k + 3, 0, 144), at("RS"), at("PP", *ln), A.mult, A.add)
 
-    def final(s):
-        chs, C, lo = SETS[s]
-        w, o, n, k = W[s], 3 * lo, 48 * C, int(C == 4)
-        ts(T.MD[:, 0:3 * C], w[:, 0:3 * C], float(NV), -float(NV), A.is_ge, A.mult, wk(s)[0:3], ["MD"])
-        tt(w[:, 0:3 * C], w[:, 0:3 * C], T.MD[:, 0:3 * C], A.add, wk(s)[0:3] + ["MD"], wk(s)[0:3])
-        tt(T.RO[:, o:o + n], w[:, 0:12 * C].indirect(T.LO[:, 24 * k:24 * k + 3 * C]), T.BG[:, 384 * k:384 * k + n], A.mult, wall(s) + ["LO%d" % k, "BG"], ["RO%d" % s])
-        for c in range(C):
-            mm(T.PL[0:48, 16 * c:16 * c + 16], T.RO[:, o + c:o + n:C], T.DGh[:], True, True, ["RO%d" % s, "DGh"], "#PL")
-        act(T.OUT[0:48, lo:lo + 16 * C], T.PL[0:48, 0:16 * C], F.Copy, ["#PL"], ["OUT%d" % s])
+    def final(ch):
+        w, o = at3("W", 3 * ST + ch, 0, 144), 32 * ch
+        ts(at("FM", o, o + 16), by(w, LA), NV - 1, None, A.bitwise_and)
+        ts(at("FM", o + 16, o + 32), by(w, LB), 15, None, A.bitwise_and)
+        tt(at("RO", L * ch, L * ch + L), by(at("FM", o, o + 32), at("LO")), at("BG"), A.mult)
+        mm(*[(at("PD", 384 + 16 * c, 400 + 16 * c, p=(0, 48)), at("RO", L * ch + c, L * ch + L, 4), at("DGh"), True, True) for c in range(4)])
+        act(at("OUT", 64 * ch, 64 * ch + 64, p=(0, 48)), at("PD", 384, 448, p=(0, 48)), F.Copy)
 
-    for j in range(4):
-        convert(j)
-    last = len(SETS) - 1
-    for s in range(last + 1):
-        start_state(s)
-        ask(s, 0, "V")
-    turn_cases()
-    send_cases(0)
-    update_lists()
-
-    later_constants()
-    update_lists_2()
     for t in range(ST):
-        more = t + 1 < ST
-        if t:
-            update(last, t - 1)
-            ask(last, t, ON["ask"][last])
-        for s in range(last + 1):
-            serve(s, t, ON["serve"][s])
-        n = 0
-        for name in PIECES.split():
-            level, ch, p = (int(x) for x in name)
-            if t == 0 and name == "200":
-                wide_cases(0, n)
-            if name in FUSED:
-                compare(t, ch, p)
-            else:
-                gather(t, n, level, ch, p)
-                widen(t, n, level, ch, p)
-                mask(t, n, level, ch, p)
-                n += 1
-            if level == 1 and ch == 0:
-                send_half(t, p)
-            elif p == 1 and level == 1:
-                pick(1, ch)
-                send_b(t, ch)
-                if ch == 2 and more:
-                    send_cases(t + 1)
-            elif p == 1 and level == 2:
-                pick(2, ch)
-                take_t(t, ch)
-                if ch < 2:
-                    before(ch)
-            elif p == 1:
-                if ch == 2:
-                    before(ch)
-                count(t, ch)
-                signs(ch)
-                verdict(ch)
-                answer(t, ch)
-        if more:
-            wide_cases(t + 1, n)
-        for chs in WRITES:
-            run(write_ops(chs))
-        run([scatter(c) for c in range(11, -1, -1)])
-        for s in range(last):
-            update(s, t)
-            if more:
-                ask(s, t + 1, ON["ask"][s])
-            else:
-                final(s)
+        cases(t)
+        for ch in CHS:
+            part(t - 1, "ask", ch)
+            ask(t, ch)
+        for ch in CHS:
+            part(t, "one", ch)
+            level1(t, ch)
+        for ch in CHS:
+            level2(t, ch)
+            level3(t, ch)
+        for lo, hi in WRITES:
+            writes(t, lo, hi)
+        for c in range(11, -1, -1):
+            part(t, "scatter", c // 4)
+            scatter(c)
+        for ch in CHS:
+            part(t, "update", ch)
+            update(t, ch)
+    for (n0, tag), (n1, nxt) in zip(marks, marks[1:] + [(len(ops), None)]):
+        ops[n0:n1] = [o + (tag,) for o in ops[n0:n1]]
 
-    for ch in range(3):
-        arrive("yt%d" % ch, ["YL%d" % ch])
-    dma("Y", "oyt", T.yt[:], T.YL[:], ["YL0", "YL1", "YL2"], [])
-    ms(T.Y4[0:1, :], 32768.0, ["Y4"])
-    mm(T.PC[:, 0:256], T.NO[0:1, :], T.Y4[0:1, :], True, False, ["NO", "Y4"], "#PC")
-    for m in range(9):
-        mm(T.PC[:, 0:256], T.NI[:], T.TAB[:, 256 * m:256 * m + 256], False, False, ["NI"] + TABK, "#PC")
-    tt(T.Y1[:, 0:768], T.TAB[:, 2560:3328], T.TAB[:, 3328:4096], A.add, TABK, ["Y1a"])
-    tt(T.Y2[:, 0:256], T.TAB[:, 2304:2560], T.Y1[:, 0:256], A.add, TABK + ["Y1a"], ["Y2a"])
-    tt(T.Y2[:, 256:512], T.Y1[:, 256:512], T.Y1[:, 512:768], A.add, ["Y1a"], ["Y2b"])
-    mm(T.PC[:, 0:256], T.NI[:], T.Y2[:, 0:256], False, True, ["NI", "Y2a"], "#PC")
-    update(last, ST - 1)
-    final(last)
-    outs = ["OUT%d" % s for s in range(last + 1)]
-    dma("S", "o0", T.yvp[:], T.OUT[0:24, :], outs, [])
-    dma("Y", "o1", T.yact[8:16, :], T.OUT[24:32, :], outs, [])
-    dma("S", "o2", T.yact[0:8, :], T.OUT[32:40, :], outs, [])
-    dma("Y", "o3", T.ydep[:], T.OUT[40:41, :], outs, [])
-    tt(T.YG[:], T.Y2[:, 256:512], T.PC[:, 0:256], A.subtract, ["Y2b", "#PC"], ["YG"])
-    dma("Y", "oyg", T.yg[:], T.YG[:], ["YG"], [])
+    for ch in CHS:
+        arrive(at("YL", 64 * ch, 64 * ch + 64), "yt%d" % ch)
+        final(ch)
+    dma("Y", "oyt", rows("yt", 0, 128), at("YL"))
+    for j in range(4):
+        for h, on in enumerate("VS"):
+            o = 1024 * j + 512 * h
+            move(on, at("YH", o, o + 512), at("TAB", SP + o, SP + o + 512))
+            chain([(at("PA0", 256, 512), Ib, at("YH", o + 256 * m, o + 256 * m + 256)) for m in range(2)], first=o == 0, last=o == NA - 512)
+    ts(at("YG"), at("PA0", 256, 512), 32768.0, None, A.add)
+    dma("Y", "oyg", rows("yg", 0, 128), at("YG"))
+    dma("S", "o0", rows("yvp", 0, 24), at("OUT", p=(0, 24)))
+    dma("S", "o1", rows("yact", 0, 16), at("OUT", p=(32, 48)))
+    dma("Y", "o2", rows("ydep", 0, 1), at("OUT", p=(24, 25)))
     return ops

@@ -8,7 +8,7 @@ SP = 40
 CHS = (2, 1, 0)
 NE = 8
 WW = 160
-CUT = (0, 1280, 2560, 3584, 4096)
+CUT = (0, 1536, 3072, 3840, 4096)
 AT = {"v": (0, 7), "a2": (28, 5), "a1": (48, 6), "d": (72, 6), "p1": (96, 6), "p2": (120, 6)}
 END = {"v": (5, 7), "w": (6, 7), "a2": (32, 5), "a1": (53, 6), "d": (77, 6), "p1": (101, 6), "p2": (125, 6),
        "tf": (144, 1), "code": (148, 1), "one": (158, 0), "six": (159, 0)}
@@ -25,24 +25,24 @@ def _s(n, dt):
 
 SCRATCH = {
     "GI": _s(NA, i32), "TAB": _s(SP + NA, f32), "FX": _s(NA, b16), "RF": _s(NV + 8, i32),
-    "CNs": _s(320, b16), "CN": _s(ST * 320, b16), "CX": _s([3 * ST, 512], b16), "NDi": _s(16, i32),
+    "CNs": _s(320, b16), "CN": _s(ST * 320, b16), "CX": _s([3 * ST, 512], b16), "G3": _s(3072, b16), "D4": _s(L, f32), "NDi": _s(16, i32),
     "SI": _s(L, i32), "SH": _s(L, h16), "DI": _s(L, i32), "DH": _s(L, h16),
     "W": _s([3 * (ST + 1), WW], i32), "BS": _s(ST * 240, u16), "BL": _s(ST * 240, u16),
     "RP": _s(ST * 24, i32), "YS": _s(L, f32), "YL": _s(L, f32),
     "R16": _s(L, u16), "TU": _s(L, u16), "G1": _s(3072, h16), "G2": _s(3072, h16), "CB": _s(3072, b16),
-    "MK1": _s(L, b16), "MK2": _s(L, b16), "MX1": _s(1536, b16), "MX2": _s(1536, b16), "XA": _s(384, h16), "XB": _s(384, h16),
+    "MK1": _s(2 * L, b16), "MK2": _s(2 * L, b16), "MX1": _s(1536, b16), "MX2": _s(1536, b16), "XA": _s(384, h16), "XB": _s(384, h16),
     "BB": _s(216, h16), "SG": _s(384, b16), "ST": _s(384, i32), "SB": _s([3, 144], h16),
     "D1": _s(L, h16), "OB": _s(12, u16), "EE": _s(L, f32), "SC": _s(L, f32), "OF": _s(24, u16), "DD": _s(L, f32), "TH": _s(L, f32),
     "FF": _s(432, f32), "PP": _s(432, f32), "FM": _s(96, i32), "RO": _s(576, h16), "OUT": _s(L, f32), "YH": _s(NA, h16), "YG": _s(256, f32),
     "PI": _s(4, i32), "PJ": _s(8, i32), "PF": _s(8, f32), "PG": _s(8, f32), "SR": _s(512, f32), "DM": _s(128, f32), "XI": _s(240, f32),
-    "ONE": _s(720, b16), "Ib": _s(128, b16), "I32": _s(128, b16), "MKT": _s(512, b16), "DG": _s(416, f32), "DGh": _s(16, h16),
+    "ONE": _s(720, b16), "Ib": _s(128, b16), "I32": _s(128, b16), "If": _s(128, f32), "MKT": _s(512, b16), "DG": _s(416, f32), "DGh": _s(16, h16),
     "LXi": _s(4, f32), "LX": _s(4, u16), "LN": _s(8, u16), "S2": _s(128, b16), "RM": _s(260, b16), "RA": _s(64, f32), "RB": _s(64, f32),
     "RC": _s(64, f32), "RE": _s(64, f32), "CE": _s(64, f32), "CR": _s(260, b16), "CS": _s(4, h16), "RS1": _s(128, f32), "RS2": _s(132, f32), "TRI": _s(L, b16),
     "GB": _s(128, f32), "BD": _s(128, b16), "NI": _s(128, b16), "SEL": _s(2048, b16), "SED": _s(2048, b16), "EW": _s(960, b16), "M2": _s(8, b16), "WQ": _s(720, b16), "W2": _s(144, b16),
     "WY": _s(960, b16), "RT": _s(416, f32), "RU": _s(416, f32), "RV": _s(416, f32), "RZ": _s(416, f32), "LS": _s(26, u16),
     "CD": _s(144, f32), "RS": _s(144, f32), "LI": _s(12, f32), "LO": _s(12, u16), "BI": _s(L, f32), "BG": _s(L, f32),
 }
-BANKS = ("PA0", "PA1", "PB0", "PB1", "PC", "PZ0", "PZ1", "PD")
+BANKS = ("PA0", "PA1", "PB0", "PX", "PC", "PZ0", "PZ1", "PD")
 for _n in BANKS:
     SCRATCH[_n] = ("psum", [128, 512], f32)
 IO = {"refs": [128, NV], "gloss": [128, NA], "facts": [128, NA], "cases": [128, L], "need": [ST, L], "vp0": [24, L],
@@ -51,7 +51,7 @@ IO = {"refs": [128, NV], "gloss": [128, NA], "facts": [128, NA], "cases": [128, 
 SEMAPHORES = (["eV", "eS", "eT", "eP", "ls", "g0", "g1", "g2", "g3", "fx", "rf", "rw", "cs", "nd", "s0", "s1", "s2", "dp",
                "oyt", "oyg", "o0", "o1", "o2", "yt0", "yt1", "yt2"]
               + ["%s%d" % (n, t) for t in range(ST) for n in ("cn",)]
-              + ["%s%d_%d" % (n, ch, t) for t in range(ST) for ch in range(3) for n in "abhr"])
+              + ["%s%d_%d" % (n, ch, t) for t in range(ST) for ch in range(3) for n in ("a", "b", "h", "r", "m1", "m2")])
 
 
 def at(name, c0=None, c1=None, step=None, p=(0, 128)):
@@ -128,17 +128,27 @@ def banks(op):
     return {x[0] for x in rd + wr if x[0] in BANKS}
 
 
+def spreads(op):
+    return op[2][0][0][:2] == "MX"
+
+
+def ticks(op):
+    return NE if op[1] == "arr" else 128 if spreads(op) else 16
+
+
 def cost(op):
     eng, kind, args = op[:3]
     if kind == "arr":
         return 100.0 + count(args[0]) * SIZE[SCRATCH[args[0][0]][2]] * 128 / 40.0, FAR - 100.0
+    if kind == "dma" and spreads(op):
+        return 8 * 70.0, NEAR + 200.0
     if kind == "dma":
         sb = args[0] if args[0][0] in SCRATCH else args[1]
         return 60.0, NEAR + count(sb) * SIZE[SCRATCH[sb[0]][2]] * 128 / 200.0
     if kind == "send":
         return ISSUE, -WAKE
     if kind == "mm":
-        return sum(max(min(64, count(m[1])), count(m[2])) * PEC + PEFIX for m in args), 60.0
+        return sum(max(min(64, count(m[1])), count(m[2])) * PEC * (4 if m[1][0] == "If" else 1) + PEFIX for m in args), 60.0
     n = count(args[0])
     if eng == "P":
         return 150.0 + 2 * n * CYC, 0.0
@@ -188,7 +198,7 @@ def arrange(ops, net=None):
     for i, o in enumerate(ops):
         if len(o) > 3:
             inside[i] = max([inside[j] + busy[j] + lag for j, lag in back[i] if ops[j][3:] == o[3:]], default=0.0)
-            rank[i] = o[3][0] * PERIOD + WHEN[o[3][1]][o[3][2]] + inside[i]
+            rank[i] = (o[3][0] * PERIOD + WHEN[o[3][1]][o[3][2]] if o[3][0] >= 0 else -PERIOD - 100.0 * o[3][2]) + inside[i]
         elif any(rank[j] is not None for j, lag in back[i]):
             rank[i] = max(rank[j] + busy[j] + lag for j, lag in back[i] if rank[j] is not None)
     for i in reversed(range(n)):
@@ -241,12 +251,105 @@ def arrange(ops, net=None):
             left[u] -= 1
             if not left[u]:
                 release(u)
+    if TRIES:
+        order, start = polish(ops, order, dur, eng, bank, busy, back)
     return order, deps, start, [s + sum(d) for s, d in zip(start, dur)]
 
 
+def polish(ops, order, dur, eng, bank, busy, back):
+    n, rng = len(ops), np.random.default_rng(SEED)
+    twin, seen, kin = [None] * n, {}, {}
+    for i, o in enumerate(ops):
+        if len(o) > 3:
+            seen[o[3]] = seen.get(o[3], 0) + 1
+            twin[i] = (o[3][1:], seen[o[3]])
+            kin[twin[i], o[3][0]] = i
+    lands = {back[i][0][0]: i for i in range(n) if eng[i] == "link"}
+    hold, total = [sum(d) + WAKE for d in dur], [sum(d) for d in dur]
+    bank = [tuple(b) for b in bank]
+
+    def timed(line):
+        start, cause, free, held = [0.0] * n, [None] * n, {}, {}
+        for i in line:
+            t, why, e = 0.0, None, eng[i]
+            for j, lag in back[i]:
+                if start[j] + busy[j] + lag > t:
+                    t, why = start[j] + busy[j] + lag, (j, False)
+            if e in free and free[e][0] > t:
+                t, why = free[e][0], (free[e][1], True)
+            for b in bank[i]:
+                if b in held and held[b][0] != e and held[b][1] > t:
+                    t, why = held[b][1], (held[b][2], True)
+                held[b] = (e, t + hold[i], i)
+            start[i], cause[i], free[e] = t, why, (t + busy[i], i)
+        last = max(range(n), key=lambda i: start[i] + total[i])
+        return start[last] + total[last], start, cause, last
+
+    def ahead_of(line, i, j):
+        a, b = line.index(j), line.index(i)
+        if a > b:
+            return line
+        want, take = {k for k, lag in back[i]}, [i]
+        for k in reversed(line[a:b]):
+            if k in want:
+                if k == j:
+                    return None
+                take.append(k)
+                want.update(x for x, lag in back[k])
+        if i in lands and line[b + 1] == lands[i]:
+            take.insert(0, lands[i])
+            b += 1
+        rest = set(take)
+        return line[:a] + take[::-1] + [k for k in line[a:b + 1] if k not in rest] + line[b + 1:]
+
+    def behind(line, i, j):
+        a, b = line.index(j), line.index(i)
+        if a > b:
+            return line
+        take = {j}
+        for k in line[a + 1:b + 1]:
+            if any(x in take for x, lag in back[k]):
+                if k == i:
+                    return None
+                take.add(k)
+        if i in lands and line[b + 1] == lands[i]:
+            b += 1
+        return line[:a] + [k for k in line[a:b + 1] if k not in take] + [k for k in line[a:b + 1] if k in take] + line[b + 1:]
+    order = [k for i in order if eng[i] != "link" for k in ([i, lands[i]] if i in lands else [i])]
+    now, start, cause, last = timed(order)
+    best = (now, order, start)
+    for move in range(TRIES):
+        queued, i = [], last
+        while cause[i]:
+            if cause[i][1] and eng[i] != "link":
+                queued.append((i, cause[i][0]))
+            i = cause[i][0]
+        i, j = queued[int(rng.integers(len(queued)))]
+        shift, far = (ahead_of, behind)[move % 2], int(rng.integers(4)) if move % 3 else 0
+        mates = [k for k in order if eng[k] == eng[i]] if far and eng[i] == eng[j] else None
+        if mates and shift is ahead_of:
+            j = mates[max(0, mates.index(j) - far)]
+        elif mates:
+            i = mates[min(len(mates) - 1, mates.index(i) + far)]
+        line = shift(order, i, j)
+        if line and twin[i] and twin[j] and move % 5:
+            for t in range(-1, ST):
+                pair = kin.get((twin[i], t)), kin.get((twin[j], t + ops[j][3][0] - ops[i][3][0]))
+                if None not in pair:
+                    line = shift(line, *pair) or line
+        if line:
+            result = timed(line)
+            if result[0] <= now + SLACK * (1.0 - move / TRIES) * float(rng.random()):
+                order, (now, start, cause, last) = line, result
+                if now < best[0]:
+                    best = (now, order, start)
+    return best[1:]
+
+
+TRIES, SLACK, SEED = 12000, 200.0, 1
 PERIOD, EARLY, PATIENCE = 20000.0, 3000.0, 0.3
 URGENT = {}
-WHEN = {'one': [21000, 9300, 2450], 'acts': [14850, 2200, 11950], 'two': [14300, 13200, 3500], 'before': [10350, 9500, 36300], 'three': [17250, 9500, 13100], 'reply': [17700, 19600, -5050], 'writes': [-8600, 13150, 9750], 'scatter': [18800, 17350, 23000], 'update': [28900, 23050, 21950], 'ask': [17500, 16250, 16650], 'cases': [15150, 12550, 5450], 'yt': [43800, 14150, 14050], 'old': [-4350, 36500, -13850], 'keys': [-2500, 9450, -6250], 'found': [10700, 24900, 12200], 'count': [5000, -100, -1900], 'XA': [-3200, 14700, -5700], 'XB': [9800, -5250, -11650], 'mask': [22000, 25850, 25850]}
+WHEN = {'one': [21550, 1400, -2300], 'acts': [10150, 2550, 9150], 'two': [7700, 150, -11150], 'before': [7500, 15000, 27900], 'three': [12800, 14150, 21650], 'reply': [25500, 28100, -9350], 'writes': [-8700, 25350, 11000], 'scatter': [16650, 14450, 23650], 'update': [45400, 23850, 23250], 'ask': [17600, 13900, 15300], 'cases': [10400, 23050, -2200], 'yt': [38900, 18050, 21800], 'old': [-11600, 26750, -18600], 'keys': [-5550, 19250, -11750], 'found': [13100, 28050, 26300], 'count': [14350, 8100, -11100], 'XA': [4650, 14250, -4550], 'XB': [15050, 350, -6400], 'mask': [23900, 21050, 26900], 'wide': [20500, 18550, 17600], 'last': [25200, 24450, 26900], 'final': [25450, 43000, 36200], 'sum': [32250, 1900, 4550]}
 
 
 PLAN = []
@@ -306,7 +409,7 @@ def emit(g, core, T, topo, ops, order, waits, need):
         e = q[eng]
         for j in waits[i]:
             if ops[j][1] in ("dma", "arr"):
-                e.wait_ge(T.sem[ops[j][2][-1]], 16 if ops[j][1] == "dma" else NE)
+                e.wait_ge(T.sem[ops[j][2][-1]], ticks(ops[j]))
                 seen.add(j)
             else:
                 e.wait_ge(T.sem["e" + ops[j][0]], num[j])
@@ -315,6 +418,12 @@ def emit(g, core, T, topo, ops, order, waits, need):
             rid, pid = topo.addr(dst)[:2]
             e.remote_dma(real(args[1]), real(args[2]), T.sem[args[3]], T.sem.ls, pid, rid, sum(1 << k for k in topo.engines(core, dst)[:NE]))
             sent += NE
+            continue
+        if kind == "dma" and spreads(ops[i]):
+            o, (a, b) = args[0][1][1].start, (args[1][1][1].start, args[1][1][1].stop)
+            for k in range(8):
+                p = (16 * k, 16 * k + 16)
+                e.dma_start(real(at(args[0][0], o + 64 * k, o + 64 * k + 64, p=p)), real(at(args[1][0], a, b, p=p))).then_inc(T.sem[args[2]], 16)
             continue
         if kind == "dma":
             e.dma_start(real(args[0]), real(args[1])).then_inc(T.sem[args[2]], 16)
@@ -343,7 +452,7 @@ def emit(g, core, T, topo, ops, order, waits, need):
             ins.then_inc(T.sem["e" + eng], 1)
     for i in order:
         if ops[i][1] in ("dma", "arr") and i not in seen:
-            g.wait_ge(T.sem[ops[i][2][-1]], 16 if ops[i][1] == "dma" else NE)
+            g.wait_ge(T.sem[ops[i][2][-1]], ticks(ops[i]))
     for eng, k in tick.items():
         g.wait_ge(T.sem["e" + eng], k)
     g.wait_ge(T.sem.ls, sent)
@@ -364,8 +473,7 @@ AHEAD = (2, 1, 0)
 WRITES = ((1, 3), (0, 1))
 HALVED = (0, 1, 2)
 PARTS = {2: ((0, 4),), 1: ((0, 4),), 0: ((0, 4),)}
-FACTS = [256, 256, 256]
-ON = {"cx": "SSSS", "G1": ["V1S1V1S1", "V1S1S1S1", "V1S1V1S1"], "G2": ["S1S1S1S1", "V1S1S1S1", "V1S1V1S1"], "XA": "SSS", "XB": "SSS", "SG": "SSS"}
+ON = {"MX1": "VVV", "MX2": "VVV", "cx": "SSS", "sum": "TSSVSVSV", "EE": "VSV", "G3": ["W-SS", "VVVV", "VVVV"], "G1": ["V1S1V1S1", "V1S1S1S1", "V1S1V1S1"], "G2": ["S1S1S1S1", "V1S1S1S1", "V1S1V1S1"], "XA": "SSS", "XB": "SSS", "SG": "SSS"}
 
 
 def calls(rank, n_ranks):
@@ -439,7 +547,7 @@ def calls(rank, n_ranks):
 
     def bank(k):
         turn[k] += 1
-        return ("PA", "PB")[k] + str(turn[k] % 2)
+        return "PB0" if k else "PA%d" % (turn[k] % 2)
 
     for j in range(4):
         dma("Y", "g%d" % j, at("GI", CUT[j], CUT[j + 1]), rows("gloss", 0, 128, CUT[j], CUT[j + 1]))
@@ -486,8 +594,8 @@ def calls(rank, n_ranks):
     ts(at("LN"), at("SR", 0, 128, 16), x16, None, A.add)
     ts(at("CNs", L, 320), by(at("NDi"), at("LN")), 2.0, -1.0, A.mult, A.add)
     ts(spare, x16, -2.0, -2050.0, A.mult, A.add)
-    ts(place, x16, 8.0, grp, A.mult, A.add)
-    iota(at("LXi"), [[128, 4]])
+    ts(place, grp, 64.0, x16, A.mult, A.add)
+    iota(at("LXi"), [[16, 4]])
     ts(at("LX"), at("LXi"), place, None, A.add)
     ms(at("TAB", 0, SP), 0.0)
     for name in ("MX2", "MX1"):
@@ -543,6 +651,7 @@ def calls(rank, n_ranks):
     ts(at("RS2", 0, 128), at("SR", 0, 128), 60000.0, spare, A.mult, A.add)
     ts(at("RS2", 128, 132), at("SR", 0, 64, 16), spare, None, A.add)
     ts(at("D1"), at("SR", 0, L), 0.0, spare, A.mult, A.add)
+    act(at("D4"), at("D1"), bias=2048.0 + SP)
     ts(at("TRI"), at("SR", 0, L), x16, 8192.0, A.is_gt, A.mult)
     ms(at("M2"), -2.0)
     for j in range(3):
@@ -565,6 +674,7 @@ def calls(rank, n_ranks):
     ts(at("BG"), at("BI"), grp, None, A.is_equal)
     ts(at("BG", 96, 128), at("BI", 96, 128), grp, 0.5, A.is_equal, A.mult)
     cp(at("DGh"), at("DG", 0, 16))
+    act(at("If"), Ib, F.Copy)
     for j in range(4):
         ts(at("TAB", SP + CUT[j], SP + CUT[j + 1]), at("GI", CUT[j], CUT[j + 1]), -2048.0, None, A.add)
 
@@ -580,12 +690,16 @@ def calls(rank, n_ranks):
             move(on[w // 64], at3("CX", k, w, 2 * w), at3("CX", k, 0, w))
         part(t - 1, "cases", 2)
         for ch in CHS:
-            if FACTS[ch] == 512:
-                move(on[3], at3("CX", 3 * t + ch, 256, 512), at3("CX", 3 * t + ch, 0, 256))
+            if "W" in ON["G3"][ch]:
+                move(on[2], at3("CX", 3 * t + ch, 256, 512), at3("CX", 3 * t + ch, 0, 256))
 
-    def masks(name, ch, acts):
-        act(at("MK" + name, 64 * ch, 64 * ch + 64), by(at("MKT"), acts), F.Copy)
-        cp(by(at("MX" + name, 512 * ch, 512 * ch + 512), at("LX")), at("MK" + name, 64 * ch, 64 * ch + 64))
+    def masks(t, name, ch, acts):
+        mk = at("MK" + name, L * (t % 2) + 64 * ch, L * (t % 2) + 64 * ch + 64)
+        act(mk, by(at("MKT"), acts), F.Copy)
+        if ON["MX" + name][ch] == "V":
+            cp(by(at("MX" + name, 512 * ch, 512 * ch + 512), at("LX")), mk)
+        else:
+            ops.append(("Y", "dma", (at("MX" + name, 512 * ch, 512 * ch + 512), mk, "m%s%d_%d" % (name, ch, t))))
 
     def pick(t, level, ch, q0, q1, x):
         pa, g, mx, lists = bank(0), "G%d" % level, "MX%d" % (3 - level), ("R16", 64 * ch) if level == 1 else ("BL", 240 * t + 80 * ch + 16)
@@ -598,7 +712,7 @@ def calls(rank, n_ranks):
                 for lane in range(16 * a, 16 * q):
                     o, r, p0 = 1024 * ch + lane // 16 * 256, lane % 16, lane // 16 * 32
                     lt = at(g, o + 16 * r, o + 16 * r + 16) if level == 1 else at(g, o + r, o + 256, 16)
-                    group.append((at(pa, r, 128, 16, p=(p0, p0 + 16)), lt, at(mx, 512 * ch + 8 * lane, 512 * ch + 8 * lane + 8), True, True))
+                    group.append((at(pa, r, 128, 16, p=(p0, p0 + 16)), lt, at(mx, 512 * ch + lane, 512 * ch + 512, 64), True, True))
                 mm(*group)
         p = (32 * q0, 32 * q1)
         part(t, x, ch)
@@ -615,7 +729,7 @@ def calls(rank, n_ranks):
             send(partner(t), at("BL", o + 8, o + 16), at("BS", o + 8, o + 16), "a%d_%d" % (ch, t))
         cp(at("R16", 64 * ch, 64 * ch + 64), by(at("RF"), at("BS", o, o + 4)))
         part(t - 1, "mask", ch)
-        masks("2", ch, at("BS", o + 4, o + 8))
+        masks(t, "2", ch, at("BS", o + 4, o + 8))
 
     def message(t, ch, q0, q1):
         o = 240 * t + 80 * ch + 16
@@ -637,7 +751,7 @@ def calls(rank, n_ranks):
             arrive(at("BL", o - 8, o), "a%d_%d" % (ch, t))
         for n, (q0, q1) in enumerate(PARTS[ch]):
             arrive(at("BL", *message(t, ch, q0, q1)), "%s%d_%d" % ("bh"[n], ch, t))
-        masks("1", ch, at("BL", o - 8, o - 4))
+        masks(t, "1", ch, at("BL", o - 8, o - 4))
         part(t, "keys", ch)
         ts(at("BB", 72 * ch, 72 * ch + 68), at("BL", o - 4, o + 64), -2048.0, None, A.add)
         part(t, "two", ch)
@@ -655,14 +769,25 @@ def calls(rank, n_ranks):
 
     def level3(t, ch):
         z, x, d2 = "PZ%d" % (ch % 2), at("XB", 128 * ch, 128 * ch + 128), at("BB", 72 * ch, 72 * ch + 4)
+        if "S" in ON["G3"][ch]:
+            part(t, "wide", ch)
+            act(at("PX", 256 * (ch % 2), 256 * (ch % 2) + 256), at3("CX", 3 * t + ch, 0, 256), F.Copy)
         part(t, "before", ch)
         chain([(at(z, 0, 260), at("ONE", 0, 128, p=row), at("CR", p=row)), (at(z, 128, 192), Ib, at("BB", 72 * ch + 4, 72 * ch + 68)),
                (at(z, 78, 128, 16), Ib, d2), (at(z, 79, 128, 16), Ib, d2), (at(z, 256, 260), at("I32"), d2),
                (at(z, 256, 260), at("ONE", 0, 128, p=row), at("CS", p=row)),
                (at(z, 0, 64), x, at("S2", 64, 128)), (at(z, 192, 256), x, at("S2", 64, 128))], last=False)
         part(t, "three", ch)
-        for o in range(1024 * ch, 1024 * ch + 1024, FACTS[ch]):
-            tt(at("CB", o, o + FACTS[ch]), by(at("FX"), at("TU", o // 16, (o + FACTS[ch]) // 16)), at3("CX", 3 * t + ch, 0, FACTS[ch]), A.is_le)
+        for n, on in enumerate(ON["G3"][ch]):
+            o, w = 1024 * ch + 256 * n, 512 if on == "W" else 256
+            facts = by(at("FX"), at("TU", o // 16, (o + w) // 16))
+            if on == "-":
+                continue
+            if on != "S":
+                tt(at("CB", o, o + w), facts, at3("CX", 3 * t + ch, 0, w), A.is_le)
+            else:
+                act(at("G3", o, o + 256), facts, F.Copy)
+                tt(at("CB", o, o + 256), at("G3", o, o + 256), at("PX", 256 * (ch % 2), 256 * (ch % 2) + 256), A.is_le)
         part(t, "count", ch)
         for r0, r1 in ((0, 32), (32, 64)) if ch in HALVED else ((0, 64),):
             o, e = 1024 * ch + 16 * r0, 64 * (3 * t + ch)
@@ -689,16 +814,23 @@ def calls(rank, n_ranks):
         tt(art, at3("SB", k, 15, 64, 16), at3("SB", k, 128, 132), A.min)
         chain([(at("PD", 0, w), Ib, at("TRI", 0, w))]
               + [(at("PD", r + 1, w, 16), at("SED", 128 * r, 128 * r + 128), art) for r in range(15)])
-        ts(at("EE", *ln), at("PD", 0, w), 0.0, -8192.0, A.is_equal, A.mult)
-        scan(at("SC", *ln), at("EE", *ln), at("D1", *ln), A.add, A.max)
-        ts(at("OF", 8 * lo, 8 * hi, 2), at("SC", ln[0] + 15, ln[1], 16), 2048.0 + SP, None, A.add)
+        if ON["EE"][lo] == "S":
+            act(at("D4", ln[0], ln[1], 16), art, bias=2048.0 + SP)
+            act(at("EE", *ln), at("PD", 0, w), F.Abs, scale=8192.0)
+            scan(at("SC", *ln), at("EE", *ln), at("D4", *ln), A.min, A.max)
+            cp(at("OF", 8 * lo, 8 * hi, 2), at("SC", ln[0] + 15, ln[1], 16))
+        else:
+            ts(at("EE", *ln), at("PD", 0, w), 0.0, -8192.0, A.is_equal, A.mult)
+            scan(at("SC", *ln), at("EE", *ln), at("D1", *ln), A.add, A.max)
+            ts(at("OF", 8 * lo, 8 * hi, 2), at("SC", ln[0] + 15, ln[1], 16), 2048.0 + SP, None, A.add)
         part(t, "old", lo)
         ts(at("OB", 4 * lo, 4 * hi), art, 2048.0 + SP, None, A.add)
         pb = bank(1)
-        chain([(at(pb, 0, w), Ib, at("MK1", *ln))]
+        mk = at("MK1", L * (t % 2) + ln[0], L * (t % 2) + ln[1])
+        chain([(at(pb, 0, w), Ib, mk)]
               + [(at(pb, r, w, 16), at("SEL", 128 * r, 128 * r + 128), at3("SB", k, 79, 128, 16)) for r in range(16)])
         act(at("TH", *ln), at(pb, 0, w), bias=-8192.0)
-        tt(at("DD", *ln), by(whole, at("OB", 4 * lo, 4 * hi)), at("MK1", *ln), A.subtract)
+        tt(at("DD", *ln), by(whole, at("OB", 4 * lo, 4 * hi)), mk, A.subtract)
 
     def scatter(c):
         ln = (16 * c, 16 * c + 16)
@@ -736,23 +868,28 @@ def calls(rank, n_ranks):
             part(t, "scatter", c // 4)
             scatter(c)
         for ch in CHS:
-            part(t, "update", ch)
+            part(t, "update" if t + 1 < ST else "last", ch)
             update(t, ch)
-    for (n0, tag), (n1, nxt) in zip(marks, marks[1:] + [(len(ops), None)]):
-        ops[n0:n1] = [o + (tag,) for o in ops[n0:n1]]
 
     for ch in CHS:
+        part(ST - 1, "final", ch)
         arrive(at("YL", 64 * ch, 64 * ch + 64), "yt%d" % ch)
         final(ch)
     dma("Y", "oyt", rows("yt", 0, 128), at("YL"))
-    for j in range(4):
-        for h, on in enumerate("VS"):
-            o = 1024 * j + 512 * h
+    part(ST - 1, "sum", 0)
+    for j, on in enumerate(ON["sum"]):
+        o = 512 * j
+        if on == "T":
+            pair = [(at("If"), at("TAB", SP + o + 256 * m, SP + o + 256 * m + 256)) for m in range(2)]
+        else:
             move(on, at("YH", o, o + 512), at("TAB", SP + o, SP + o + 512))
-            chain([(at("PA0", 256, 512), Ib, at("YH", o + 256 * m, o + 256 * m + 256)) for m in range(2)], first=o == 0, last=o == NA - 512)
-    ts(at("YG"), at("PA0", 256, 512), 32768.0, None, A.add)
+            pair = [(Ib, at("YH", o + 256 * m, o + 256 * m + 256)) for m in range(2)]
+        chain([(at("PA0", 256, 512),) + x for x in pair], first=o == 0, last=o == NA - 512)
+    act(at("YG"), at("PA0", 256, 512), bias=32768.0)
     dma("Y", "oyg", rows("yg", 0, 128), at("YG"))
-    dma("S", "o0", rows("yvp", 0, 24), at("OUT", p=(0, 24)))
-    dma("S", "o1", rows("yact", 0, 16), at("OUT", p=(32, 48)))
+    dma("Y", "o0", rows("yvp", 0, 24), at("OUT", p=(0, 24)))
+    dma("Y", "o1", rows("yact", 0, 16), at("OUT", p=(32, 48)))
     dma("Y", "o2", rows("ydep", 0, 1), at("OUT", p=(24, 25)))
+    for (n0, tag), (n1, nxt) in zip(marks, marks[1:] + [(len(ops), None)]):
+        ops[n0:n1] = [o + (tag,) for o in ops[n0:n1]]
     return ops

import numpy as np
from concourse.mybir import AluOpType, ActivationFunctionType

A, F = AluOpType, ActivationFunctionType

L, ST, NA, NV = 192, 5, 4096, 512
SP = 40
CHS = (2, 1, 0)
NE = 8
WW = 160
CUT = (0, 1536, 3072, 3840, 4096)
AT = {"v": (0, 7), "a2": (28, 5), "a1": (48, 6), "d": (72, 6), "p1": (96, 6), "p2": (120, 6)}
END = {"v": (5, 7), "w": (6, 7), "a2": (32, 5), "a1": (53, 6), "d": (77, 6), "p1": (101, 6), "p2": (125, 6),
       "tf": (144, 1), "code": (148, 1), "one": (158, 0), "six": (159, 0)}
CELLS = (2050, 2048, 2052, 2048, 2052, 2050, 1, 6)
MOVES = (("v", 0, "tf"), ("v", 1, "w"), ("v", 2, "tf"), ("v", 3, "p1"), ("v", 4, "w"), ("v", 5, "p2"), ("v", 6, "one"),
         ("a2", 2, "tf"), ("a1", 0, "tf"), ("p1", 0, "w"), ("p2", 2, "w"))

f32, b16, h16, i32, u16 = "float32", "bfloat16", "float16", "int32", "uint16"


def _s(n, dt):
    return ("sbuf", [128] + (n if isinstance(n, list) else [n]), dt)


SCRATCH = {
    "GI": _s(NA, i32), "TAB": _s(SP + NA, f32), "FX": _s(NA, b16), "RF": _s(NV + 8, i32),
    "CNs": _s(320, b16), "CN": _s(ST * 320, b16), "CX": _s([3 * ST, 512], b16), "G3": _s(3072, b16), "D4": _s(L, f32), "NDi": _s(16, i32),
    "SI": _s(L, i32), "SH": _s(L, h16), "DI": _s(L, i32), "DH": _s(L, h16),
    "W": _s([3 * (ST + 1), WW], i32), "BS": _s(ST * 240, u16), "BL": _s(ST * 240, u16),
    "RP": _s(ST * 24, i32), "YS": _s(L, f32), "YL": _s(L, f32),
    "R16": _s(L, u16), "TU": _s(L, u16), "G1": _s(3072, h16), "G2": _s(3072, h16), "CB": _s(3072, b16),
    "MK1": _s(2 * L, b16), "MK2": _s(2 * L, b16), "MX1": _s(1536, b16), "MX2": _s(1536, b16), "XA": _s(384, h16), "XB": _s(384, h16),
    "BB": _s(216, h16), "SG": _s(384, b16), "ST": _s(384, i32), "SB": _s([3, 144], h16),
    "D1": _s(L, h16), "OB": _s(12, u16), "EE": _s(L, f32), "SC": _s(L, f32), "OF": _s(24, u16), "DD": _s(L, f32), "TH": _s(L, f32),
    "FF": _s(432, f32), "PP": _s(432, f32), "FM": _s(96, i32), "RO": _s(576, h16), "OUT": _s(L, f32), "YH": _s(NA, h16), "YG": _s(256, f32),
    "PI": _s(4, i32), "PJ": _s(8, i32), "PF": _s(8, f32), "PG": _s(8, f32), "SR": _s(512, f32), "DM": _s(128, f32), "XI": _s(240, f32),
    "ONE": _s(720, b16), "Ib": _s(128, b16), "I32": _s(128, b16), "If": _s(128, f32), "MKT": _s(512, b16), "DG": _s(416, f32), "DGh": _s(16, h16),
    "LXi": _s(4, f32), "LX": _s(4, u16), "LN": _s(8, u16), "S2": _s(128, b16), "RM": _s(260, b16), "RA": _s(64, f32), "RB": _s(64, f32),
    "RC": _s(64, f32), "RE": _s(64, f32), "CE": _s(64, f32), "CR": _s(260, b16), "CS": _s(4, h16), "RS1": _s(128, f32), "RS2": _s(132, f32), "TRI": _s(L, b16),
    "GB": _s(128, f32), "BD": _s(128, b16), "NI": _s(128, b16), "SEL": _s(2048, b16), "SED": _s(2048, b16), "EW": _s(960, b16), "M2": _s(8, b16), "WQ": _s(720, b16), "W2": _s(144, b16),
    "WY": _s(960, b16), "RT": _s(416, f32), "RU": _s(416, f32), "RV": _s(416, f32), "RZ": _s(416, f32), "LS": _s(26, u16),
    "CD": _s(144, f32), "RS": _s(144, f32), "LI": _s(12, f32), "LO": _s(12, u16), "BI": _s(L, f32), "BG": _s(L, f32),
}
BANKS = ("PA0", "PA1", "PB0", "PX", "PC", "PZ0", "PZ1", "PD")
for _n in BANKS:
    SCRATCH[_n] = ("psum", [128, 512], f32)
IO = {"refs": [128, NV], "gloss": [128, NA], "facts": [128, NA], "cases": [128, L], "need": [ST, L], "vp0": [24, L],
      "act0": [16, L], "dep0": [1, L], "yt": [128, L], "yg": [128, 256], "yvp": [24, L], "yact": [16, L], "ydep": [1, L]}

SEMAPHORES = (["eV", "eS", "eT", "eP", "ls", "g0", "g1", "g2", "g3", "fx", "rf", "rw", "cs", "nd", "s0", "s1", "s2", "dp",
               "oyt", "oyg", "o0", "o1", "o2", "yt0", "yt1", "yt2"]
              + ["%s%d" % (n, t) for t in range(ST) for n in ("cn",)]
              + ["%s%d_%d" % (n, ch, t) for t in range(ST) for ch in range(3) for n in ("a", "b", "h", "r", "m1", "m2")])


def at(name, c0=None, c1=None, step=None, p=(0, 128)):
    return (name, (slice(p[0], p[1]), slice(c0, c1, step)))


def at3(name, k, c0=None, c1=None, step=None):
    return (name, (slice(0, 128), k, slice(c0, c1, step)))


def by(win, off):
    return win + (off,)


CYC, GATHER, SCATTER, FIX, WAKE, FAR, NEAR, PEC, ISSUE = 0.85, 1.56, 3.8, 50.0, 140.0, 2500.0, 1900.0, 0.43, 400.0
PEFIX = 4.0
SIZE = {f32: 4, i32: 4, b16: 2, h16: 2, u16: 2}


def cells(ap):
    shape = SCRATCH[ap[0]][1]
    return np.arange(int(np.prod(shape[1:]))).reshape(shape[1:])[ap[1][1:]].ravel()


def count(ap):
    return 16 * len(cells(ap[2])) if len(ap) == 3 else len(cells(ap))


def foot(ap, memo={}):
    key = (ap[0], str(ap[1]))
    if key not in memo:
        bits = np.zeros(int(np.prod(SCRATCH[ap[0]][1][1:])), bool)
        bits[cells(ap)] = True
        memo[key] = (ap[0], ap[1][0].start, ap[1][0].stop, int.from_bytes(np.packbits(bits, bitorder="little").tobytes(), "little"))
    return memo[key]


def sides(op):
    kind, args = op[1], op[2]
    if kind == "mm":
        rd, wr = [x for m in args for x in m[1:3]], [m[0] for m in args]
    elif kind == "send":
        rd, wr = [args[2]], []
    else:
        rd, wr = [x for x in args[1:] if isinstance(x, tuple)], [args[0]]
    rd = rd + [x[2] for x in rd + wr if len(x) == 3]
    return [list({foot(x) for x in s if x[0] in SCRATCH}) for s in (rd, wr)]


def depends(ops):
    log, out = {}, []
    for i, op in enumerate(ops):
        rd, wr = sides(op)
        raw, other = set(), set()
        for mine, writes in ((rd, False), (wr, True)):
            for name, p0, p1, bits in mine:
                for j, q0, q1, theirs, wrote in log.get(name, ()):
                    if (wrote or writes) and q0 < p1 and p0 < q1 and bits & theirs:
                        (other if writes and wrote else raw).add(j)
        for name, p0, p1, bits in wr:
            log[name] = [e for e in log.get(name, ()) if not (p0 <= e[1] and e[2] <= p1 and e[3] & ~bits == 0)]
        for mine, writes in ((rd, False), (wr, True)):
            for name, p0, p1, bits in mine:
                log.setdefault(name, []).append((i, p0, p1, bits, writes))
        out.append({j: j in raw or ops[j][0] != op[0] or op[0] != IN_ORDER or "dma" in (op[1], ops[j][1]) for j in (raw | other) - {i}})
    return out


IN_ORDER = "T"


def banks(op):
    rd, wr = sides(op)
    return {x[0] for x in rd + wr if x[0] in BANKS}


def spreads(op):
    return op[2][0][0][:2] == "MX"


def ticks(op):
    return NE if op[1] == "arr" else 128 if spreads(op) else 16


def cost(op):
    eng, kind, args = op[:3]
    if kind == "arr":
        return 100.0 + count(args[0]) * SIZE[SCRATCH[args[0][0]][2]] * 128 / 40.0, FAR - 100.0
    if kind == "dma" and spreads(op):
        return 8 * 70.0, NEAR + 200.0
    if kind == "dma":
        sb = args[0] if args[0][0] in SCRATCH else args[1]
        return 60.0, NEAR + count(sb) * SIZE[SCRATCH[sb[0]][2]] * 128 / 200.0
    if kind == "send":
        return ISSUE, -WAKE
    if kind == "mm":
        return sum(max(min(64, count(m[1])), count(m[2])) * PEC * (4 if m[1][0] == "If" else 1) + PEFIX for m in args), 60.0
    n = count(args[0])
    if eng == "P":
        return 150.0 + 2 * n * CYC, 0.0
    if len(args[0]) == 3:
        return FIX + n * SCATTER * CYC, 0.0
    fix = FIX + (20.0 if eng == "S" else 5.0)
    if kind != "ms" and len(args[1]) == 3:
        return fix + n * GATHER * CYC, 0.0
    full = [x for x in args if isinstance(x, tuple) and count(x) == n]
    per = 0.5 if eng == "V" and all(SIZE[SCRATCH[x[0]][2]] == 2 for x in full) else 1.0
    if kind == "tt" and not any(x[0] in BANKS for x in full[1:]):
        per = 2.0
    return fix + max(16, n * per) * CYC, 0.0


def network(ops):
    n, deps, dur = len(ops), depends(ops), [cost(o) for o in ops]
    sender = {o[2][3]: i for i, o in enumerate(ops) if o[1] == "send"}
    loaded, before = 1200.0, {}
    first = [0.0] * n
    for i, o in enumerate(ops):
        if o[1] == "arr":
            deps[i][sender[o[2][1]]] = True
        elif o[1] == "dma" and o[2][1][0] in IO:
            first[i] = 1e6 - i
            loaded += dur[i][1] - NEAR if o[0] == "Y" else 0.0
            dur[i] = (60.0, NEAR + (loaded if o[0] == "Y" else 600.0))
    eng, bank, busy = [o[0] or "link" for o in ops], [banks(o) for o in ops], [d[0] for d in dur]
    back, ahead = [[] for o in ops], [[] for o in ops]
    for i in range(n):
        for j in set(deps[i]) | ({before[eng[i]]} if first[i] and eng[i] in before else set()):
            lag = 0.0 if (not deps[i].get(j) or eng[j] == eng[i] == "T") else dur[j][1] + (WAKE if eng[i] else 0.0)
            back[i].append((j, lag))
            ahead[j].append((i, lag))
        if first[i]:
            before[eng[i]] = i
    for t in range(1, ST):
        back[sender["cn%d" % t]].append((sender["b0_%d" % (t - 1)], 0.0))
        ahead[sender["b0_%d" % (t - 1)]].append((sender["cn%d" % t], 0.0))
    return ops, deps, dur, eng, bank, busy, back, ahead


def arrange(ops, net=None):
    ops, deps, dur, eng, bank, busy, back, ahead = net or network(ops)
    n = len(ops)
    inside, rank = [0.0] * n, [None] * n
    for i, o in enumerate(ops):
        if len(o) > 3:
            inside[i] = max([inside[j] + busy[j] + lag for j, lag in back[i] if ops[j][3:] == o[3:]], default=0.0)
            rank[i] = (o[3][0] * PERIOD + WHEN[o[3][1]][o[3][2]] if o[3][0] >= 0 else -PERIOD - 100.0 * o[3][2]) + inside[i]
        elif any(rank[j] is not None for j, lag in back[i]):
            rank[i] = max(rank[j] + busy[j] + lag for j, lag in back[i] if rank[j] is not None)
    for i in reversed(range(n)):
        if rank[i] is None:
            rank[i] = min([rank[u] - lag - (EARLY if len(ops[u]) > 3 else 0.0) for u, lag in ahead[i]], default=0.0) - busy[i]
    left, start, ready, free, held, order = [len(b) for b in back], [0.0] * n, {}, {}, {}, []
    pool = {e: [] for e in sorted(set(eng))}

    def release(i):
        ready[i] = max([0.0] + [start[j] + busy[j] + lag for j, lag in back[i]])
        pool[eng[i]].append((ready[i] if eng[i] == "link" else rank[i], i))
        pool[eng[i]].sort()
        first.pop(eng[i], None)

    def when(i):
        t = ready[i]
        for b in bank[i]:
            if b in held and held[b][0] != eng[i] and held[b][1] > t:
                t = held[b][1]
        return t
    first = {}
    for i in range(n):
        if not left[i]:
            release(i)
    while len(order) < n:
        for e, c in pool.items():
            if e not in first:
                first[e] = min([when(i) for r, i in c], default=1e18)
        now, e = min((max(free.get(e, 0.0), t), e) for e, t in first.items())
        soon, strict, pick = 1e18, 1e18, None
        for r, i in pool[e]:
            if when(i) > now + 1.0:
                soon = min(soon, when(i))
                if len(ops[i]) > 3 and ops[i][3][1] in URGENT:
                    strict = min(strict, when(i) + URGENT[ops[i][3][1]])
            elif now + busy[i] * PATIENCE <= soon and now + busy[i] <= strict:
                pick = i
                break
        if pick is None:
            free[e] = soon
            continue
        pool[e].remove((r, pick))
        order.append(pick)
        start[pick], free[e] = now, now + busy[pick]
        first.pop(e)
        for b in bank[pick]:
            held[b] = (e, now + sum(dur[pick]) + WAKE)
            first.clear()
        for u, lag in ahead[pick]:
            left[u] -= 1
            if not left[u]:
                release(u)
    if TRIES:
        order, start = polish(ops, order, dur, eng, bank, busy, back)
    return order, deps, start, [s + sum(d) for s, d in zip(start, dur)]


def polish(ops, order, dur, eng, bank, busy, back):
    n, rng = len(ops), np.random.default_rng(SEED)
    twin, seen, kin = [None] * n, {}, {}
    for i, o in enumerate(ops):
        if len(o) > 3:
            seen[o[3]] = seen.get(o[3], 0) + 1
            twin[i] = (o[3][1:], seen[o[3]])
            kin[twin[i], o[3][0]] = i
    lands = {back[i][0][0]: i for i in range(n) if eng[i] == "link"}
    hold, total = [sum(d) + WAKE for d in dur], [sum(d) for d in dur]
    bank = [tuple(b) for b in bank]

    def timed(line):
        start, cause, free, held = [0.0] * n, [None] * n, {}, {}
        for i in line:
            t, why, e = 0.0, None, eng[i]
            for j, lag in back[i]:
                if start[j] + busy[j] + lag > t:
                    t, why = start[j] + busy[j] + lag, (j, False)
            if e in free and free[e][0] > t:
                t, why = free[e][0], (free[e][1], True)
            for b in bank[i]:
                if b in held and held[b][0] != e and held[b][1] > t:
                    t, why = held[b][1], (held[b][2], True)
                held[b] = (e, t + hold[i], i)
            start[i], cause[i], free[e] = t, why, (t + busy[i], i)
        last = max(range(n), key=lambda i: start[i] + total[i])
        return start[last] + total[last], start, cause, last

    def ahead_of(line, i, j):
        a, b = line.index(j), line.index(i)
        if a > b:
            return line
        want, take = {k for k, lag in back[i]}, [i]
        for k in reversed(line[a:b]):
            if k in want:
                if k == j:
                    return None
                take.append(k)
                want.update(x for x, lag in back[k])
        if i in lands and line[b + 1] == lands[i]:
            take.insert(0, lands[i])
            b += 1
        rest = set(take)
        return line[:a] + take[::-1] + [k for k in line[a:b + 1] if k not in rest] + line[b + 1:]

    def behind(line, i, j):
        a, b = line.index(j), line.index(i)
        if a > b:
            return line
        take = {j}
        for k in line[a + 1:b + 1]:
            if any(x in take for x, lag in back[k]):
                if k == i:
                    return None
                take.add(k)
        if i in lands and line[b + 1] == lands[i]:
            b += 1
        return line[:a] + [k for k in line[a:b + 1] if k not in take] + [k for k in line[a:b + 1] if k in take] + line[b + 1:]
    order = [k for i in order if eng[i] != "link" for k in ([i, lands[i]] if i in lands else [i])]
    now, start, cause, last = timed(order)
    best = (now, order, start)
    for move in range(TRIES):
        queued, i = [], last
        while cause[i]:
            if cause[i][1] and eng[i] != "link":
                queued.append((i, cause[i][0]))
            i = cause[i][0]
        i, j = queued[int(rng.integers(len(queued)))]
        shift, far = (ahead_of, behind)[move % 2], int(rng.integers(4)) if move % 3 else 0
        mates = [k for k in order if eng[k] == eng[i]] if far and eng[i] == eng[j] else None
        if mates and shift is ahead_of:
            j = mates[max(0, mates.index(j) - far)]
        elif mates:
            i = mates[min(len(mates) - 1, mates.index(i) + far)]
        line = shift(order, i, j)
        if line and twin[i] and twin[j] and move % 5:
            for t in range(-1, ST):
                pair = kin.get((twin[i], t)), kin.get((twin[j], t + ops[j][3][0] - ops[i][3][0]))
                if None not in pair:
                    line = shift(line, *pair) or line
        if line:
            result = timed(line)
            if result[0] <= now + SLACK * (1.0 - move / TRIES) * float(rng.random()):
                order, (now, start, cause, last) = line, result
                if now < best[0]:
                    best = (now, order, start)
    return best[1:]


TRIES, SLACK, SEED = 12000, 200.0, 1
PERIOD, EARLY, PATIENCE = 20000.0, 3000.0, 0.3
URGENT = {}
WHEN = {'one': [21550, 1400, -2300], 'acts': [10150, 2550, 9150], 'two': [7700, 150, -11150], 'before': [7500, 15000, 27900], 'three': [12800, 14150, 21650], 'reply': [25500, 28100, -9350], 'writes': [-8700, 25350, 11000], 'scatter': [16650, 14450, 23650], 'update': [45400, 23850, 23250], 'ask': [17600, 13900, 15300], 'cases': [10400, 23050, -2200], 'yt': [38900, 18050, 21800], 'old': [-11600, 26750, -18600], 'keys': [-5550, 19250, -11750], 'found': [13100, 28050, 26300], 'count': [14350, 8100, -11100], 'XA': [4650, 14250, -4550], 'XB': [15050, 350, -6400], 'mask': [23900, 21050, 26900], 'wide': [20500, 18550, 17600], 'last': [25200, 24450, 26900], 'final': [25450, 43000, 36200], 'sum': [32250, 1900, 4550]}


PLAN = []


def waits_of(ops, order, deps):
    place = {i: k for k, i in enumerate(order)}
    known = {e: ({}, set()) for e in "VSTPY"}
    clock, waits, need, held = {}, {}, set(), {}
    for i in order:
        eng = ops[i][0]
        if eng is None:
            clock[i] = ({}, set())
            continue
        mine, all_deps = [], {j for j, hard in deps[i].items() if hard}
        for b in banks(ops[i]):
            if b in held and ops[held[b]][0] != eng:
                all_deps.add(held[b])
            held[b] = i
        kc, ks = known[eng]
        for j in sorted(all_deps, key=lambda j: -place[j]):
            ej = ops[j][0]
            if ops[j][1] in ("dma", "arr"):
                if j in ks:
                    continue
                ks.add(j)
            else:
                if ej == eng == "T" or kc.get(ej, -1) >= place[j]:
                    continue
                kc[ej] = place[j]
                need.add(j)
            mine.append(j)
            for e, k in clock[j][0].items():
                kc[e] = max(kc.get(e, -1), k)
            ks.update(clock[j][1])
        clock[i] = (dict(kc), set(ks))
        waits[i] = mine
    return waits, need


def emit(g, core, T, topo, ops, order, waits, need):
    q = {"V": g.vector, "S": g.scalar, "T": g.tensor, "P": g, "Y": g.sync}

    def real(x):
        if not isinstance(x, tuple):
            return x
        ap = T[x[0]][x[1]]
        return ap.indirect(real(x[2])) if len(x) == 3 else ap
    tick, num, seen, sent = {}, {}, set(), 0
    for i in order:
        if i in need:
            tick[ops[i][0]] = num[i] = tick.get(ops[i][0], 0) + 1
    for i in order:
        eng, kind, args = ops[i][:3]
        if eng is None:
            continue
        e = q[eng]
        for j in waits[i]:
            if ops[j][1] in ("dma", "arr"):
                e.wait_ge(T.sem[ops[j][2][-1]], ticks(ops[j]))
                seen.add(j)
            else:
                e.wait_ge(T.sem["e" + ops[j][0]], num[j])
        if kind == "send":
            dst = T.cores[args[0]]
            rid, pid = topo.addr(dst)[:2]
            e.remote_dma(real(args[1]), real(args[2]), T.sem[args[3]], T.sem.ls, pid, rid, sum(1 << k for k in topo.engines(core, dst)[:NE]))
            sent += NE
            continue
        if kind == "dma" and spreads(ops[i]):
            o, (a, b) = args[0][1][1].start, (args[1][1][1].start, args[1][1][1].stop)
            for k in range(8):
                p = (16 * k, 16 * k + 16)
                e.dma_start(real(at(args[0][0], o + 64 * k, o + 64 * k + 64, p=p)), real(at(args[1][0], a, b, p=p))).then_inc(T.sem[args[2]], 16)
            continue
        if kind == "dma":
            e.dma_start(real(args[0]), real(args[1])).then_inc(T.sem[args[2]], 16)
            continue
        a = [real(x) for x in args] if kind != "mm" else None
        if kind == "mm":
            for m in args:
                ins = e.matmul(real(m[0]), real(m[1]), real(m[2]), m[3], m[4])
        elif kind == "ts":
            ins = e.tensor_scalar(*(a if a[5] is not None else a[:5]))
        elif kind == "tt":
            ins = e.tensor_tensor(*a)
        elif kind == "cp":
            ins = e.tensor_copy(*a)
        elif kind == "ms":
            ins = e.memset(*a)
        elif kind == "scan":
            ins = e.tensor_tensor_scan(*a)
        elif kind == "act":
            ins = e.activation(a[0], a[1], a[2], bias=a[3], scale=a[4])
        elif kind == "iota":
            ins = e.iota(*a) if SCRATCH[args[0][0]][2] == i32 else e.iota(*a, allow_small_or_imprecise_dtypes=True)
        else:
            ins = e.affine_select(*a)
        if i in need:
            ins.then_inc(T.sem["e" + eng], 1)
    for i in order:
        if ops[i][1] in ("dma", "arr") and i not in seen:
            g.wait_ge(T.sem[ops[i][2][-1]], ticks(ops[i]))
    for eng, k in tick.items():
        g.wait_ge(T.sem["e" + eng], k)
    g.wait_ge(T.sem.ls, sent)


def rank_program(g, core, T, topo):
    rank = T.rank_of(core)
    if rank is None:
        return
    ops = calls(rank, len(T.cores))
    if not PLAN:
        order, deps = arrange(ops)[:2]
        PLAN.extend((order,) + waits_of(ops, order, deps))
    emit(g, core, T, topo, ops, *PLAN)


AHEAD = (2, 1, 0)
WRITES = ((1, 3), (0, 1))
HALVED = (0, 1, 2)
PARTS = {2: ((0, 4),), 1: ((0, 4),), 0: ((0, 4),)}
ON = {"MX1": "VVV", "MX2": "VVV", "cx": "SSS", "sum": "TSSVSVSV", "EE": "VSV", "G3": ["W-SS", "VVVV", "VVVV"], "G1": ["V1S1V1S1", "V1S1S1S1", "V1S1V1S1"], "G2": ["S1S1S1S1", "V1S1S1S1", "V1S1V1S1"], "XA": "SSS", "XB": "SSS", "SG": "SSS"}


def calls(rank, n_ranks):
    ops, marks = [], []

    def part(*tag):
        marks.append((len(ops), tag))

    def ts(out, a, s1, s2, o0, o1=None):
        ops.append(("V", "ts", (out, a, s1, s2, o0, o1)))

    def tt(out, a, b, o):
        ops.append(("V", "tt", (out, a, b, o)))

    def cp(out, a):
        ops.append(("V", "cp", (out, a)))

    def ms(out, val):
        ops.append(("V", "ms", (out, val)))

    def scan(out, d0, d1, o0, o1):
        ops.append(("V", "scan", (out, d0, d1, 0.0, o0, o1)))

    def act(out, a, fn=F.Identity, bias=0.0, scale=1.0):
        ops.append(("S", "act", (out, a, fn, bias, scale)))

    def move(on, out, a):
        if on == "S":
            act(out, a, F.Copy)
        elif on == "P":
            sel(out, a, [[0, count(out)]], 0, 0)
        else:
            cp(out, a)

    def mm(*group):
        ops.append(("T", "mm", group))

    def chain(items, first=True, last=True):
        mm(*[m + (first and k == 0, last and k == len(items) - 1) for k, m in enumerate(items)])

    def iota(out, pat, base=0, cm=0):
        ops.append(("P", "iota", (out, pat, base, cm)))

    def sel(out, a, pat, base, cm, o=A.is_equal, other=0.0):
        ops.append(("P", "sel", (out, a, pat, o, other, base, cm)))

    def dma(eng, sem, out, a):
        ops.append((eng, "dma", (out, a, sem)))

    def send(dst, out, a, sem):
        ops.append(("P", "send", (dst, out, a, sem)))

    def arrive(out, sem):
        ops.append((None, "arr", (out, sem)))

    def partner(t):
        return (rank + 1 + t % (n_ranks - 1)) % n_ranks

    def asker(t):
        return (rank - 1 - t % (n_ranks - 1)) % n_ranks

    def rows(name, r0, r1, c0=None, c1=None):
        return (name, (slice(r0, r1), slice(c0, c1)))

    x16, grp, x4, x32 = (at("PF", j, j + 1) for j in range(4))
    spare, place = at("PG", 0, 1), at("PG", 1, 2)
    table, whole = at("TAB", SP, SP + NA), at("TAB")
    LC, LF, LV, LA, LB = at("LS", 0, 9), at("LS", 10, 19), at("LS", 20, 21), at("LS", 22, 23), at("LS", 24, 25)
    Ib = at("Ib")
    turn = [0, 0]

    def bank(k):
        turn[k] += 1
        return "PB0" if k else "PA%d" % (turn[k] % 2)

    for j in range(4):
        dma("Y", "g%d" % j, at("GI", CUT[j], CUT[j + 1]), rows("gloss", 0, 128, CUT[j], CUT[j + 1]))
    dma("Y", "fx", at("FX"), rows("facts", 0, 128))
    dma("S", "s0", at("SI", p=(0, 24)), rows("vp0", 0, 24))
    dma("S", "s1", at("SI", p=(24, 32)), rows("act0", 8, 16))
    dma("S", "s2", at("SI", p=(32, 40)), rows("act0", 0, 8))
    dma("S", "dp", at("DI", p=(0, 1)), rows("dep0", 0, 1))
    dma("S", "rf", at("RF", 0, NV), rows("refs", 0, 128))
    dma("S", "rw", at("RF", NV, NV + 8), rows("refs", 0, 128, 0, 8))
    dma("S", "cs", at("CNs", 0, L), rows("cases", 0, 128))
    ms(at("NDi"), 1)
    dma("S", "nd", at("NDi", p=(0, 12 * ST)), rows("need", 0, ST))

    ms(at("ONE"), 1.0)
    iota(at("PI", 0, 1), [[0, 1]], 0, 1)
    iota(at("SR"), [[0, 32], [1, 16]])
    sel(at("WQ", p=(0, 64)), at("ONE", p=(0, 64)), [[128, 5], [1, 144]], -15, -16)
    iota(at("DM"), [[1, 128]], 0, -1)
    for j, (num, o) in enumerate(((15, A.bitwise_and), (4, A.logical_shift_right), (3, A.bitwise_and), (31, A.bitwise_and),
                                  (5, A.logical_shift_right))):
        ts(at("PJ", j, j + 1), at("PI", 0, 1), num, None, o)
    cp(at("PF", 0, 5), at("PJ", 0, 5))
    ts(at("W2", p=(0, 1)), at("SR", 0, 144, p=(0, 1)), 15.0, None, A.is_equal)
    cp(at("SH", p=(0, 40)), at("SI", p=(0, 40)))
    ts(at("DH", p=(0, 1)), at("DI", p=(0, 1)), 2.0, 2048.0, A.mult, A.add)
    for qq, name in enumerate(("v", "p1", "p2", "a2", "a1", "d")):
        out = at("PZ1", 12 * qq, 12 * qq + 12)
        if name == "d":
            chain([(out, at("W2", 15 - r, 143 - r, p=(0, 1)), at("DH", r, L, 16, p=(0, 1))) for r in range(16)])
        else:
            chain([(out, at("WQ", 144 * qq + 15 - r, 144 * qq + 143 - r, p=(0, 40)), at("SH", r, L, 16, p=(0, 40))) for r in range(16)])
    ms(at3("W", slice(0, 3), 0, 144), 0)
    for qq, name in enumerate(("v", "p1", "p2", "a2", "a1", "d")):
        for nm, add in ((name, 0.0),) + ((("w", 1.0),) if name == "v" else ()):
            o, s = END[nm]
            ts(at3("W", slice(0, 3), o, o + 3 * s + 1, s), at("PZ1", 12 * qq, 12 * qq + 12), add, None, A.add)
    for k, val in enumerate(CELLS):
        ms(at3("W", slice(0, 3 * ST), 152 + k, 153 + k), val)
    ts(at("DG"), at("SR", 0, 416), x16, None, A.is_equal)
    ts(at("RZ"), at("SR", 0, 416), 0.0, None, A.not_equal)
    ts(at("MKT"), at("SR"), x16, 8192.0, A.is_equal, A.mult)
    ts(Ib, at("DM"), 0.0, None, A.is_equal)
    ts(at("LN"), at("SR", 0, 128, 16), x16, None, A.add)
    ts(at("CNs", L, 320), by(at("NDi"), at("LN")), 2.0, -1.0, A.mult, A.add)
    ts(spare, x16, -2.0, -2050.0, A.mult, A.add)
    ts(place, grp, 64.0, x16, A.mult, A.add)
    iota(at("LXi"), [[16, 4]])
    ts(at("LX"), at("LXi"), place, None, A.add)
    ms(at("TAB", 0, SP), 0.0)
    for name in ("MX2", "MX1"):
        ms(at(name), 0.0)
    for name in ("PA0", "PA1"):
        ms(at(name, 0, 128), 0.0)
    sel(at("S2", 0, 64), at("ONE", 0, 64), [[-1, 16], [-32, 4]], 0, 1)
    sel(at("S2", 64, 128), at("ONE", 0, 64), [[-32, 4], [-1, 16]], 0, 1)

    ms(at("RT"), 0.0)
    for name in ("a2", "a1", "p1", "p2"):
        o, s = AT[name]
        iota(at("RT", o, o + 4 * s), [[END[name][1], 4], [0, s]], END[name][0])
    iota(at("RT", 72, 96), [[0, 4], [1, 6]], 152)
    for name, case, src in MOVES:
        o, s = AT[name]
        iota(at("RT", o + case, o + case + 3 * s + 1, s), [[END[src][1], 4]], END[src][0])
    for o, s, blocks in ((0, 7, 1), (28, 5, 1), (48, 6, 4)):
        iota(at("RT", 160 + o, 160 + o + 4 * s * blocks), [[0, blocks], [1, 4], [0, s]], END["code"][0])
        iota(at("CD", o, o + 4 * s * blocks), [[0, 4 * blocks], [1, s]])
    iota(at("RT", 166, 188, 7), [[0, 4]], END["six"][0])
    iota(at("RT", 211, 230, 6), [[0, 4]], END["six"][0])
    for o, names in ((320, ("v", "a2", "a1", "d")), (352, ("v", "p1", "p2", "d")), (384, ("a1", "a2"))):
        for k, name in enumerate(names):
            iota(at("RT", o + 4 * k, o + 4 * k + 4), [[END[name][1], 4]], END[name][0])
    for a, b in ((320, 336), (0, 160), (160, 320), (336, 416)):
        tt(at("RU", a, b), at("RT", a, b), at("DG", a, b), A.mult)
        scan(at("RV", a, b), at("RZ", a, b), at("RU", a, b), A.mult, A.add)
        cp(at("LS", a // 16, b // 16), at("RV", a + 15, b, 16))
    ts(at("RS"), at("CD"), 0.0, None, A.not_equal)

    top = (0, 64)
    iota(at("RA", p=top), [[1, 4], [4, 16]], 0, -1)
    iota(at("RB", p=top), [[1, 4], [0, 16]])
    ts(at("CE", p=top), at("RB", p=top), at("PF", 2, 3, p=top), None, A.is_equal)
    ts(at("RC", p=top), at("RA", p=top), 0.0, 16384.0, A.is_equal, A.mult)
    ts(at("RE", p=top), at("RA", p=top), 0.0, -8192.0, A.is_ge, A.mult)
    tt(at("RC", p=top), at("RC", p=top), at("RE", p=top), A.add)
    tt(at("RM", 0, 64, p=top), at("RC", p=top), at("CE", p=top), A.mult)
    ms(at("RM", 64, 128, p=top), 0.0)
    ts(at("RM", 79, 128, 16, p=top), at("CE", 0, 64, 16, p=top), -1.0, None, A.mult)
    cp(at("RM", 128, 192, p=top), at("RM", 0, 64, p=top))
    ts(at("RM", 192, 256, p=top), at("RM", 0, 64, p=top), -1.0, None, A.mult)
    ts(at("RM", 256, 260, p=top), at("CE", 0, 64, 16, p=top), -2080.0, None, A.mult)
    row = (0, 1)
    ts(at("CR", 0, 64, p=row), at("SR", 0, 64, p=row), -8192.0, -4096.0, A.mult, A.add)
    ts(at("CR", 64, 128, p=row), at("SR", 0, 64, p=row), 15.0, -15.0, A.is_equal, A.mult)
    ts(at("CR", 128, 256, p=row), at("SR", 0, 128, p=row), -8192.0, -8192.0, A.mult, A.add)
    ms(at("CR", 256, 260, p=row), -131072.0)
    ms(at("CS", p=row), 31168.0)
    ts(at("I32"), at("DM"), 0.0, 32768.0, A.is_equal, A.mult)
    ts(at("RS1"), at("SR", 0, 128), 0.0, None, A.not_equal)
    ts(at("RS2", 0, 128), at("SR", 0, 128), 60000.0, spare, A.mult, A.add)
    ts(at("RS2", 128, 132), at("SR", 0, 64, 16), spare, None, A.add)
    ts(at("D1"), at("SR", 0, L), 0.0, spare, A.mult, A.add)
    act(at("D4"), at("D1"), bias=2048.0 + SP)
    ts(at("TRI"), at("SR", 0, L), x16, 8192.0, A.is_gt, A.mult)
    ms(at("M2"), -2.0)
    for j in range(3):
        sel(at("EW", 320 * j, 320 * j + 320, p=top), at("ONE", 0, 320, p=top), [[-4, 5], [0, 16], [-1, 4]], -20 * j, 1)
    iota(at("GB"), [[1, 8], [0, 16]])
    ts(at("BD"), at("GB"), grp, None, A.is_equal)
    ts(at("NI"), at("DM"), 0.0, -1.0, A.is_equal, A.mult)
    for r in range(16):
        act(at("SEL", 128 * r, 128 * r + 128), at("BD"), scale=at("DG", r, r + 1))
    for j in range(4):
        chain([(at("PC"), Ib, at("SEL", 512 * j, 512 * j + 512))] + [(at("PC", 128 * r, 128 * r + 128), Ib, at("NI")) for r in range(4)])
        act(at("SED", 512 * j, 512 * j + 512), at("PC"), F.Copy)
    iota(at("XI"), [[1, 240]], -112)
    ts(at("PG", 4, 8), at("SR", 0, 4), at("PF", 4, 5), None, A.is_equal)
    for q in range(4):
        ts(at("WY", 240 * q, 240 * q + 240), at("XI"), x32, at("PG", 4 + q, 5 + q), A.is_equal, A.mult)
    iota(at("LI"), [[4, 6], [0, 2]])
    iota(at("BI"), [[0, 6], [1, 8], [0, 4]])
    ts(at("LO"), at("LI"), x4, None, A.add)
    ts(at("BG"), at("BI"), grp, None, A.is_equal)
    ts(at("BG", 96, 128), at("BI", 96, 128), grp, 0.5, A.is_equal, A.mult)
    cp(at("DGh"), at("DG", 0, 16))
    act(at("If"), Ib, F.Copy)
    for j in range(4):
        ts(at("TAB", SP + CUT[j], SP + CUT[j + 1]), at("GI", CUT[j], CUT[j + 1]), -2048.0, None, A.add)

    def cases(t):
        part(t - 1, "cases", 0)
        send(partner(t), at("CN", 320 * t, 320 * t + 320), at("CNs"), "cn%d" % t)
        arrive(at("CN", 320 * t, 320 * t + 320), "cn%d" % t)
        k = slice(3 * t, 3 * t + 3)
        part(t - 1, "cases", 1)
        on = ON["cx"] if t else "SSSS"
        move(on[0], at3("CX", k, 0, 64), at("CN", 320 * t, 320 * t + L))
        for w in (64, 128):
            move(on[w // 64], at3("CX", k, w, 2 * w), at3("CX", k, 0, w))
        part(t - 1, "cases", 2)
        for ch in CHS:
            if "W" in ON["G3"][ch]:
                move(on[2], at3("CX", 3 * t + ch, 256, 512), at3("CX", 3 * t + ch, 0, 256))

    def masks(t, name, ch, acts):
        mk = at("MK" + name, L * (t % 2) + 64 * ch, L * (t % 2) + 64 * ch + 64)
        act(mk, by(at("MKT"), acts), F.Copy)
        if ON["MX" + name][ch] == "V":
            cp(by(at("MX" + name, 512 * ch, 512 * ch + 512), at("LX")), mk)
        else:
            ops.append(("Y", "dma", (at("MX" + name, 512 * ch, 512 * ch + 512), mk, "m%s%d_%d" % (name, ch, t))))

    def pick(t, level, ch, q0, q1, x):
        pa, g, mx, lists = bank(0), "G%d" % level, "MX%d" % (3 - level), ("R16", 64 * ch) if level == 1 else ("BL", 240 * t + 80 * ch + 16)
        plan, q = ON[g][ch], 0
        for on, blocks in zip(plan[::2], plan[1::2]):
            a, q = q, q + int(blocks)
            if q0 <= a < q1:
                move(on, at(g, 1024 * ch + 256 * a, 1024 * ch + 256 * q), by(table, at(lists[0], lists[1] + 16 * a, lists[1] + 16 * q)))
                group = []
                for lane in range(16 * a, 16 * q):
                    o, r, p0 = 1024 * ch + lane // 16 * 256, lane % 16, lane // 16 * 32
                    lt = at(g, o + 16 * r, o + 16 * r + 16) if level == 1 else at(g, o + r, o + 256, 16)
                    group.append((at(pa, r, 128, 16, p=(p0, p0 + 16)), lt, at(mx, 512 * ch + lane, 512 * ch + 512, 64), True, True))
                mm(*group)
        p = (32 * q0, 32 * q1)
        part(t, x, ch)
        if ON[x][ch] == "S":
            act(at(x, 128 * ch, 128 * ch + 128, p=p), at(pa, 0, 128, p=p), scale=1.0 / 8192.0)
        else:
            ts(at(x, 128 * ch, 128 * ch + 128, p=p), at(pa, 0, 128, p=p), 1.0 / 8192.0, None, A.mult)
        return at(x, 128 * ch, 128 * ch + 128, p=p), p

    def ask(t, ch):
        o = 240 * t + 80 * ch
        cp(at("BS", o, o + 16), by(at3("W", 3 * t + ch, 0, 144), LV))
        if ch in AHEAD:
            send(partner(t), at("BL", o + 8, o + 16), at("BS", o + 8, o + 16), "a%d_%d" % (ch, t))
        cp(at("R16", 64 * ch, 64 * ch + 64), by(at("RF"), at("BS", o, o + 4)))
        part(t - 1, "mask", ch)
        masks(t, "2", ch, at("BS", o + 4, o + 8))

    def message(t, ch, q0, q1):
        o = 240 * t + 80 * ch + 16
        return o + 16 * q0 - (8 if q0 == 0 and ch not in AHEAD else 0), o + 16 * q1

    def level1(t, ch):
        for n, (q0, q1) in enumerate(PARTS[ch]):
            part(t, "one", ch)
            x, p = pick(t, 1, ch, q0, q1, "XA")
            pb, o, w = bank(1), 240 * t + 80 * ch + 16 + 16 * q0, 16 * (q1 - q0)
            mm((at(pb, 0, w), x, at("S2", 64 + 16 * q0, 64 + 16 * q1, p=p), True, True))
            ts(at("BS", o, o + w), at(pb, 0, w), 2048.0, None, A.add)
            send(partner(t), at("BL", *message(t, ch, q0, q1)), at("BS", *message(t, ch, q0, q1)), "%s%d_%d" % ("bh"[n], ch, t))

    def level2(t, ch):
        o = 240 * t + 80 * ch + 16
        part(t, "acts", ch)
        if ch in AHEAD:
            arrive(at("BL", o - 8, o), "a%d_%d" % (ch, t))
        for n, (q0, q1) in enumerate(PARTS[ch]):
            arrive(at("BL", *message(t, ch, q0, q1)), "%s%d_%d" % ("bh"[n], ch, t))
        masks(t, "1", ch, at("BL", o - 8, o - 4))
        part(t, "keys", ch)
        ts(at("BB", 72 * ch, 72 * ch + 68), at("BL", o - 4, o + 64), -2048.0, None, A.add)
        part(t, "two", ch)
        x, p = pick(t, 2, ch, 0, 4, "XB")
        pb, ln = bank(1), (64 * ch, 64 * ch + 64)
        mm((at(pb, 0, 64), x, at("S2", 0, 64), True, True))
        ts(at("TU", *ln), at(pb, 0, 64), 2048.0, None, A.add)
        part(t, "yt", ch)
        if t == ST - 1:
            for q in range(4):
                chain([(at("PD", 256 + 16 * q, 272 + 16 * q), at("WY", 240 * q + 112 - 16 * g, 240 * q + 240 - 16 * g),
                        at("XB", 128 * ch + 16 * g, 128 * ch + 16 * g + 16)) for g in range(8)])
            act(at("YS", *ln), at("PD", 256, 320), bias=2048.0)
            send(asker(t), at("YL", *ln), at("YS", *ln), "yt%d" % ch)

    def level3(t, ch):
        z, x, d2 = "PZ%d" % (ch % 2), at("XB", 128 * ch, 128 * ch + 128), at("BB", 72 * ch, 72 * ch + 4)
        if "S" in ON["G3"][ch]:
            part(t, "wide", ch)
            act(at("PX", 256 * (ch % 2), 256 * (ch % 2) + 256), at3("CX", 3 * t + ch, 0, 256), F.Copy)
        part(t, "before", ch)
        chain([(at(z, 0, 260), at("ONE", 0, 128, p=row), at("CR", p=row)), (at(z, 128, 192), Ib, at("BB", 72 * ch + 4, 72 * ch + 68)),
               (at(z, 78, 128, 16), Ib, d2), (at(z, 79, 128, 16), Ib, d2), (at(z, 256, 260), at("I32"), d2),
               (at(z, 256, 260), at("ONE", 0, 128, p=row), at("CS", p=row)),
               (at(z, 0, 64), x, at("S2", 64, 128)), (at(z, 192, 256), x, at("S2", 64, 128))], last=False)
        part(t, "three", ch)
        for n, on in enumerate(ON["G3"][ch]):
            o, w = 1024 * ch + 256 * n, 512 if on == "W" else 256
            facts = by(at("FX"), at("TU", o // 16, (o + w) // 16))
            if on == "-":
                continue
            if on != "S":
                tt(at("CB", o, o + w), facts, at3("CX", 3 * t + ch, 0, w), A.is_le)
            else:
                act(at("G3", o, o + 256), facts, F.Copy)
                tt(at("CB", o, o + 256), at("G3", o, o + 256), at("PX", 256 * (ch % 2), 256 * (ch % 2) + 256), A.is_le)
        part(t, "count", ch)
        for r0, r1 in ((0, 32), (32, 64)) if ch in HALVED else ((0, 64),):
            o, e = 1024 * ch + 16 * r0, 64 * (3 * t + ch)
            chain([(at("PC", 0, 128, p=(r0, r1)), at("EW", e + r0, e + r1, p=(0, 12 * ST)), at("CN", 320 * t + L, 320 * t + 320, p=(0, 12 * ST)))]
                  + [(at("PC", r, 128, 16, p=(r0, r1)), at("CB", o + r, o + 16 * (r1 - r0), 16), at("M2")) for r in range(16)])
        sg = at("SG", 128 * ch, 128 * ch + 128, p=top)
        if ON["SG"][ch] == "S":
            act(sg, at("PC", 0, 128, p=top), F.Sign)
        else:
            ts(sg, at("PC", 0, 128, p=top), -1.0, 1.0, A.max, A.min)
        chain([(at(z, 0, 260), sg, at("RM", p=top))], first=False)
        o, a = 128 * ch, 24 * t + 8 * ch
        part(t, "reply", ch)
        scan(at("ST", o, o + 128), at("RS1"), at(z, 0, 128), A.mult, A.max)
        ts(at("RP", a, a + 8), at("ST", o + 15, o + 128, 16), NV - 1, None, A.bitwise_and)
        send(asker(t), at3("W", 3 * t + ch, 144, 152), at("RP", a, a + 8), "r%d_%d" % (ch, t))
        part(t, "found", ch)
        scan(at3("SB", ch, 0, 132), at("RS2"), at(z, 128, 260), A.min, A.max)

    def writes(t, lo, hi):
        ln, w, k = (64 * lo, 64 * hi), 64 * (hi - lo), slice(lo, hi)
        art = at("D1", ln[0], ln[1], 16)
        part(t, "writes", lo)
        tt(art, at3("SB", k, 15, 64, 16), at3("SB", k, 128, 132), A.min)
        chain([(at("PD", 0, w), Ib, at("TRI", 0, w))]
              + [(at("PD", r + 1, w, 16), at("SED", 128 * r, 128 * r + 128), art) for r in range(15)])
        if ON["EE"][lo] == "S":
            act(at("D4", ln[0], ln[1], 16), art, bias=2048.0 + SP)
            act(at("EE", *ln), at("PD", 0, w), F.Abs, scale=8192.0)
            scan(at("SC", *ln), at("EE", *ln), at("D4", *ln), A.min, A.max)
            cp(at("OF", 8 * lo, 8 * hi, 2), at("SC", ln[0] + 15, ln[1], 16))
        else:
            ts(at("EE", *ln), at("PD", 0, w), 0.0, -8192.0, A.is_equal, A.mult)
            scan(at("SC", *ln), at("EE", *ln), at("D1", *ln), A.add, A.max)
            ts(at("OF", 8 * lo, 8 * hi, 2), at("SC", ln[0] + 15, ln[1], 16), 2048.0 + SP, None, A.add)
        part(t, "old", lo)
        ts(at("OB", 4 * lo, 4 * hi), art, 2048.0 + SP, None, A.add)
        pb = bank(1)
        mk = at("MK1", L * (t % 2) + ln[0], L * (t % 2) + ln[1])
        chain([(at(pb, 0, w), Ib, mk)]
              + [(at(pb, r, w, 16), at("SEL", 128 * r, 128 * r + 128), at3("SB", k, 79, 128, 16)) for r in range(16)])
        act(at("TH", *ln), at(pb, 0, w), bias=-8192.0)
        tt(at("DD", *ln), by(whole, at("OB", 4 * lo, 4 * hi)), mk, A.subtract)

    def scatter(c):
        ln = (16 * c, 16 * c + 16)
        tt(by(whole, at("OF", 2 * c, 2 * c + 1)), at("TH", *ln), at("DD", *ln), A.max)

    def update(t, ch):
        k, ln = 3 * t + ch, (144 * ch, 144 * ch + 144)
        arrive(at3("W", k, 144, 152), "r%d_%d" % (ch, t))
        tt(at("FF", *ln), by(at3("W", k), LF), at("CD"), A.is_equal)
        tt(at("PP", *ln), by(at3("W", k), LC), at("FF", *ln), A.mult)
        scan(at3("W", k + 3, 0, 144), at("RS"), at("PP", *ln), A.mult, A.add)

    def final(ch):
        w, o = at3("W", 3 * ST + ch, 0, 144), 32 * ch
        ts(at("FM", o, o + 16), by(w, LA), NV - 1, None, A.bitwise_and)
        ts(at("FM", o + 16, o + 32), by(w, LB), 15, None, A.bitwise_and)
        tt(at("RO", L * ch, L * ch + L), by(at("FM", o, o + 32), at("LO")), at("BG"), A.mult)
        mm(*[(at("PD", 384 + 16 * c, 400 + 16 * c, p=(0, 48)), at("RO", L * ch + c, L * ch + L, 4), at("DGh"), True, True) for c in range(4)])
        act(at("OUT", 64 * ch, 64 * ch + 64, p=(0, 48)), at("PD", 384, 448, p=(0, 48)), F.Copy)

    for t in range(ST):
        cases(t)
        for ch in CHS:
            part(t - 1, "ask", ch)
            ask(t, ch)
        for ch in CHS:
            part(t, "one", ch)
            level1(t, ch)
        for ch in CHS:
            level2(t, ch)
            level3(t, ch)
        for lo, hi in WRITES:
            writes(t, lo, hi)
        for c in range(11, -1, -1):
            part(t, "scatter", c // 4)
            scatter(c)
        for ch in CHS:
            part(t, "update" if t + 1 < ST else "last", ch)
            update(t, ch)

    for ch in CHS:
        part(ST - 1, "final", ch)
        arrive(at("YL", 64 * ch, 64 * ch + 64), "yt%d" % ch)
        final(ch)
    dma("Y", "oyt", rows("yt", 0, 128), at("YL"))
    part(ST - 1, "sum", 0)
    for j, on in enumerate(ON["sum"]):
        o = 512 * j
        if on == "T":
            pair = [(at("If"), at("TAB", SP + o + 256 * m, SP + o + 256 * m + 256)) for m in range(2)]
        else:
            move(on, at("YH", o, o + 512), at("TAB", SP + o, SP + o + 512))
            pair = [(Ib, at("YH", o + 256 * m, o + 256 * m + 256)) for m in range(2)]
        chain([(at("PA0", 256, 512),) + x for x in pair], first=o == 0, last=o == NA - 512)
    act(at("YG"), at("PA0", 256, 512), bias=32768.0)
    dma("Y", "oyg", rows("yg", 0, 128), at("YG"))
    dma("Y", "o0", rows("yvp", 0, 24), at("OUT", p=(0, 24)))
    dma("Y", "o1", rows("yact", 0, 16), at("OUT", p=(32, 48)))
    dma("Y", "o2", rows("ydep", 0, 1), at("OUT", p=(24, 25)))
    for (n0, tag), (n1, nxt) in zip(marks, marks[1:] + [(len(ops), None)]):
        ops[n0:n1] = [o + (tag,) for o in ops[n0:n1]]
    return ops
